import numpy as np
import ml_dtypes


def mxq(x, axis, fmt="e4m3"):
    dtype, down = {"e4m3": (ml_dtypes.float8_e4m3fn, 7), "e5m2": (ml_dtypes.float8_e5m2, 14)}[fmt]
    v = np.moveaxis(np.asarray(x, np.float32).astype(ml_dtypes.bfloat16).astype(np.float64), axis, -1)
    blocks = v.reshape(v.shape[:-1] + (-1, 32))
    amax = np.abs(blocks).max(-1, keepdims=True)
    byte = np.maximum(np.where(amax > 0, np.frexp(amax)[1] - 1 + 127, 0) - down, 1)
    scale = np.exp2(byte - 127.0)
    codes = (blocks / scale).astype(np.float32).astype(dtype).astype(np.float64)
    return np.moveaxis((codes * scale).reshape(v.shape), -1, axis)


WIDE = False


def mx_kscale(k):
    if not WIDE:
        return np.ones(k)
    levels = np.array([18, -18])
    if k % 512:
        return np.exp2(np.random.permutation(np.resize(levels, k // 32))).repeat(32)
    a = np.empty((k // 512, 16))
    for p in range(k // 512):
        a[p, :8] = np.random.permutation(np.resize(levels, 8))
        for g in range(8):
            far = levels[np.abs(levels - a[p, g]) >= 10]
            a[p, g + 8] = far[np.random.randint(len(far))]
    return np.exp2(a.ravel()).repeat(32)


def f64(x):
    return np.asarray(x).astype(np.float64)


def striped(idx):
    return np.tile(np.asarray(idx).reshape(-1, 16).T, (8, 1)).astype(np.uint16)


def unstriped(offs):
    return offs[:16].T.reshape(-1).astype(np.int64)


B, N, T, D, DV, R = 1, 512, 2048, 512, 512, 1024


def setup_inputs():
    n = np.random.standard_normal
    idx = np.random.permutation(T)[:B * N]
    s = mx_kscale(D)[:, None]
    v = mx_kscale(DV)[:, None]
    q = n((B, D, R))
    do = n((B, DV, R))
    u = np.ones(T)
    u[idx] = mx_kscale(B * N)
    r = np.random.uniform(0.5, 2.0, T) * u
    return {
        "qT": (q * s).astype(np.float32),
        "kT": (n((D, T)) * (1.00 / np.sqrt(D)) / s / r).astype(np.float32),
        "vT": (n((DV, T)) / np.sqrt(DV) / v).astype(np.float32),
        "doT": (do * v).astype(np.float32),
        "rw": (np.random.uniform(0.5, 1.5, (B, R, 1)) * 1.0 / np.sqrt(R)).astype(np.float32),
        "ts": np.tile(r, (128, 1)).astype(np.float32),
        "offs": striped(idx),
    }


def reference(qT, kT, vT, doT, rw, ts, offs):
    idx = unstriped(offs)
    pick = lambda x: x[:, idx].reshape(x.shape[0], B, N).transpose(1, 0, 2)
    k = pick(f64(kT))
    a = mxq(f64(qT), 1, "e4m3").transpose(0, 2, 1) @ mxq(k, 1, "e4m3")
    ts_ = pick(f64(ts))[:, :1, :]
    a = a * ts_
    dp = mxq(f64(doT), 1, "e5m2").transpose(0, 2, 1) @ mxq(pick(f64(vT)), 1, "e4m3")
    ds = f64(rw) * dp * 2.0 * np.maximum(a, 0.0)
    ds = ts_ * ds
    gq = mxq(ds, 2, "e5m2") @ mxq(k, 2, "e4m3").transpose(0, 2, 1)
    return gq

@@ -1,0 +1,223 @@
+from contextlib import ExitStack
+
+import concourse.mybir as mybir
+from concourse.masks import make_identity
+
+F32 = mybir.dt.float32
+BF16 = mybir.dt.bfloat16
+U32 = mybir.dt.uint32
+U16 = mybir.dt.uint16
+U8 = mybir.dt.uint8
+E4M3 = mybir.dt.float8_e4m3fn_x4
+E5M2 = mybir.dt.float8_e5m2_x4
+MULT = mybir.AluOpType.mult
+RELU = mybir.ActivationFunctionType.Relu
+
+P = 128
+PACK = 4
+N, T, D, R = 512, 2048, 512, 1024
+CHUNKS = R // P
+Q_COLS = 512
+DO_COLS = 256
+GROUPS = [(0, 1), (2, 3), (4, 5), (6,), (7,)]
+
+FLOPS = 3 * 2 * R * N * D
+
+
+def tile_attend_gat_q_ts_kernel(tc, qT, kT, vT, doT, rw, ts, offs, out):
+    nc = tc.nc
+
+    with ExitStack() as ctx:
+        keep = ctx.enter_context(tc.tile_pool(name="keep", bufs=1))
+        ring = ctx.enter_context(tc.tile_pool(name="ring", bufs=3))
+        ps_mm = ctx.enter_context(tc.psum_pool(name="ps_mm", bufs=3))
+        ps_tr = ctx.enter_context(tc.psum_pool(name="ps_tr", bufs=3))
+        ps_out = ctx.enter_context(tc.psum_pool(name="ps_out", bufs=2))
+
+        def held(name, shape, dtype):
+            return keep.tile(shape, dtype, name=name, align_bytes=64)
+
+        def copy_on(engine, dst, src):
+            if engine == "vector":
+                nc.vector.tensor_copy(out=dst, in_=src)
+            else:
+                nc.scalar.copy(out=dst, in_=src)
+
+        def interleave(engine, grouped, planes, lo, hi):
+            copy_on(
+                engine,
+                grouped[:, lo:hi, :].rearrange("p (c i) j -> p c j i", i=4),
+                planes[:, :, lo:hi].rearrange("p j (c i) -> p c j i", i=4),
+            )
+
+        def quantize(name, grouped, width, fmt):
+            codes = held(name + "_codes", [P, width], U32)
+            scales = held(name + "_scales", [P, width], U8)
+            nc.vector.quantize_mx(out=codes[:].bitcast(fmt), scales=scales[:], in_=grouped)
+            return codes, scales, fmt
+
+        def product(bank, stationary, first, moving):
+            s_codes, s_scales, s_fmt = stationary
+            m_codes, m_scales, m_fmt = moving
+            nc.tensor.matmul_mx(
+                out=bank[:],
+                lhsT=s_codes[:, first : first + P].bitcast(s_fmt),
+                lhsT_scale=s_scales[:, first : first + P],
+                rhs=m_codes[:].bitcast(m_fmt),
+                rhs_scale=m_scales[:],
+                start=True,
+                stop=True,
+            )
+
+        offsets = keep.tile([P, N // 16], U16, name="offsets")
+        nc.sync.dma_start(offsets[:], offs)
+
+        ts_pool = held("ts_pool", [P, T], F32)
+        nc.sync.dma_start(out=ts_pool[P - 1 : P, :], in_=ts[0:1, :])
+        nc.vector.memset(ts_pool[0 : P - 1, :], 0.0)
+        rw_rows = held("rw_rows", [P, P], F32)
+        nc.sync.dma_start(out=rw_rows[P - CHUNKS : P, :], in_=rw[0].rearrange("(c p) o -> c (p o)", p=P))
+        nc.vector.memset(rw_rows[0 : P - CHUNKS, :], 0.0)
+
+        def load_pool(name, src):
+            planes = []
+            for j in range(PACK):
+                plane = held(name + str(j), [P, T], F32)
+                nc.sync.dma_start(out=plane[:], in_=src.rearrange("(p j) t -> p j t", j=PACK)[:, j, :])
+                planes.append(plane)
+            return planes
+
+        def load_columns(name, src, width):
+            parts = []
+            for h in range(R // width):
+                part = held(name + str(h), [P, PACK, width], F32)
+                rows = src[0].rearrange("(p j) r -> p j r", j=PACK)
+                nc.sync.dma_start(out=part[:], in_=rows[:, :, h * width : (h + 1) * width])
+                parts.append(part)
+            return parts
+
+        k_pool = load_pool("k_pool", kT)
+        q_raw = load_columns("q_raw", qT, Q_COLS)
+        v_pool = load_pool("v_pool", vT)
+        do_raw = load_columns("do_raw", doT, DO_COLS)
+
+        ident = held("ident", [P, P], F32)
+        make_identity(nc, ident[:])
+
+        ts_listed = held("ts_listed", [P, N], F32)
+        nc.vector.tensor_copy(out=ts_listed[:], in_=ts_pool[:].indirect(offsets[:]))
+        bank = ps_tr.tile([P, PACK, P], F32, name="tr")
+        for c in range(PACK):
+            nc.tensor.transpose(bank[:, c, :], ts_listed[:, c * P : (c + 1) * P], ident[:])
+        ts_col = held("ts_col", [P, PACK], F32)
+        nc.scalar.copy(out=ts_col[:], in_=bank[:, :, P - 1])
+        bank = ps_tr.tile([P, PACK, P], F32, name="tr")
+        for c in range(PACK):
+            nc.tensor.transpose(bank[:, c, :], ts_col[:, c : c + 1].to_broadcast([P, P]), ident[:])
+        ts_row = held("ts_row", [P, N], F32)
+        nc.scalar.copy(out=ts_row[:], in_=bank[:].rearrange("p c s -> p (c s)"))
+        bank = ps_tr.tile([P, PACK, P], F32, name="tr")
+        nc.tensor.transpose(bank[:, 0, :], rw_rows[:], ident[:])
+        rw2 = held("rw2", [P, CHUNKS], F32)
+        nc.scalar.mul(rw2[:], bank[:, 0, P - CHUNKS : P], 2.0)
+
+        k_listed = held("k_listed", [P, PACK, N], F32)
+        for j in range(PACK):
+            nc.vector.tensor_copy(out=k_listed[:, j, :], in_=k_pool[j][:].indirect(offsets[:]))
+        k_grouped = held("k_grouped", [P, N, PACK], BF16)
+        interleave("vector", k_grouped, k_listed, 0, N)
+        k_mx = quantize("k", k_grouped[:].rearrange("p s j -> p (s j)"), N, E4M3)
+
+        weights = []
+        for h in range(R // Q_COLS):
+            q_grouped = held("q_grouped" + str(h), [P, Q_COLS, PACK], BF16)
+            if h == 0:
+                interleave("scalar", q_grouped, q_raw[h], 0, Q_COLS // 2)
+                interleave("vector", q_grouped, q_raw[h], Q_COLS // 2, Q_COLS)
+            else:
+                interleave("scalar", q_grouped, q_raw[h], 0, Q_COLS // 2)
+                interleave("scalar", q_grouped, q_raw[h], Q_COLS // 2, Q_COLS)
+            q_mx = quantize("q" + str(h), q_grouped[:].rearrange("p r j -> p (r j)"), Q_COLS, E4M3)
+            relu_t = held("relu_t" + str(h), [P, PACK, Q_COLS], F32)
+            for c in range(PACK):
+                bank = ps_mm.tile([P, Q_COLS], F32, name="mm")
+                product(bank, k_mx, c * P, q_mx)
+                nc.scalar.activation(out=relu_t[:, c, :], in_=bank[:], func=RELU, scale=ts_col[:, c : c + 1])
+            for i in range(Q_COLS // P):
+                chunk = h * (Q_COLS // P) + i
+                bank = ps_tr.tile([P, PACK, P], F32, name="tr")
+                for c in range(PACK):
+                    nc.tensor.transpose(bank[:, c, :], relu_t[:, c, i * P : (i + 1) * P], ident[:])
+                weight = held("weight" + str(chunk), [P, N], F32)
+                nc.vector.scalar_tensor_tensor(
+                    out=weight[:],
+                    in0=bank[:].rearrange("p c s -> p (c s)"),
+                    scalar=rw2[:, chunk : chunk + 1],
+                    in1=ts_row[:],
+                    op0=MULT,
+                    op1=MULT,
+                )
+                weights.append(weight)
+
+        v_listed = held("v_listed", [P, PACK, N], F32)
+        for j in range(PACK - 1):
+            nc.vector.tensor_copy(out=v_listed[:, j, :], in_=v_pool[j][:].indirect(offsets[:]))
+        v_grouped = held("v_grouped", [P, N, PACK], BF16)
+        half = N // 2
+        for part, engine in ((0, "scalar"), (1, "vector")):
+            nc.vector.tensor_copy(
+                out=v_listed[:, PACK - 1, part * half : (part + 1) * half],
+                in_=v_pool[PACK - 1][:].indirect(offsets[:, part * half // 16 : (part + 1) * half // 16]),
+            )
+            interleave(engine, v_grouped, v_listed, part * half, (part + 1) * half)
+        v_mx = quantize("v", v_grouped[:].rearrange("p s j -> p (s j)"), N, E4M3)
+
+        kt_grouped = held("kt_grouped", [P, PACK, P, PACK], BF16)
+        for j in range(PACK):
+            bank = ps_tr.tile([P, PACK, P], F32, name="tr")
+            for t in range(PACK):
+                nc.tensor.transpose(bank[:, t, :], k_listed[:, j, t:N:PACK], ident[:])
+            nc.scalar.copy(out=kt_grouped[:, j, :, :], in_=bank[:].rearrange("m t p -> m p t"))
+        kt_mx = quantize("kt", kt_grouped[:].rearrange("m j p t -> m (j p t)"), D, E4M3)
+
+        do_mx = {}
+
+        def prepare_do(h):
+            do_grouped = held("do_grouped" + str(h), [P, DO_COLS, PACK], BF16)
+            interleave("scalar" if h < 2 else "vector", do_grouped, do_raw[h], 0, DO_COLS)
+            do_mx[h] = quantize("do" + str(h), do_grouped[:].rearrange("p r j -> p (r j)"), DO_COLS, E5M2)
+
+        for g, group in enumerate(GROUPS):
+            size = len(group)
+            turned = ps_tr.tile([P, size, 2, P], F32, name="tr")
+            for n, chunk in enumerate(group):
+                h, first = divmod(chunk * P, DO_COLS)
+                if h not in do_mx:
+                    prepare_do(h)
+                bank = ps_mm.tile([P, N], F32, name="mm")
+                product(bank, do_mx[h], first, v_mx)
+                ds = ring.tile([P, 2, P, 2], BF16, name="ds")
+                nc.vector.tensor_tensor(
+                    out=ds[:].rearrange("p u m e -> p m u e"),
+                    in0=bank[:].rearrange("p (m u e) -> p m u e", u=2, e=2),
+                    in1=weights[chunk][:].rearrange("p (m u e) -> p m u e", u=2, e=2),
+                    op=MULT,
+                )
+                words = ds[:].rearrange("p u m e -> p (u m e)").bitcast(F32)
+                for u in range(2):
+                    nc.tensor.transpose(turned[:, n, u, :], words[:, u * P : (u + 1) * P], ident[:])
+            ds_grouped = held("ds_grouped" + str(g), [P, size * P * PACK], BF16)
+            nc.scalar.copy(
+                out=ds_grouped[:].bitcast(F32).rearrange("m (n r u) -> m n r u", n=size, u=2),
+                in_=turned[:].rearrange("m n u r -> m n r u"),
+            )
+            ds_mx = quantize("ds" + str(g), ds_grouped[:], size * P, E5M2)
+            for n, chunk in enumerate(group):
+                bank = ps_out.tile([P, D], F32, name="gq")
+                product(bank, ds_mx, n * P, kt_mx)
+                result = ring.tile([P, P, PACK], F32, name="result")
+                nc.scalar.copy(out=result[:], in_=bank[:].rearrange("r (j p) -> r p j", j=PACK))
+                nc.sync.dma_start(
+                    out=out[0, chunk * P : (chunk + 1) * P, :],
+                    in_=result[:].rearrange("r p j -> r (p j)"),
+                )

@@ -12,14 +12,20 @@ E4M3 = mybir.dt.float8_e4m3fn_x4
 E5M2 = mybir.dt.float8_e5m2_x4
 MULT = mybir.AluOpType.mult
 RELU = mybir.ActivationFunctionType.Relu
+COPY = mybir.ActivationFunctionType.Copy
 
 P = 128
 PACK = 4
 N, T, D, R = 512, 2048, 512, 1024
 CHUNKS = R // P
 Q_COLS = 512
-DO_COLS = 256
-GROUPS = [(0, 1), (2, 3), (4, 5), (6,), (7,)]
+DO_WIDTHS = [256, 512, 256]
+Q_ENGINES = "svsv"
+DO_ENGINES = "sssv"
+OUT_ENGINES = "ssssssss"
+BANKS = [3, 3, 2]
+LOADS = "kkkkqqvvvvddd"
+ORDER = [("qi", 0), ("qi", 1), ("qq", 0), ("qi", 2), ("qi", 3), ("qq", 1), ("kt", 0), ("kt", 1), ("sc", 0), ("ts", 0), ("sc", 1), ("ts", 1), ("sc", 2), ("ts", 2), ("sc", 3), ("ts", 3), ("sc", 4), ("ts", 4), ("sc", 5), ("ts", 5), ("sc", 6), ("ts", 6), ("sc", 7), ("ts", 7), ("gv", 0), ("gv", 1), ("gv", 2), ("gv", 3), ("vq", 0), ("ktq", 0), ("w", 0), ("w", 1), ("w", 2), ("w", 3), ("di", 0), ("dq", 0), ("w", 4), ("w", 5), ("ds", 0), ("di", 1), ("dq", 1), ("tr", 0), ("ds", 1), ("w", 6), ("di", 2), ("dq", 2), ("g", 0), ("tr", 1), ("ds", 2), ("w", 7), ("g", 1), ("tr", 2), ("ds", 3), ("di", 3), ("dq", 3), ("g", 2), ("tr", 3), ("ds", 4), ("g", 3), ("tr", 4), ("ds", 5), ("g", 4), ("tr", 5), ("ds", 6), ("g", 5), ("tr", 6), ("ds", 7), ("g", 6), ("tr", 7), ("g", 7)]
 
 FLOPS = 3 * 2 * R * N * D
 
@@ -29,24 +35,24 @@ def tile_attend_gat_q_ts_kernel(tc, qT, kT, vT, doT, rw, ts, offs, out):
 
     with ExitStack() as ctx:
         keep = ctx.enter_context(tc.tile_pool(name="keep", bufs=1))
-        ring = ctx.enter_context(tc.tile_pool(name="ring", bufs=3))
-        ps_mm = ctx.enter_context(tc.psum_pool(name="ps_mm", bufs=3))
-        ps_tr = ctx.enter_context(tc.psum_pool(name="ps_tr", bufs=3))
-        ps_out = ctx.enter_context(tc.psum_pool(name="ps_out", bufs=2))
+        ring = ctx.enter_context(tc.tile_pool(name="ring", bufs=4))
+        ps_mm = ctx.enter_context(tc.psum_pool(name="ps_mm", bufs=BANKS[0]))
+        ps_tr = ctx.enter_context(tc.psum_pool(name="ps_tr", bufs=BANKS[1]))
+        ps_out = ctx.enter_context(tc.psum_pool(name="ps_out", bufs=BANKS[2]))
 
         def held(name, shape, dtype):
             return keep.tile(shape, dtype, name=name, align_bytes=64)
 
         def copy_on(engine, dst, src):
-            if engine == "vector":
+            if engine == "v":
                 nc.vector.tensor_copy(out=dst, in_=src)
             else:
                 nc.scalar.copy(out=dst, in_=src)
 
-        def interleave(engine, grouped, planes, lo, hi):
+        def interleave(engine, grouped, planes, lo, hi, at):
             copy_on(
                 engine,
-                grouped[:, lo:hi, :].rearrange("p (c i) j -> p c j i", i=4),
+                grouped[:, at : at + hi - lo, :].rearrange("p (c i) j -> p c j i", i=4),
                 planes[:, :, lo:hi].rearrange("p j (c i) -> p c j i", i=4),
             )
 
@@ -71,7 +77,6 @@ def tile_attend_gat_q_ts_kernel(tc, qT, kT, vT, doT, rw, ts, offs, out):
 
         offsets = keep.tile([P, N // 16], U16, name="offsets")
         nc.sync.dma_start(offsets[:], offs)
-
         ts_pool = held("ts_pool", [P, T], F32)
         nc.sync.dma_start(out=ts_pool[P - 1 : P, :], in_=ts[0:1, :])
         nc.vector.memset(ts_pool[0 : P - 1, :], 0.0)
@@ -79,27 +84,22 @@ def tile_attend_gat_q_ts_kernel(tc, qT, kT, vT, doT, rw, ts, offs, out):
         nc.sync.dma_start(out=rw_rows[P - CHUNKS : P, :], in_=rw[0].rearrange("(c p) o -> c (p o)", p=P))
         nc.vector.memset(rw_rows[0 : P - CHUNKS, :], 0.0)
 
-        def load_pool(name, src):
-            planes = []
-            for j in range(PACK):
-                plane = held(name + str(j), [P, T], F32)
+        k_pool, v_pool, q_raw, do_raw = [], [], [], []
+        for kind in LOADS:
+            if kind in "kv":
+                planes, src = (k_pool, kT) if kind == "k" else (v_pool, vT)
+                j = len(planes)
+                plane = held(kind + "_pool" + str(j), [P, T], F32)
                 nc.sync.dma_start(out=plane[:], in_=src.rearrange("(p j) t -> p j t", j=PACK)[:, j, :])
                 planes.append(plane)
-            return planes
-
-        def load_columns(name, src, width):
-            parts = []
-            for h in range(R // width):
-                part = held(name + str(h), [P, PACK, width], F32)
+            else:
+                parts, src, widths = (q_raw, qT, (Q_COLS, Q_COLS)) if kind == "q" else (do_raw, doT, DO_WIDTHS)
+                h = len(parts)
+                first = sum(widths[:h])
+                part = held(kind + "_raw" + str(h), [P, PACK, widths[h]], F32)
                 rows = src[0].rearrange("(p j) r -> p j r", j=PACK)
-                nc.sync.dma_start(out=part[:], in_=rows[:, :, h * width : (h + 1) * width])
-                parts.append(part)
-            return parts
-
-        k_pool = load_pool("k_pool", kT)
-        q_raw = load_columns("q_raw", qT, Q_COLS)
-        v_pool = load_pool("v_pool", vT)
-        do_raw = load_columns("do_raw", doT, DO_COLS)
+                nc.sync.dma_start(out=part[:], in_=rows[:, :, first : first + widths[h]])
+                parts.append((first, part))
 
         ident = held("ident", [P, P], F32)
         make_identity(nc, ident[:])
@@ -112,112 +112,116 @@ def tile_attend_gat_q_ts_kernel(tc, qT, kT, vT, doT, rw, ts, offs, out):
         ts_col = held("ts_col", [P, PACK], F32)
         nc.scalar.copy(out=ts_col[:], in_=bank[:, :, P - 1])
         bank = ps_tr.tile([P, PACK, P], F32, name="tr")
-        for c in range(PACK):
-            nc.tensor.transpose(bank[:, c, :], ts_col[:, c : c + 1].to_broadcast([P, P]), ident[:])
-        ts_row = held("ts_row", [P, N], F32)
-        nc.scalar.copy(out=ts_row[:], in_=bank[:].rearrange("p c s -> p (c s)"))
-        bank = ps_tr.tile([P, PACK, P], F32, name="tr")
         nc.tensor.transpose(bank[:, 0, :], rw_rows[:], ident[:])
         rw2 = held("rw2", [P, CHUNKS], F32)
         nc.scalar.mul(rw2[:], bank[:, 0, P - CHUNKS : P], 2.0)
 
-        k_listed = held("k_listed", [P, PACK, N], F32)
-        for j in range(PACK):
-            nc.vector.tensor_copy(out=k_listed[:, j, :], in_=k_pool[j][:].indirect(offsets[:]))
         k_grouped = held("k_grouped", [P, N, PACK], BF16)
-        interleave("vector", k_grouped, k_listed, 0, N)
-        k_mx = quantize("k", k_grouped[:].rearrange("p s j -> p (s j)"), N, E4M3)
-
-        weights = []
-        for h in range(R // Q_COLS):
-            q_grouped = held("q_grouped" + str(h), [P, Q_COLS, PACK], BF16)
-            if h == 0:
-                interleave("scalar", q_grouped, q_raw[h], 0, Q_COLS // 2)
-                interleave("vector", q_grouped, q_raw[h], Q_COLS // 2, Q_COLS)
-            else:
-                interleave("scalar", q_grouped, q_raw[h], 0, Q_COLS // 2)
-                interleave("scalar", q_grouped, q_raw[h], Q_COLS // 2, Q_COLS)
-            q_mx = quantize("q" + str(h), q_grouped[:].rearrange("p r j -> p (r j)"), Q_COLS, E4M3)
-            relu_t = held("relu_t" + str(h), [P, PACK, Q_COLS], F32)
-            for c in range(PACK):
-                bank = ps_mm.tile([P, Q_COLS], F32, name="mm")
-                product(bank, k_mx, c * P, q_mx)
-                nc.scalar.activation(out=relu_t[:, c, :], in_=bank[:], func=RELU, scale=ts_col[:, c : c + 1])
-            for i in range(Q_COLS // P):
-                chunk = h * (Q_COLS // P) + i
-                bank = ps_tr.tile([P, PACK, P], F32, name="tr")
-                for c in range(PACK):
-                    nc.tensor.transpose(bank[:, c, :], relu_t[:, c, i * P : (i + 1) * P], ident[:])
-                weight = held("weight" + str(chunk), [P, N], F32)
-                nc.vector.scalar_tensor_tensor(
-                    out=weight[:],
-                    in0=bank[:].rearrange("p c s -> p (c s)"),
-                    scalar=rw2[:, chunk : chunk + 1],
-                    in1=ts_row[:],
-                    op0=MULT,
-                    op1=MULT,
-                )
-                weights.append(weight)
-
-        v_listed = held("v_listed", [P, PACK, N], F32)
-        for j in range(PACK - 1):
-            nc.vector.tensor_copy(out=v_listed[:, j, :], in_=v_pool[j][:].indirect(offsets[:]))
-        v_grouped = held("v_grouped", [P, N, PACK], BF16)
-        half = N // 2
-        for part, engine in ((0, "scalar"), (1, "vector")):
-            nc.vector.tensor_copy(
-                out=v_listed[:, PACK - 1, part * half : (part + 1) * half],
-                in_=v_pool[PACK - 1][:].indirect(offsets[:, part * half // 16 : (part + 1) * half // 16]),
-            )
-            interleave(engine, v_grouped, v_listed, part * half, (part + 1) * half)
-        v_mx = quantize("v", v_grouped[:].rearrange("p s j -> p (s j)"), N, E4M3)
-
-        kt_grouped = held("kt_grouped", [P, PACK, P, PACK], BF16)
         for j in range(PACK):
+            nc.vector.tensor_copy(out=k_grouped[:, :, j], in_=k_pool[j][:].indirect(offsets[:]))
+        mx = {"k": quantize("k", k_grouped[:].rearrange("p s j -> p (s j)"), N, E4M3)}
+        k_words = k_grouped[:].rearrange("p s j -> p (s j)").bitcast(F32)
+        kt_grouped = held("kt_grouped", [P, 2, 2 * P, PACK], BF16)
+        v_grouped = held("v_grouped", [P, N, PACK], BF16)
+        q_grouped = [held("q_grouped" + str(h), [P, Q_COLS, PACK], BF16) for h in range(2)]
+        gated = [held("gated" + str(h), [P, PACK, Q_COLS], F32) for h in range(2)]
+        do_grouped = [held("do_grouped" + str(h), [P, 2 * P, PACK], BF16) for h in range(4)]
+        tiles = {}
+
+        def turn_keys(u):
             bank = ps_tr.tile([P, PACK, P], F32, name="tr")
             for t in range(PACK):
-                nc.tensor.transpose(bank[:, t, :], k_listed[:, j, t:N:PACK], ident[:])
-            nc.scalar.copy(out=kt_grouped[:, j, :, :], in_=bank[:].rearrange("m t p -> m p t"))
-        kt_mx = quantize("kt", kt_grouped[:].rearrange("m j p t -> m (j p t)"), D, E4M3)
+                nc.tensor.transpose(bank[:, t, :], k_words[:, 2 * t + u : 2 * N : 2 * PACK], ident[:])
+            nc.scalar.copy(out=kt_grouped[:, u, :, :], in_=bank[:].bitcast(BF16).rearrange("m t x -> m x t"))
 
-        do_mx = {}
+        def quantize_turned_keys(unused):
+            mx["kt"] = quantize("kt", kt_grouped[:].rearrange("m u x t -> m (u x t)"), D, E4M3)
 
-        def prepare_do(h):
-            do_grouped = held("do_grouped" + str(h), [P, DO_COLS, PACK], BF16)
-            interleave("scalar" if h < 2 else "vector", do_grouped, do_raw[h], 0, DO_COLS)
-            do_mx[h] = quantize("do" + str(h), do_grouped[:].rearrange("p r j -> p (r j)"), DO_COLS, E5M2)
+        def group_q(n):
+            h, part = divmod(n, 2)
+            lo = part * Q_COLS // 2
+            interleave(Q_ENGINES[n], q_grouped[h], q_raw[h][1], lo, lo + Q_COLS // 2, lo)
 
-        for g, group in enumerate(GROUPS):
-            size = len(group)
-            turned = ps_tr.tile([P, size, 2, P], F32, name="tr")
-            for n, chunk in enumerate(group):
-                h, first = divmod(chunk * P, DO_COLS)
-                if h not in do_mx:
-                    prepare_do(h)
-                bank = ps_mm.tile([P, N], F32, name="mm")
-                product(bank, do_mx[h], first, v_mx)
-                ds = ring.tile([P, 2, P, 2], BF16, name="ds")
-                nc.vector.tensor_tensor(
-                    out=ds[:].rearrange("p u m e -> p m u e"),
-                    in0=bank[:].rearrange("p (m u e) -> p m u e", u=2, e=2),
-                    in1=weights[chunk][:].rearrange("p (m u e) -> p m u e", u=2, e=2),
-                    op=MULT,
-                )
-                words = ds[:].rearrange("p u m e -> p (u m e)").bitcast(F32)
-                for u in range(2):
-                    nc.tensor.transpose(turned[:, n, u, :], words[:, u * P : (u + 1) * P], ident[:])
-            ds_grouped = held("ds_grouped" + str(g), [P, size * P * PACK], BF16)
-            nc.scalar.copy(
-                out=ds_grouped[:].bitcast(F32).rearrange("m (n r u) -> m n r u", n=size, u=2),
-                in_=turned[:].rearrange("m n u r -> m n r u"),
+        def quantize_q(h):
+            mx["q", h] = quantize("q" + str(h), q_grouped[h][:].rearrange("p r j -> p (r j)"), Q_COLS, E4M3)
+
+        def scores(n):
+            h, c = divmod(n, PACK)
+            bank = ps_mm.tile([P, Q_COLS], F32, name="mm")
+            product(bank, mx["k"], c * P, mx["q", h])
+            relu = ring.tile([P, Q_COLS], F32, name="relu")
+            nc.scalar.activation(out=relu[:], in_=bank[:], func=RELU, scale=ts_col[:, c : c + 1])
+            tiles["relu", n] = relu
+
+        def scale_again(n):
+            h, c = divmod(n, PACK)
+            nc.vector.tensor_scalar(
+                out=gated[h][:, c, :], in0=tiles["relu", n][:], scalar1=ts_col[:, c : c + 1], scalar2=None, op0=MULT
             )
-            ds_mx = quantize("ds" + str(g), ds_grouped[:], size * P, E5M2)
-            for n, chunk in enumerate(group):
-                bank = ps_out.tile([P, D], F32, name="gq")
-                product(bank, ds_mx, n * P, kt_mx)
-                result = ring.tile([P, P, PACK], F32, name="result")
-                nc.scalar.copy(out=result[:], in_=bank[:].rearrange("r (j p) -> r p j", j=PACK))
-                nc.sync.dma_start(
-                    out=out[0, chunk * P : (chunk + 1) * P, :],
-                    in_=result[:].rearrange("r p j -> r (p j)"),
-                )
+
+        def weights(chunk):
+            h, first = divmod(chunk * P, Q_COLS)
+            bank = ps_tr.tile([P, PACK, P], F32, name="tr")
+            for c in range(PACK):
+                nc.tensor.transpose(bank[:, c, :], gated[h][:, c, first : first + P], ident[:])
+            weight = held("weight" + str(chunk), [P, N], F32)
+            nc.scalar.activation(
+                out=weight[:], in_=bank[:].rearrange("p c s -> p (c s)"), func=COPY, scale=rw2[:, chunk : chunk + 1]
+            )
+            tiles["weight", chunk] = weight
+
+        def gather_v(j):
+            nc.vector.tensor_copy(out=v_grouped[:, :, j], in_=v_pool[j][:].indirect(offsets[:]))
+
+        def quantize_v(unused):
+            mx["v"] = quantize("v", v_grouped[:].rearrange("p s j -> p (s j)"), N, E4M3)
+
+        def group_do(h):
+            first, part = [x for x in do_raw if x[0] <= h * 2 * P][-1]
+            lo = h * 2 * P - first
+            interleave(DO_ENGINES[h], do_grouped[h], part, lo, lo + 2 * P, 0)
+
+        def quantize_do(h):
+            mx["do", h] = quantize("do" + str(h), do_grouped[h][:].rearrange("p r j -> p (r j)"), 2 * P, E5M2)
+
+        def make_ds(chunk):
+            h, first = divmod(chunk * P, 2 * P)
+            bank = ps_mm.tile([P, N], F32, name="mm")
+            product(bank, mx["do", h], first, mx["v"])
+            ds = ring.tile([P, 2, P, 2], BF16, name="ds")
+            nc.vector.tensor_tensor(
+                out=ds[:].rearrange("p u m e -> p m u e"),
+                in0=bank[:].rearrange("p (m u e) -> p m u e", u=2, e=2),
+                in1=tiles["weight", chunk][:].rearrange("p (m u e) -> p m u e", u=2, e=2),
+                op=MULT,
+            )
+            tiles["ds", chunk] = ds
+
+        def turn_ds(chunk):
+            words = tiles["ds", chunk][:].rearrange("p u m e -> p (u m e)").bitcast(F32)
+            turned = ps_tr.tile([P, 2, P], F32, name="tr")
+            for u in range(2):
+                nc.tensor.transpose(turned[:, u, :], words[:, u * P : (u + 1) * P], ident[:])
+            ds_grouped = held("ds_grouped" + str(chunk), [P, P * PACK], BF16)
+            nc.scalar.copy(
+                out=ds_grouped[:].bitcast(F32).rearrange("m (r u) -> m r u", u=2),
+                in_=turned[:].rearrange("m u r -> m r u"),
+            )
+            mx["ds", chunk] = quantize("ds" + str(chunk), ds_grouped[:], P, E5M2)
+
+        def finish(chunk):
+            bank = ps_out.tile([P, D], F32, name="gq")
+            product(bank, mx["ds", chunk], 0, mx["kt"])
+            result = held("result" + str(chunk), [P, P, 2, 2], F32)
+            copy_on(OUT_ENGINES[chunk], result[:], bank[:].rearrange("r (u p e) -> r p u e", u=2, e=2))
+            nc.sync.dma_start(
+                out=out[0, chunk * P : (chunk + 1) * P, :], in_=result[:].rearrange("r p u e -> r (p u e)")
+            )
+
+        steps = {
+            "kt": turn_keys, "ktq": quantize_turned_keys, "qi": group_q, "qq": quantize_q, "sc": scores,
+            "ts": scale_again, "w": weights, "gv": gather_v, "vq": quantize_v, "di": group_do, "dq": quantize_do,
+            "ds": make_ds, "tr": turn_ds, "g": finish,
+        }
+        for name, n in ORDER:
+            steps[name](n)

@@ -16,18 +16,22 @@ COPY = mybir.ActivationFunctionType.Copy
 
 P = 128
 PACK = 4
-N, T, D, R = 512, 2048, 512, 1024
-CHUNKS = R // P
+SLOTS, TOKENS, FEATURES, QUERIES = 512, 2048, 512, 1024
+CHUNKS = QUERIES // P
 Q_COLS = 512
-DO_WIDTHS = [256, 512, 256]
-Q_ENGINES = "svsv"
-DO_ENGINES = "sssv"
-OUT_ENGINES = "ssssssss"
-BANKS = [3, 3, 2]
-LOADS = "kkkkqqvvvvddd"
-ORDER = [("qi", 0), ("qi", 1), ("qq", 0), ("qi", 2), ("qi", 3), ("qq", 1), ("kt", 0), ("kt", 1), ("sc", 0), ("ts", 0), ("sc", 1), ("ts", 1), ("sc", 2), ("ts", 2), ("sc", 3), ("ts", 3), ("sc", 4), ("ts", 4), ("sc", 5), ("ts", 5), ("sc", 6), ("ts", 6), ("sc", 7), ("ts", 7), ("gv", 0), ("gv", 1), ("gv", 2), ("gv", 3), ("vq", 0), ("ktq", 0), ("w", 0), ("w", 1), ("w", 2), ("w", 3), ("di", 0), ("dq", 0), ("w", 4), ("w", 5), ("ds", 0), ("di", 1), ("dq", 1), ("tr", 0), ("ds", 1), ("w", 6), ("di", 2), ("dq", 2), ("g", 0), ("tr", 1), ("ds", 2), ("w", 7), ("g", 1), ("tr", 2), ("ds", 3), ("di", 3), ("dq", 3), ("g", 2), ("tr", 3), ("ds", 4), ("g", 3), ("tr", 4), ("ds", 5), ("g", 4), ("tr", 5), ("ds", 6), ("g", 5), ("tr", 6), ("ds", 7), ("g", 6), ("tr", 7), ("g", 7)]
+DO_COLS = 256
+TURN_LAG = 2
+OUT_LAG = 4
 
-FLOPS = 3 * 2 * R * N * D
+VECTOR, SCALAR = "vector", "scalar"
+Q_ENGINES = ((SCALAR, VECTOR), (VECTOR, VECTOR))
+DO_ENGINES = (VECTOR, SCALAR, VECTOR, SCALAR)
+RESULT_ENGINES = (SCALAR,) * 4 + (VECTOR, SCALAR) * 2
+
+GATED_ON = (None, "v_pool1")
+WEIGHTS_ON = (None, "do_raw0", None, "do_raw1")
+
+FLOPS = 3 * 2 * QUERIES * SLOTS * FEATURES
 
 
 def tile_attend_gat_q_ts_kernel(tc, qT, kT, vT, doT, rw, ts, offs, out):
@@ -35,32 +39,40 @@ def tile_attend_gat_q_ts_kernel(tc, qT, kT, vT, doT, rw, ts, offs, out):
 
     with ExitStack() as ctx:
         keep = ctx.enter_context(tc.tile_pool(name="keep", bufs=1))
-        ring = ctx.enter_context(tc.tile_pool(name="ring", bufs=4))
-        ps_mm = ctx.enter_context(tc.psum_pool(name="ps_mm", bufs=BANKS[0]))
-        ps_tr = ctx.enter_context(tc.psum_pool(name="ps_tr", bufs=BANKS[1]))
-        ps_out = ctx.enter_context(tc.psum_pool(name="ps_out", bufs=BANKS[2]))
+        ring = ctx.enter_context(tc.tile_pool(name="ring", bufs=TURN_LAG + 2))
+        ps_product = ctx.enter_context(tc.psum_pool(name="ps_product", bufs=3))
+        ps_turn = ctx.enter_context(tc.psum_pool(name="ps_turn", bufs=3))
+        ps_result = ctx.enter_context(tc.psum_pool(name="ps_result", bufs=2))
 
-        def held(name, shape, dtype):
-            return keep.tile(shape, dtype, name=name, align_bytes=64)
+        def held(name, shape, dtype, tag=None):
+            return keep.tile(shape, dtype, name=name, tag=tag or name, align_bytes=64)
 
         def copy_on(engine, dst, src):
-            if engine == "v":
+            if engine == VECTOR:
                 nc.vector.tensor_copy(out=dst, in_=src)
             else:
                 nc.scalar.copy(out=dst, in_=src)
 
-        def interleave(engine, grouped, planes, lo, hi, at):
+        def interleave(engine, grouped, planes):
             copy_on(
                 engine,
-                grouped[:, at : at + hi - lo, :].rearrange("p (c i) j -> p c j i", i=4),
-                planes[:, :, lo:hi].rearrange("p j (c i) -> p c j i", i=4),
+                grouped.rearrange("p (c i) j -> p c j i", i=4),
+                planes.rearrange("p j (c i) -> p c j i", i=4),
             )
 
-        def quantize(name, grouped, width, fmt):
-            codes = held(name + "_codes", [P, width], U32)
-            scales = held(name + "_scales", [P, width], U8)
-            nc.vector.quantize_mx(out=codes[:].bitcast(fmt), scales=scales[:], in_=grouped)
-            return codes, scales, fmt
+        def mx_tiles(name, width, fmt):
+            return held(name + "_codes", [P, width], U32), held(name + "_scales", [P, width], U8), fmt
+
+        def quantize(operand, cols, grouped):
+            codes, scales, fmt = operand
+            nc.vector.quantize_mx(
+                out=codes[:, cols].bitcast(fmt), scales=scales[:, cols], in_=grouped.rearrange("p w j -> p (w j)")
+            )
+
+        def quantized(name, grouped, width, fmt):
+            operand = mx_tiles(name, width, fmt)
+            quantize(operand, slice(0, width), grouped)
+            return operand
 
         def product(bank, stationary, first, moving):
             s_codes, s_scales, s_fmt = stationary
@@ -75,153 +87,154 @@ def tile_attend_gat_q_ts_kernel(tc, qT, kT, vT, doT, rw, ts, offs, out):
                 stop=True,
             )
 
-        offsets = keep.tile([P, N // 16], U16, name="offsets")
+        offsets = keep.tile([P, SLOTS // 16], U16, name="offsets")
         nc.sync.dma_start(offsets[:], offs)
-        ts_pool = held("ts_pool", [P, T], F32)
+        ts_pool = held("ts_pool", [P, TOKENS], F32)
         nc.sync.dma_start(out=ts_pool[P - 1 : P, :], in_=ts[0:1, :])
         nc.vector.memset(ts_pool[0 : P - 1, :], 0.0)
         rw_rows = held("rw_rows", [P, P], F32)
         nc.sync.dma_start(out=rw_rows[P - CHUNKS : P, :], in_=rw[0].rearrange("(c p) o -> c (p o)", p=P))
         nc.vector.memset(rw_rows[0 : P - CHUNKS, :], 0.0)
 
-        k_pool, v_pool, q_raw, do_raw = [], [], [], []
-        for kind in LOADS:
-            if kind in "kv":
-                planes, src = (k_pool, kT) if kind == "k" else (v_pool, vT)
-                j = len(planes)
-                plane = held(kind + "_pool" + str(j), [P, T], F32)
-                nc.sync.dma_start(out=plane[:], in_=src.rearrange("(p j) t -> p j t", j=PACK)[:, j, :])
-                planes.append(plane)
-            else:
-                parts, src, widths = (q_raw, qT, (Q_COLS, Q_COLS)) if kind == "q" else (do_raw, doT, DO_WIDTHS)
-                h = len(parts)
-                first = sum(widths[:h])
-                part = held(kind + "_raw" + str(h), [P, PACK, widths[h]], F32)
-                rows = src[0].rearrange("(p j) r -> p j r", j=PACK)
-                nc.sync.dma_start(out=part[:], in_=rows[:, :, first : first + widths[h]])
-                parts.append((first, part))
+        def load_plane(name, src, j):
+            plane = held(name + str(j), [P, TOKENS], F32)
+            nc.sync.dma_start(out=plane[:], in_=src.rearrange("(p j) t -> p j t", j=PACK)[:, j, :])
+            return plane
+
+        def load_part(name, src, width, h):
+            part = held(name + str(h), [P, PACK, width], F32)
+            rows = src[0].rearrange("(p j) r -> p j r", j=PACK)
+            nc.sync.dma_start(out=part[:], in_=rows[:, :, h * width : (h + 1) * width])
+            return part
+
+        k_pool = [load_plane("k_pool", kT, j) for j in range(PACK)]
+        q_raw = [load_part("q_raw", qT, Q_COLS, h) for h in range(QUERIES // Q_COLS)]
+        v_pool = [load_plane("v_pool", vT, j) for j in range(PACK // 2)]
+        do_raw = [load_part("do_raw", doT, DO_COLS, 0)]
+        v_pool += [load_plane("v_pool", vT, j) for j in range(PACK // 2, PACK)]
+        do_raw += [load_part("do_raw", doT, DO_COLS, h) for h in range(1, QUERIES // DO_COLS)]
 
         ident = held("ident", [P, P], F32)
         make_identity(nc, ident[:])
 
-        ts_listed = held("ts_listed", [P, N], F32)
+        ts_listed = held("ts_listed", [P, SLOTS], F32)
         nc.vector.tensor_copy(out=ts_listed[:], in_=ts_pool[:].indirect(offsets[:]))
-        bank = ps_tr.tile([P, PACK, P], F32, name="tr")
-        for c in range(PACK):
+        bank = ps_turn.tile([P, PACK, P], F32, name="turn")
+        for c in range(SLOTS // P):
             nc.tensor.transpose(bank[:, c, :], ts_listed[:, c * P : (c + 1) * P], ident[:])
-        ts_col = held("ts_col", [P, PACK], F32)
+        ts_col = held("ts_col", [P, SLOTS // P], F32)
         nc.scalar.copy(out=ts_col[:], in_=bank[:, :, P - 1])
-        bank = ps_tr.tile([P, PACK, P], F32, name="tr")
+        bank = ps_turn.tile([P, PACK, P], F32, name="turn")
         nc.tensor.transpose(bank[:, 0, :], rw_rows[:], ident[:])
         rw2 = held("rw2", [P, CHUNKS], F32)
         nc.scalar.mul(rw2[:], bank[:, 0, P - CHUNKS : P], 2.0)
 
-        k_grouped = held("k_grouped", [P, N, PACK], BF16)
-        for j in range(PACK):
-            nc.vector.tensor_copy(out=k_grouped[:, :, j], in_=k_pool[j][:].indirect(offsets[:]))
-        mx = {"k": quantize("k", k_grouped[:].rearrange("p s j -> p (s j)"), N, E4M3)}
-        k_words = k_grouped[:].rearrange("p s j -> p (s j)").bitcast(F32)
-        kt_grouped = held("kt_grouped", [P, 2, 2 * P, PACK], BF16)
-        v_grouped = held("v_grouped", [P, N, PACK], BF16)
-        q_grouped = [held("q_grouped" + str(h), [P, Q_COLS, PACK], BF16) for h in range(2)]
-        gated = [held("gated" + str(h), [P, PACK, Q_COLS], F32) for h in range(2)]
-        do_grouped = [held("do_grouped" + str(h), [P, 2 * P, PACK], BF16) for h in range(4)]
-        tiles = {}
+        def gather_pool(name, pool, tag=None):
+            listed = held(name + "_listed", [P, PACK, SLOTS], F32, tag=tag)
+            grouped = held(name + "_grouped", [P, SLOTS, PACK], BF16)
+            for j in range(PACK - 1):
+                nc.vector.tensor_copy(out=listed[:, j, :], in_=pool[j][:].indirect(offsets[:]))
+            halves = [slice(half * SLOTS // 2, (half + 1) * SLOTS // 2) for half in range(2)]
+            for cols in halves:
+                entries = offsets[:, cols.start // 16 : cols.stop // 16]
+                nc.vector.tensor_copy(out=listed[:, PACK - 1, cols], in_=pool[PACK - 1][:].indirect(entries))
+            for engine, cols in zip((SCALAR, VECTOR), halves):
+                interleave(engine, grouped[:, cols, :], listed[:, :, cols])
+            return listed, quantized(name, grouped[:], SLOTS, E4M3)
 
-        def turn_keys(u):
-            bank = ps_tr.tile([P, PACK, P], F32, name="tr")
-            for t in range(PACK):
-                nc.tensor.transpose(bank[:, t, :], k_words[:, 2 * t + u : 2 * N : 2 * PACK], ident[:])
-            nc.scalar.copy(out=kt_grouped[:, u, :, :], in_=bank[:].bitcast(BF16).rearrange("m t x -> m x t"))
+        k_listed, k_mx = gather_pool("k", k_pool)
 
-        def quantize_turned_keys(unused):
-            mx["kt"] = quantize("kt", kt_grouped[:].rearrange("m u x t -> m (u x t)"), D, E4M3)
+        do_mx = []
+        for h, part in enumerate(do_raw):
+            grouped = held("do_grouped" + str(h), [P, DO_COLS, PACK], BF16)
+            interleave(DO_ENGINES[h], grouped[:], part[:])
+            do_mx.append(quantized("do" + str(h), grouped[:], DO_COLS, E5M2))
 
-        def group_q(n):
-            h, part = divmod(n, 2)
-            lo = part * Q_COLS // 2
-            interleave(Q_ENGINES[n], q_grouped[h], q_raw[h][1], lo, lo + Q_COLS // 2, lo)
+        v_mx = gather_pool("v", v_pool, tag="ts_pool")[1]
 
-        def quantize_q(h):
-            mx["q", h] = quantize("q" + str(h), q_grouped[h][:].rearrange("p r j -> p (r j)"), Q_COLS, E4M3)
+        def prepare_queries(h):
+            grouped = held("q_grouped" + str(h), [P, Q_COLS, PACK], BF16)
+            for half in range(2):
+                cols = slice(half * Q_COLS // 2, (half + 1) * Q_COLS // 2)
+                interleave(Q_ENGINES[h][half], grouped[:, cols, :], q_raw[h][:, :, cols])
+            return quantized("q" + str(h), grouped[:], Q_COLS, E4M3)
 
-        def scores(n):
-            h, c = divmod(n, PACK)
-            bank = ps_mm.tile([P, Q_COLS], F32, name="mm")
-            product(bank, mx["k"], c * P, mx["q", h])
-            relu = ring.tile([P, Q_COLS], F32, name="relu")
-            nc.scalar.activation(out=relu[:], in_=bank[:], func=RELU, scale=ts_col[:, c : c + 1])
-            tiles["relu", n] = relu
+        kt_mx = mx_tiles("kt", FEATURES, E4M3)
 
-        def scale_again(n):
-            h, c = divmod(n, PACK)
-            nc.vector.tensor_scalar(
-                out=gated[h][:, c, :], in0=tiles["relu", n][:], scalar1=ts_col[:, c : c + 1], scalar2=None, op0=MULT
-            )
+        def turn_keys(pair, tag=None):
+            grouped = held("kt_grouped" + str(pair), [P, 2 * P, PACK], BF16, tag=tag)
+            for half in range(2):
+                bank = ps_turn.tile([P, PACK, P], F32, name="turn")
+                for t in range(PACK):
+                    nc.tensor.transpose(bank[:, t, :], k_listed[:, 2 * pair + half, t:SLOTS:PACK], ident[:])
+                nc.scalar.copy(out=grouped[:, half * P : (half + 1) * P, :], in_=bank[:].rearrange("m t p -> m p t"))
+            quantize(kt_mx, slice(pair * 2 * P, (pair + 1) * 2 * P), grouped[:])
 
-        def weights(chunk):
+        q_mx = [prepare_queries(0)]
+        turn_keys(0)
+        q_mx.append(prepare_queries(1))
+        turn_keys(1, tag="q_raw0")
+
+        gated = []
+        for h in range(QUERIES // Q_COLS):
+            gated.append(held("gated" + str(h), [P, SLOTS // P, Q_COLS], F32, tag=GATED_ON[h]))
+            for c in range(SLOTS // P):
+                bank = ps_product.tile([P, Q_COLS], F32, name="product")
+                product(bank, k_mx, c * P, q_mx[h])
+                relu = held("relu" + str(h) + str(c), [P, Q_COLS], F32)
+                nc.scalar.activation(out=relu[:], in_=bank[:], func=RELU, scale=ts_col[:, c : c + 1])
+                nc.vector.tensor_scalar(
+                    out=gated[h][:, c, :], in0=relu[:], scalar1=ts_col[:, c : c + 1], scalar2=None, op0=MULT
+                )
+
+        weights = []
+        for chunk in range(CHUNKS):
             h, first = divmod(chunk * P, Q_COLS)
-            bank = ps_tr.tile([P, PACK, P], F32, name="tr")
-            for c in range(PACK):
+            bank = ps_turn.tile([P, PACK, P], F32, name="turn")
+            for c in range(SLOTS // P):
                 nc.tensor.transpose(bank[:, c, :], gated[h][:, c, first : first + P], ident[:])
-            weight = held("weight" + str(chunk), [P, N], F32)
+            if chunk % 2 == 0:
+                pair = held("weights" + str(chunk // 2), [P, 2, 2, P, 2], F32, tag=WEIGHTS_ON[chunk // 2])
+            weight = pair[:, chunk % 2]
             nc.scalar.activation(
-                out=weight[:], in_=bank[:].rearrange("p c s -> p (c s)"), func=COPY, scale=rw2[:, chunk : chunk + 1]
+                out=weight,
+                in_=bank[:].rearrange("r c s -> r (c s)").rearrange("r (m u e) -> r u m e", u=2, e=2),
+                func=COPY,
+                scale=rw2[:, chunk : chunk + 1],
             )
-            tiles["weight", chunk] = weight
+            weights.append(weight)
 
-        def gather_v(j):
-            nc.vector.tensor_copy(out=v_grouped[:, :, j], in_=v_pool[j][:].indirect(offsets[:]))
-
-        def quantize_v(unused):
-            mx["v"] = quantize("v", v_grouped[:].rearrange("p s j -> p (s j)"), N, E4M3)
-
-        def group_do(h):
-            first, part = [x for x in do_raw if x[0] <= h * 2 * P][-1]
-            lo = h * 2 * P - first
-            interleave(DO_ENGINES[h], do_grouped[h], part, lo, lo + 2 * P, 0)
-
-        def quantize_do(h):
-            mx["do", h] = quantize("do" + str(h), do_grouped[h][:].rearrange("p r j -> p (r j)"), 2 * P, E5M2)
+        ds_tiles, ds_mx = [], []
 
         def make_ds(chunk):
-            h, first = divmod(chunk * P, 2 * P)
-            bank = ps_mm.tile([P, N], F32, name="mm")
-            product(bank, mx["do", h], first, mx["v"])
+            h, first = divmod(chunk * P, DO_COLS)
+            bank = ps_product.tile([P, SLOTS], F32, name="product")
+            product(bank, do_mx[h], first, v_mx)
             ds = ring.tile([P, 2, P, 2], BF16, name="ds")
             nc.vector.tensor_tensor(
-                out=ds[:].rearrange("p u m e -> p m u e"),
-                in0=bank[:].rearrange("p (m u e) -> p m u e", u=2, e=2),
-                in1=tiles["weight", chunk][:].rearrange("p (m u e) -> p m u e", u=2, e=2),
-                op=MULT,
+                out=ds[:], in0=bank[:].rearrange("r (m u e) -> r u m e", u=2, e=2), in1=weights[chunk], op=MULT
             )
-            tiles["ds", chunk] = ds
+            ds_tiles.append(ds)
 
         def turn_ds(chunk):
-            words = tiles["ds", chunk][:].rearrange("p u m e -> p (u m e)").bitcast(F32)
-            turned = ps_tr.tile([P, 2, P], F32, name="tr")
+            words = ds_tiles[chunk][:].rearrange("r u m e -> r (u m e)").bitcast(F32)
+            bank = ps_turn.tile([P, 2, P], F32, name="turn")
             for u in range(2):
-                nc.tensor.transpose(turned[:, u, :], words[:, u * P : (u + 1) * P], ident[:])
-            ds_grouped = held("ds_grouped" + str(chunk), [P, P * PACK], BF16)
-            nc.scalar.copy(
-                out=ds_grouped[:].bitcast(F32).rearrange("m (r u) -> m r u", u=2),
-                in_=turned[:].rearrange("m u r -> m r u"),
-            )
-            mx["ds", chunk] = quantize("ds" + str(chunk), ds_grouped[:], P, E5M2)
+                nc.tensor.transpose(bank[:, u, :], words[:, u * P : (u + 1) * P], ident[:])
+            grouped = held("ds_grouped" + str(chunk), [P, P, PACK], BF16)
+            nc.scalar.copy(out=grouped[:].bitcast(F32), in_=bank[:].rearrange("m u r -> m r u"))
+            ds_mx.append(quantized("ds" + str(chunk), grouped[:], P, E5M2))
 
         def finish(chunk):
-            bank = ps_out.tile([P, D], F32, name="gq")
-            product(bank, mx["ds", chunk], 0, mx["kt"])
-            result = held("result" + str(chunk), [P, P, 2, 2], F32)
-            copy_on(OUT_ENGINES[chunk], result[:], bank[:].rearrange("r (u p e) -> r p u e", u=2, e=2))
+            bank = ps_result.tile([P, FEATURES], F32, name="result_bank")
+            product(bank, ds_mx[chunk], 0, kt_mx)
+            result = held("result" + str(chunk), [P, P, PACK], F32)
+            copy_on(RESULT_ENGINES[chunk], result[:], bank[:].rearrange("r (j p) -> r p j", j=PACK))
             nc.sync.dma_start(
-                out=out[0, chunk * P : (chunk + 1) * P, :], in_=result[:].rearrange("r p u e -> r (p u e)")
+                out=out[0, chunk * P : (chunk + 1) * P, :], in_=result[:].rearrange("r p j -> r (p j)")
             )
 
-        steps = {
-            "kt": turn_keys, "ktq": quantize_turned_keys, "qi": group_q, "qq": quantize_q, "sc": scores,
-            "ts": scale_again, "w": weights, "gv": gather_v, "vq": quantize_v, "di": group_do, "dq": quantize_do,
-            "ds": make_ds, "tr": turn_ds, "g": finish,
-        }
-        for name, n in ORDER:
-            steps[name](n)
+        for step in range(CHUNKS + OUT_LAG):
+            for stage, lag in ((make_ds, 0), (turn_ds, TURN_LAG), (finish, OUT_LAG)):
+                if 0 <= step - lag < CHUNKS:
+                    stage(step - lag)

@@ -16,12 +16,16 @@ COPY = mybir.ActivationFunctionType.Copy
 
 P = 128
 PACK = 4
+LIST_ROWS = 16
+LINE = 4
 SLOTS, TOKENS, FEATURES, QUERIES = 512, 2048, 512, 1024
 CHUNKS = QUERIES // P
 Q_COLS = 512
 DO_COLS = 256
+SLOT_TILES = SLOTS // P
 TURN_LAG = 2
 OUT_LAG = 4
+HALVED_CHUNKS = 2
 
 VECTOR, SCALAR = "vector", "scalar"
 Q_ENGINES = ((SCALAR, VECTOR), (VECTOR, VECTOR))
@@ -56,8 +60,8 @@ def tile_attend_gat_q_ts_kernel(tc, qT, kT, vT, doT, rw, ts, offs, out):
         def interleave(engine, grouped, planes):
             copy_on(
                 engine,
-                grouped.rearrange("p (c i) j -> p c j i", i=4),
-                planes.rearrange("p j (c i) -> p c j i", i=4),
+                grouped.rearrange("p (run x) j -> p run j x", x=LINE),
+                planes.rearrange("p j (run x) -> p run j x", x=LINE),
             )
 
         def mx_tiles(name, width, fmt):
@@ -66,7 +70,7 @@ def tile_attend_gat_q_ts_kernel(tc, qT, kT, vT, doT, rw, ts, offs, out):
         def quantize(operand, cols, grouped):
             codes, scales, fmt = operand
             nc.vector.quantize_mx(
-                out=codes[:, cols].bitcast(fmt), scales=scales[:, cols], in_=grouped.rearrange("p w j -> p (w j)")
+                out=codes[:, cols].bitcast(fmt), scales=scales[:, cols], in_=grouped.rearrange("p col j -> p (col j)")
             )
 
         def quantized(name, grouped, width, fmt):
@@ -87,18 +91,17 @@ def tile_attend_gat_q_ts_kernel(tc, qT, kT, vT, doT, rw, ts, offs, out):
                 stop=True,
             )
 
-        offsets = keep.tile([P, SLOTS // 16], U16, name="offsets")
-        nc.sync.dma_start(offsets[:], offs)
+        offsets = keep.tile([P, SLOTS // LIST_ROWS], U16, name="offsets")
         ts_pool = held("ts_pool", [P, TOKENS], F32)
-        nc.sync.dma_start(out=ts_pool[P - 1 : P, :], in_=ts[0:1, :])
+        nc.scalar.dma_start(out=ts_pool[P - 1 : P, :], in_=ts[0:1, :])
         nc.vector.memset(ts_pool[0 : P - 1, :], 0.0)
         rw_rows = held("rw_rows", [P, P], F32)
-        nc.sync.dma_start(out=rw_rows[P - CHUNKS : P, :], in_=rw[0].rearrange("(c p) o -> c (p o)", p=P))
+        nc.scalar.dma_start(out=rw_rows[P - CHUNKS : P, :], in_=rw[0].rearrange("(chunk p) one -> chunk (p one)", p=P))
         nc.vector.memset(rw_rows[0 : P - CHUNKS, :], 0.0)
 
         def load_plane(name, src, j):
             plane = held(name + str(j), [P, TOKENS], F32)
-            nc.sync.dma_start(out=plane[:], in_=src.rearrange("(p j) t -> p j t", j=PACK)[:, j, :])
+            nc.sync.dma_start(out=plane[:], in_=src.rearrange("(p j) token -> p j token", j=PACK)[:, j, :])
             return plane
 
         def load_part(name, src, width, h):
@@ -107,7 +110,9 @@ def tile_attend_gat_q_ts_kernel(tc, qT, kT, vT, doT, rw, ts, offs, out):
             nc.sync.dma_start(out=part[:], in_=rows[:, :, h * width : (h + 1) * width])
             return part
 
-        k_pool = [load_plane("k_pool", kT, j) for j in range(PACK)]
+        k_pool = [load_plane("k_pool", kT, 0)]
+        nc.sync.dma_start(offsets[:], offs)
+        k_pool += [load_plane("k_pool", kT, j) for j in range(1, PACK)]
         q_raw = [load_part("q_raw", qT, Q_COLS, h) for h in range(QUERIES // Q_COLS)]
         v_pool = [load_plane("v_pool", vT, j) for j in range(PACK // 2)]
         do_raw = [load_part("do_raw", doT, DO_COLS, 0)]
@@ -119,10 +124,10 @@ def tile_attend_gat_q_ts_kernel(tc, qT, kT, vT, doT, rw, ts, offs, out):
 
         ts_listed = held("ts_listed", [P, SLOTS], F32)
         nc.vector.tensor_copy(out=ts_listed[:], in_=ts_pool[:].indirect(offsets[:]))
-        bank = ps_turn.tile([P, PACK, P], F32, name="turn")
-        for c in range(SLOTS // P):
+        bank = ps_turn.tile([P, SLOT_TILES, P], F32, name="turn")
+        for c in range(SLOT_TILES):
             nc.tensor.transpose(bank[:, c, :], ts_listed[:, c * P : (c + 1) * P], ident[:])
-        ts_col = held("ts_col", [P, SLOTS // P], F32)
+        ts_col = held("ts_col", [P, SLOT_TILES], F32)
         nc.scalar.copy(out=ts_col[:], in_=bank[:, :, P - 1])
         bank = ps_turn.tile([P, PACK, P], F32, name="turn")
         nc.tensor.transpose(bank[:, 0, :], rw_rows[:], ident[:])
@@ -136,7 +141,7 @@ def tile_attend_gat_q_ts_kernel(tc, qT, kT, vT, doT, rw, ts, offs, out):
                 nc.vector.tensor_copy(out=listed[:, j, :], in_=pool[j][:].indirect(offsets[:]))
             halves = [slice(half * SLOTS // 2, (half + 1) * SLOTS // 2) for half in range(2)]
             for cols in halves:
-                entries = offsets[:, cols.start // 16 : cols.stop // 16]
+                entries = offsets[:, cols.start // LIST_ROWS : cols.stop // LIST_ROWS]
                 nc.vector.tensor_copy(out=listed[:, PACK - 1, cols], in_=pool[PACK - 1][:].indirect(entries))
             for engine, cols in zip((SCALAR, VECTOR), halves):
                 interleave(engine, grouped[:, cols, :], listed[:, :, cols])
@@ -177,8 +182,8 @@ def tile_attend_gat_q_ts_kernel(tc, qT, kT, vT, doT, rw, ts, offs, out):
 
         gated = []
         for h in range(QUERIES // Q_COLS):
-            gated.append(held("gated" + str(h), [P, SLOTS // P, Q_COLS], F32, tag=GATED_ON[h]))
-            for c in range(SLOTS // P):
+            gated.append(held("gated" + str(h), [P, SLOT_TILES, Q_COLS], F32, tag=GATED_ON[h]))
+            for c in range(SLOT_TILES):
                 bank = ps_product.tile([P, Q_COLS], F32, name="product")
                 product(bank, k_mx, c * P, q_mx[h])
                 relu = held("relu" + str(h) + str(c), [P, Q_COLS], F32)
@@ -190,15 +195,15 @@ def tile_attend_gat_q_ts_kernel(tc, qT, kT, vT, doT, rw, ts, offs, out):
         weights = []
         for chunk in range(CHUNKS):
             h, first = divmod(chunk * P, Q_COLS)
-            bank = ps_turn.tile([P, PACK, P], F32, name="turn")
-            for c in range(SLOTS // P):
+            bank = ps_turn.tile([P, SLOT_TILES, P], F32, name="turn")
+            for c in range(SLOT_TILES):
                 nc.tensor.transpose(bank[:, c, :], gated[h][:, c, first : first + P], ident[:])
             if chunk % 2 == 0:
-                pair = held("weights" + str(chunk // 2), [P, 2, 2, P, 2], F32, tag=WEIGHTS_ON[chunk // 2])
-            weight = pair[:, chunk % 2]
+                two_weights = held("weights" + str(chunk // 2), [P, 2, 2, P, 2], F32, tag=WEIGHTS_ON[chunk // 2])
+            weight = two_weights[:, chunk % 2]
             nc.scalar.activation(
                 out=weight,
-                in_=bank[:].rearrange("r c s -> r (c s)").rearrange("r (m u e) -> r u m e", u=2, e=2),
+                in_=bank[:].rearrange("r c p -> r (c p)").rearrange("r (m u z) -> r u m z", u=2, z=2),
                 func=COPY,
                 scale=rw2[:, chunk : chunk + 1],
             )
@@ -212,12 +217,12 @@ def tile_attend_gat_q_ts_kernel(tc, qT, kT, vT, doT, rw, ts, offs, out):
             product(bank, do_mx[h], first, v_mx)
             ds = ring.tile([P, 2, P, 2], BF16, name="ds")
             nc.vector.tensor_tensor(
-                out=ds[:], in0=bank[:].rearrange("r (m u e) -> r u m e", u=2, e=2), in1=weights[chunk], op=MULT
+                out=ds[:], in0=bank[:].rearrange("r (m u z) -> r u m z", u=2, z=2), in1=weights[chunk], op=MULT
             )
             ds_tiles.append(ds)
 
         def turn_ds(chunk):
-            words = ds_tiles[chunk][:].rearrange("r u m e -> r (u m e)").bitcast(F32)
+            words = ds_tiles[chunk][:].rearrange("r u m z -> r (u m z)").bitcast(F32)
             bank = ps_turn.tile([P, 2, P], F32, name="turn")
             for u in range(2):
                 nc.tensor.transpose(bank[:, u, :], words[:, u * P : (u + 1) * P], ident[:])
@@ -229,10 +234,15 @@ def tile_attend_gat_q_ts_kernel(tc, qT, kT, vT, doT, rw, ts, offs, out):
             bank = ps_result.tile([P, FEATURES], F32, name="result_bank")
             product(bank, ds_mx[chunk], 0, kt_mx)
             result = held("result" + str(chunk), [P, P, PACK], F32)
-            copy_on(RESULT_ENGINES[chunk], result[:], bank[:].rearrange("r (j p) -> r p j", j=PACK))
-            nc.sync.dma_start(
-                out=out[0, chunk * P : (chunk + 1) * P, :], in_=result[:].rearrange("r p j -> r (p j)")
-            )
+            pieces = 2 if chunk >= CHUNKS - HALVED_CHUNKS else 1
+            for piece in range(pieces):
+                span = slice(piece * P // pieces, (piece + 1) * P // pieces)
+                ordered = bank[:].rearrange("r (j p) -> r p j", j=PACK)[:, span, :]
+                copy_on(RESULT_ENGINES[chunk], result[:, span, :], ordered)
+                nc.sync.dma_start(
+                    out=out[0, chunk * P : (chunk + 1) * P, span.start * PACK : span.stop * PACK],
+                    in_=result[:, span, :].rearrange("r p j -> r (p j)"),
+                )
 
         for step in range(CHUNKS + OUT_LAG):
             for stage, lag in ((make_ds, 0), (turn_ds, TURN_LAG), (finish, OUT_LAG)):

@@ -11,6 +11,7 @@ U8 = mybir.dt.uint8
 E4M3 = mybir.dt.float8_e4m3fn_x4
 E5M2 = mybir.dt.float8_e5m2_x4
 MULT = mybir.AluOpType.mult
+ADD = mybir.AluOpType.add
 RELU = mybir.ActivationFunctionType.Relu
 COPY = mybir.ActivationFunctionType.Copy
 
@@ -21,20 +22,38 @@ LINE = 4
 SLOTS, TOKENS, FEATURES, QUERIES = 512, 2048, 512, 1024
 CHUNKS = QUERIES // P
 Q_COLS = 512
-DO_COLS = 256
+DO_COLS = 512
 SLOT_TILES = SLOTS // P
-TURN_LAG = 2
-OUT_LAG = 4
-HALVED_CHUNKS = 2
+UNITS = ((0,), (1,), (2,), (3,), (4,), (5,), (6,), (7,))
+HALVED_CHUNKS = 0
 
-VECTOR, SCALAR = "vector", "scalar"
+VECTOR, SCALAR, GPSIMD = "vector", "scalar", "gpsimd"
 Q_ENGINES = ((SCALAR, VECTOR), (VECTOR, VECTOR))
-DO_ENGINES = (VECTOR, SCALAR, VECTOR, SCALAR)
-RESULT_ENGINES = (SCALAR,) * 4 + (VECTOR, SCALAR) * 2
+DO_PIECES = ((128, SCALAR, None), (128, SCALAR, None), (256, VECTOR, "do_grouped0"), (256, SCALAR, None), (256, SCALAR, None))
+RESULT_ENGINES = (SCALAR, SCALAR, SCALAR, SCALAR, VECTOR, SCALAR, VECTOR, SCALAR)
 
-GATED_ON = (None, "v_pool1")
-WEIGHTS_ON = (None, "do_raw0", None, "do_raw1")
+GATED_ON = ("k_pool0", "k_pool1")
+WEIGHTS_ON = ("k_pool2", "k_pool3", None, None, None, None, None, None)
 
+KT_EARLY = 2
+KT_CALLS = ((0, 2), (2, 2))
+KT_ON = "v_pool1"
+LAGS = (1, 2)
+
+VECTOR_WEIGHTS = (0, 0)
+POOL_SPLIT = 256
+POOL_ENGINES = {"k": (SCALAR, VECTOR), "v": (SCALAR, VECTOR)}
+SECOND_GRADIENT_STEP = 2
+BANK, BANKS = 512, 8
+BANKS_OF = {"score": (0, 1, 2), "turn": (3, 4, 5, 6, 7), "dp": (0, 1, 2), "ds": (3, 4), "result": (5, 6, 7)}
+WEAVE_SPLIT = {"k": 192, "v": 192}
+TWICE_ON = ("q_grouped1", None)
+KT_LATE_ON = "q_raw0"
+EARLY_PIECES = 3
+ORDER = "s0 s1 w0 w1 w2 w3 w4 w5 w6 w7 d0 t0 d1 t1 d2 g3 q0 t2 d3 f0 q1 t3 d4 f1 g4 q2 t4 d5 f2 q3 t5 d6 f3 q4 t6 d7 f4 q5 t7 f5 q6 f6 q7 f7"
+LOADS = "k k k k q q v v v v o o"
+FIRST = "g0 g1 g2 a0 a1"
+TWICE_ENGINES = (VECTOR, VECTOR)
 FLOPS = 3 * 2 * QUERIES * SLOTS * FEATURES
 
 
@@ -43,10 +62,14 @@ def tile_attend_gat_q_ts_kernel(tc, qT, kT, vT, doT, rw, ts, offs, out):
 
     with ExitStack() as ctx:
         keep = ctx.enter_context(tc.tile_pool(name="keep", bufs=1))
-        ring = ctx.enter_context(tc.tile_pool(name="ring", bufs=TURN_LAG + 2))
-        ps_product = ctx.enter_context(tc.psum_pool(name="ps_product", bufs=3))
-        ps_turn = ctx.enter_context(tc.psum_pool(name="ps_turn", bufs=3))
-        ps_result = ctx.enter_context(tc.psum_pool(name="ps_result", bufs=2))
+        psum = ctx.enter_context(tc.psum_pool(name="psum", bufs=1))
+        banks = [psum.tile([P, BANK], F32, name="bank" + str(b)) for b in range(BANKS)]
+        uses = {role: [] for role in BANKS_OF}
+
+        def next_bank(role):
+            numbers = BANKS_OF[role]
+            uses[role].append(numbers[len(uses[role]) % len(numbers)])
+            return banks[uses[role][-1]][:]
 
         def held(name, shape, dtype, tag=None):
             return keep.tile(shape, dtype, name=name, tag=tag or name, align_bytes=64)
@@ -54,6 +77,8 @@ def tile_attend_gat_q_ts_kernel(tc, qT, kT, vT, doT, rw, ts, offs, out):
         def copy_on(engine, dst, src):
             if engine == VECTOR:
                 nc.vector.tensor_copy(out=dst, in_=src)
+            elif engine == GPSIMD:
+                nc.gpsimd.tensor_copy(out=dst, in_=src)
             else:
                 nc.scalar.copy(out=dst, in_=src)
 
@@ -62,6 +87,13 @@ def tile_attend_gat_q_ts_kernel(tc, qT, kT, vT, doT, rw, ts, offs, out):
                 engine,
                 grouped.rearrange("p (run x) j -> p run j x", x=LINE),
                 planes.rearrange("p j (run x) -> p run j x", x=LINE),
+            )
+
+        def interleave_dealt(engine, grouped, planes, span):
+            copy_on(
+                engine,
+                grouped.rearrange("p (u m z) j -> p m j u z", u=2, z=2)[:, span],
+                planes.rearrange("p j (m u z) -> p m j u z", u=2, z=2)[:, span],
             )
 
         def mx_tiles(name, width, fmt):
@@ -82,7 +114,7 @@ def tile_attend_gat_q_ts_kernel(tc, qT, kT, vT, doT, rw, ts, offs, out):
             s_codes, s_scales, s_fmt = stationary
             m_codes, m_scales, m_fmt = moving
             nc.tensor.matmul_mx(
-                out=bank[:],
+                out=bank,
                 lhsT=s_codes[:, first : first + P].bitcast(s_fmt),
                 lhsT_scale=s_scales[:, first : first + P],
                 rhs=m_codes[:].bitcast(m_fmt),
@@ -110,141 +142,193 @@ def tile_attend_gat_q_ts_kernel(tc, qT, kT, vT, doT, rw, ts, offs, out):
             nc.sync.dma_start(out=part[:], in_=rows[:, :, h * width : (h + 1) * width])
             return part
 
-        k_pool = [load_plane("k_pool", kT, 0)]
         nc.sync.dma_start(offsets[:], offs)
-        k_pool += [load_plane("k_pool", kT, j) for j in range(1, PACK)]
-        q_raw = [load_part("q_raw", qT, Q_COLS, h) for h in range(QUERIES // Q_COLS)]
-        v_pool = [load_plane("v_pool", vT, j) for j in range(PACK // 2)]
-        do_raw = [load_part("do_raw", doT, DO_COLS, 0)]
-        v_pool += [load_plane("v_pool", vT, j) for j in range(PACK // 2, PACK)]
-        do_raw += [load_part("do_raw", doT, DO_COLS, h) for h in range(1, QUERIES // DO_COLS)]
+        k_pool, v_pool, q_raw, do_raw = [], [], [], []
+        for load in LOADS.split():
+            if load == "k":
+                k_pool.append(load_plane("k_pool", kT, len(k_pool)))
+            elif load == "v":
+                v_pool.append(load_plane("v_pool", vT, len(v_pool)))
+            elif load == "q":
+                q_raw.append(load_part("q_raw", qT, Q_COLS, len(q_raw)))
+            else:
+                do_raw.append(load_part("do_raw", doT, DO_COLS, len(do_raw)))
 
         ident = held("ident", [P, P], F32)
         make_identity(nc, ident[:])
 
         ts_listed = held("ts_listed", [P, SLOTS], F32)
         nc.vector.tensor_copy(out=ts_listed[:], in_=ts_pool[:].indirect(offsets[:]))
-        bank = ps_turn.tile([P, SLOT_TILES, P], F32, name="turn")
+        ts_dealt = held("ts_dealt", [P, SLOTS], F32)
+        nc.scalar.copy(
+            out=ts_dealt[:].rearrange("p (u m z) -> p u m z", u=2, z=2),
+            in_=ts_listed[:].rearrange("p (m u z) -> p u m z", u=2, z=2),
+        )
+        bank = next_bank("turn").rearrange("p (c x) -> p c x", x=P)
         for c in range(SLOT_TILES):
-            nc.tensor.transpose(bank[:, c, :], ts_listed[:, c * P : (c + 1) * P], ident[:])
+            nc.tensor.transpose(bank[:, c, :], ts_dealt[:, c * P : (c + 1) * P], ident[:])
         ts_col = held("ts_col", [P, SLOT_TILES], F32)
         nc.scalar.copy(out=ts_col[:], in_=bank[:, :, P - 1])
-        bank = ps_turn.tile([P, PACK, P], F32, name="turn")
+        bank = next_bank("turn").rearrange("p (c x) -> p c x", x=P)
+        for c in range(SLOT_TILES):
+            nc.tensor.transpose(bank[:, c, :], ts_col[:, c : c + 1].to_broadcast([P, P]), ident[:])
+        ts_row = held("ts_row", [P, SLOTS], F32)
+        nc.scalar.copy(out=ts_row[:], in_=bank.rearrange("r c p -> r (c p)"))
+        bank = next_bank("turn").rearrange("p (c x) -> p c x", x=P)
         nc.tensor.transpose(bank[:, 0, :], rw_rows[:], ident[:])
         rw2 = held("rw2", [P, CHUNKS], F32)
         nc.scalar.mul(rw2[:], bank[:, 0, P - CHUNKS : P], 2.0)
 
-        def gather_pool(name, pool, tag=None):
+        def gather_pool(name, pool, split, dealt, tag=None):
             listed = held(name + "_listed", [P, PACK, SLOTS], F32, tag=tag)
             grouped = held(name + "_grouped", [P, SLOTS, PACK], BF16)
             for j in range(PACK - 1):
                 nc.vector.tensor_copy(out=listed[:, j, :], in_=pool[j][:].indirect(offsets[:]))
-            halves = [slice(half * SLOTS // 2, (half + 1) * SLOTS // 2) for half in range(2)]
+            halves = [slice(0, split), slice(split, SLOTS)]
             for cols in halves:
                 entries = offsets[:, cols.start // LIST_ROWS : cols.stop // LIST_ROWS]
                 nc.vector.tensor_copy(out=listed[:, PACK - 1, cols], in_=pool[PACK - 1][:].indirect(entries))
-            for engine, cols in zip((SCALAR, VECTOR), halves):
-                interleave(engine, grouped[:, cols, :], listed[:, :, cols])
+            for engine, cols in zip(POOL_ENGINES[name], (slice(0, WEAVE_SPLIT[name]), slice(WEAVE_SPLIT[name], SLOTS))):
+                if dealt:
+                    interleave_dealt(engine, grouped[:], listed[:], slice(cols.start // PACK, cols.stop // PACK))
+                else:
+                    interleave(engine, grouped[:, cols, :], listed[:, :, cols])
             return listed, quantized(name, grouped[:], SLOTS, E4M3)
 
-        k_listed, k_mx = gather_pool("k", k_pool)
+        k_listed, k_mx = gather_pool("k", k_pool, POOL_SPLIT, True)
+
+        v_mx = gather_pool("v", v_pool, POOL_SPLIT, False, tag="ts_pool")[1]
 
         do_mx = []
-        for h, part in enumerate(do_raw):
-            grouped = held("do_grouped" + str(h), [P, DO_COLS, PACK], BF16)
-            interleave(DO_ENGINES[h], grouped[:], part[:])
-            do_mx.append(quantized("do" + str(h), grouped[:], DO_COLS, E5M2))
 
-        v_mx = gather_pool("v", v_pool, tag="ts_pool")[1]
+        def prepare_gradient(piece):
+            width, engine, tag = DO_PIECES[piece]
+            h, first = divmod(len(do_mx) * P, DO_COLS)
+            grouped = held("do_grouped" + str(piece), [P, width, PACK], BF16, tag=tag)
+            interleave(engine, grouped[:], do_raw[h][:, :, first : first + width])
+            operand = quantized("do" + str(piece), grouped[:], width, E5M2)
+            do_mx.extend((operand, col) for col in range(0, width, P))
+
 
         def prepare_queries(h):
             grouped = held("q_grouped" + str(h), [P, Q_COLS, PACK], BF16)
             for half in range(2):
                 cols = slice(half * Q_COLS // 2, (half + 1) * Q_COLS // 2)
                 interleave(Q_ENGINES[h][half], grouped[:, cols, :], q_raw[h][:, :, cols])
-            return quantized("q" + str(h), grouped[:], Q_COLS, E4M3)
+            q_mx.append(quantized("q" + str(h), grouped[:], Q_COLS, E4M3))
 
-        kt_mx = mx_tiles("kt", FEATURES, E4M3)
+        def turn_keys(grouped, col, j):
+            bank = next_bank("turn").rearrange("p (c x) -> p c x", x=P)
+            for t in range(PACK):
+                nc.tensor.transpose(bank[:, t, :], k_listed[:, j, t:SLOTS:PACK], ident[:])
+            nc.scalar.copy(out=grouped[:, col * P : (col + 1) * P, :], in_=bank.rearrange("m t p -> m p t"))
 
-        def turn_keys(pair, tag=None):
-            grouped = held("kt_grouped" + str(pair), [P, 2 * P, PACK], BF16, tag=tag)
-            for half in range(2):
-                bank = ps_turn.tile([P, PACK, P], F32, name="turn")
-                for t in range(PACK):
-                    nc.tensor.transpose(bank[:, t, :], k_listed[:, 2 * pair + half, t:SLOTS:PACK], ident[:])
-                nc.scalar.copy(out=grouped[:, half * P : (half + 1) * P, :], in_=bank[:].rearrange("m t p -> m p t"))
-            quantize(kt_mx, slice(pair * 2 * P, (pair + 1) * 2 * P), grouped[:])
-
-        q_mx = [prepare_queries(0)]
-        turn_keys(0)
-        q_mx.append(prepare_queries(1))
-        turn_keys(1, tag="q_raw0")
+        q_mx = []
+        for step in FIRST.split():
+            (prepare_gradient if step[0] == "g" else prepare_queries)(int(step[1:]))
+        kt_early = held("kt_early", [P, KT_EARLY * P, PACK], BF16)
+        for j in range(KT_EARLY):
+            turn_keys(kt_early, j, j)
+        kt_late = held("kt_late", [P, (PACK - KT_EARLY) * P, PACK], BF16, tag=KT_LATE_ON)
+        for j in range(KT_EARLY, PACK):
+            turn_keys(kt_late, j - KT_EARLY, j)
+        kt_mx = held("kt_codes", [P, FEATURES], U32, tag=KT_ON), held("kt_scales", [P, FEATURES], U8), E4M3
+        for first, width in KT_CALLS:
+            grouped, start = (kt_early, first) if first < KT_EARLY else (kt_late, first - KT_EARLY)
+            quantize(kt_mx, slice(first * P, (first + width) * P), grouped[:, start * P : (start + width) * P, :])
 
         gated = []
-        for h in range(QUERIES // Q_COLS):
-            gated.append(held("gated" + str(h), [P, SLOT_TILES, Q_COLS], F32, tag=GATED_ON[h]))
+
+        def make_scores(h):
+            relu = held("relu" + str(h), [P, SLOT_TILES, Q_COLS], F32, tag=GATED_ON[h])
+            twice = held("twice" + str(h), [P, SLOT_TILES, Q_COLS], F32, tag=TWICE_ON[h])
+            scaled = slice(VECTOR_WEIGHTS[h] * P, Q_COLS)
+            gated.append((relu, twice))
             for c in range(SLOT_TILES):
-                bank = ps_product.tile([P, Q_COLS], F32, name="product")
+                bank = next_bank("score")
                 product(bank, k_mx, c * P, q_mx[h])
-                relu = held("relu" + str(h) + str(c), [P, Q_COLS], F32)
-                nc.scalar.activation(out=relu[:], in_=bank[:], func=RELU, scale=ts_col[:, c : c + 1])
-                nc.vector.tensor_scalar(
-                    out=gated[h][:, c, :], in0=relu[:], scalar1=ts_col[:, c : c + 1], scalar2=None, op0=MULT
-                )
+                nc.scalar.activation(out=relu[:, c, :], in_=bank, func=RELU, scale=ts_col[:, c : c + 1])
+                if scaled.start < Q_COLS:
+                    if TWICE_ENGINES[h] == VECTOR:
+                        nc.vector.tensor_scalar(
+                            out=twice[:, c, scaled],
+                            in0=relu[:, c, scaled],
+                            scalar1=ts_col[:, c : c + 1],
+                            scalar2=None,
+                            op0=MULT,
+                        )
+                    else:
+                        nc.gpsimd.tensor_scalar(
+                            out=twice[:, c, scaled],
+                            in0=relu[:, c, scaled],
+                            scalar1=ts_col[:, c : c + 1],
+                            scalar2=0.0,
+                            op0=MULT,
+                            op1=ADD,
+                        )
 
         weights = []
-        for chunk in range(CHUNKS):
-            h, first = divmod(chunk * P, Q_COLS)
-            bank = ps_turn.tile([P, SLOT_TILES, P], F32, name="turn")
-            for c in range(SLOT_TILES):
-                nc.tensor.transpose(bank[:, c, :], gated[h][:, c, first : first + P], ident[:])
-            if chunk % 2 == 0:
-                two_weights = held("weights" + str(chunk // 2), [P, 2, 2, P, 2], F32, tag=WEIGHTS_ON[chunk // 2])
-            weight = two_weights[:, chunk % 2]
-            nc.scalar.activation(
-                out=weight,
-                in_=bank[:].rearrange("r c p -> r (c p)").rearrange("r (m u z) -> r u m z", u=2, z=2),
-                func=COPY,
-                scale=rw2[:, chunk : chunk + 1],
-            )
-            weights.append(weight)
 
-        ds_tiles, ds_mx = [], []
+        def make_weights(chunk):
+            h, first = divmod(chunk * P, Q_COLS)
+            source = gated[h][0 if chunk % 4 < VECTOR_WEIGHTS[h] else 1]
+            bank = next_bank("turn").rearrange("p (c x) -> p c x", x=P)
+            for c in range(SLOT_TILES):
+                nc.tensor.transpose(bank[:, c, :], source[:, c, first : first + P], ident[:])
+            weight = held("weights" + str(chunk), [P, SLOTS], F32, tag=WEIGHTS_ON[chunk])[:]
+            turned = bank.rearrange("r c p -> r (c p)")
+            if chunk % 4 < VECTOR_WEIGHTS[h]:
+                nc.vector.scalar_tensor_tensor(
+                    out=weight, in0=turned, scalar=rw2[:, chunk : chunk + 1], in1=ts_row[:], op0=MULT, op1=MULT
+                )
+            else:
+                nc.scalar.activation(out=weight, in_=turned, func=COPY, scale=rw2[:, chunk : chunk + 1])
+            weights.append(weight.rearrange("r (u m z) -> r u m z", u=2, z=2))
+
+        ds_tiles, ds_mx, turned = [], [], []
 
         def make_ds(chunk):
-            h, first = divmod(chunk * P, DO_COLS)
-            bank = ps_product.tile([P, SLOTS], F32, name="product")
-            product(bank, do_mx[h], first, v_mx)
-            ds = ring.tile([P, 2, P, 2], BF16, name="ds")
+            bank = next_bank("dp")
+            product(bank, do_mx[chunk][0], do_mx[chunk][1], v_mx)
+            ds = held("ds" + str(chunk), [P, 2, P, 2], BF16)
             nc.vector.tensor_tensor(
-                out=ds[:], in0=bank[:].rearrange("r (m u z) -> r u m z", u=2, z=2), in1=weights[chunk], op=MULT
+                out=ds[:], in0=bank.rearrange("r (m u z) -> r u m z", u=2, z=2), in1=weights[chunk], op=MULT
             )
             ds_tiles.append(ds)
 
-        def turn_ds(chunk):
-            words = ds_tiles[chunk][:].rearrange("r u m z -> r (u m z)").bitcast(F32)
-            bank = ps_turn.tile([P, 2, P], F32, name="turn")
-            for u in range(2):
-                nc.tensor.transpose(bank[:, u, :], words[:, u * P : (u + 1) * P], ident[:])
-            grouped = held("ds_grouped" + str(chunk), [P, P, PACK], BF16)
-            nc.scalar.copy(out=grouped[:].bitcast(F32), in_=bank[:].rearrange("m u r -> m r u"))
-            ds_mx.append(quantized("ds" + str(chunk), grouped[:], P, E5M2))
+        def turn_ds(unit):
+            bank = next_bank("ds")[:, : len(unit) * 2 * P].rearrange("m (c u r) -> m c u r", u=2, r=P)
+            for c, chunk in enumerate(unit):
+                words = ds_tiles[chunk][:].rearrange("r u m z -> r (u m z)").bitcast(F32)
+                for u in range(2):
+                    nc.tensor.transpose(bank[:, c, u, :], words[:, u * P : (u + 1) * P], ident[:])
+            name = "ds_turned" + str(unit[0])
+            grouped = held(name + "_grouped", [P, len(unit) * P, PACK], BF16)
+            nc.scalar.copy(
+                out=grouped[:].bitcast(F32).rearrange("m (c r) u -> m c r u", r=P),
+                in_=bank.rearrange("m c u r -> m c r u"),
+            )
+            turned.append((name, grouped))
+
+        def quantize_ds(u):
+            name, grouped = turned[u]
+            operand = quantized(name, grouped[:], len(UNITS[u]) * P, E5M2)
+            ds_mx.extend((operand, c * P) for c in range(len(UNITS[u])))
 
         def finish(chunk):
-            bank = ps_result.tile([P, FEATURES], F32, name="result_bank")
-            product(bank, ds_mx[chunk], 0, kt_mx)
+            bank = next_bank("result")
+            product(bank, ds_mx[chunk][0], ds_mx[chunk][1], kt_mx)
             result = held("result" + str(chunk), [P, P, PACK], F32)
             pieces = 2 if chunk >= CHUNKS - HALVED_CHUNKS else 1
             for piece in range(pieces):
                 span = slice(piece * P // pieces, (piece + 1) * P // pieces)
-                ordered = bank[:].rearrange("r (j p) -> r p j", j=PACK)[:, span, :]
+                ordered = bank.rearrange("r (j p) -> r p j", j=PACK)[:, span, :]
                 copy_on(RESULT_ENGINES[chunk], result[:, span, :], ordered)
                 nc.sync.dma_start(
                     out=out[0, chunk * P : (chunk + 1) * P, span.start * PACK : span.stop * PACK],
                     in_=result[:, span, :].rearrange("r p j -> r (p j)"),
                 )
 
-        for step in range(CHUNKS + OUT_LAG):
-            for stage, lag in ((make_ds, 0), (turn_ds, TURN_LAG), (finish, OUT_LAG)):
-                if 0 <= step - lag < CHUNKS:
-                    stage(step - lag)
+        stages = {"g": prepare_gradient, "d": make_ds, "t": lambda u: turn_ds(UNITS[u]), "q": quantize_ds, "f": finish, "a": prepare_queries, "s": make_scores, "w": make_weights}
+        for step in ORDER.split():
+            stages[step[0]](int(step[1:]))

@@ -22,22 +22,22 @@ LINE = 4
 SLOTS, TOKENS, FEATURES, QUERIES = 512, 2048, 512, 1024
 CHUNKS = QUERIES // P
 Q_COLS = 512
-DO_COLS = 512
+DO_LOADS = (256, 256, 512)
 SLOT_TILES = SLOTS // P
 UNITS = ((0,), (1,), (2,), (3,), (4,), (5,), (6,), (7,))
-HALVED_CHUNKS = 0
+HALVED_CHUNKS = 1
 
 VECTOR, SCALAR, GPSIMD = "vector", "scalar", "gpsimd"
 Q_ENGINES = ((SCALAR, VECTOR), (VECTOR, VECTOR))
-DO_PIECES = ((128, SCALAR, None), (128, SCALAR, None), (256, VECTOR, "do_grouped0"), (256, SCALAR, None), (256, SCALAR, None))
-RESULT_ENGINES = (SCALAR, SCALAR, SCALAR, SCALAR, VECTOR, SCALAR, VECTOR, SCALAR)
+DO_PIECES = ((128, SCALAR, None), (128, SCALAR, None), (256, SCALAR, None), (256, VECTOR, None), (256, SCALAR, None))
+RESULT_ENGINES = (SCALAR, SCALAR, SCALAR, SCALAR, SCALAR, SCALAR, SCALAR, VECTOR)
 
 GATED_ON = ("k_pool0", "k_pool1")
-WEIGHTS_ON = ("k_pool2", "k_pool3", None, None, None, None, None, None)
+WEIGHTS_ON = (None, None, None, None, None, None, None, "do_grouped1")
 
 KT_EARLY = 2
 KT_CALLS = ((0, 2), (2, 2))
-KT_ON = "v_pool1"
+KT_ON = "do_grouped0"
 LAGS = (1, 2)
 
 VECTOR_WEIGHTS = (0, 0)
@@ -47,13 +47,18 @@ SECOND_GRADIENT_STEP = 2
 BANK, BANKS = 512, 8
 BANKS_OF = {"score": (0, 1, 2), "turn": (3, 4, 5, 6, 7), "dp": (0, 1, 2), "ds": (3, 4), "result": (5, 6, 7)}
 WEAVE_SPLIT = {"k": 192, "v": 192}
-TWICE_ON = ("q_grouped1", None)
+TWICE_ON = (None, None)
 KT_LATE_ON = "q_raw0"
 EARLY_PIECES = 3
-ORDER = "s0 s1 w0 w1 w2 w3 w4 w5 w6 w7 d0 t0 d1 t1 d2 g3 q0 t2 d3 f0 q1 t3 d4 f1 g4 q2 t4 d5 f2 q3 t5 d6 f3 q4 t6 d7 f4 q5 t7 f5 q6 f6 q7 f7"
-LOADS = "k k k k q q v v v v o o"
+ORDER = "s0 s1 w0 w1 w2 w3 w4 w5 w6 w7 g3 g4 d0 t0 d1 q0 t1 d2 q1 t2 d3 f0 q2 t3 d4 f1 q3 t4 d5 f2 q4 t5 d6 f3 q5 t6 d7 f4 q6 t7 f5 q7 f6 f7"
+LOADS = "k l k k k q q v v v v o o o"
 FIRST = "g0 g1 g2 a0 a1"
-TWICE_ENGINES = (VECTOR, VECTOR)
+TWICE_ENGINES = (GPSIMD, GPSIMD)
+DO_CODES_ON = {}
+TURNED_ON = {}
+DS_ON = {}
+Q_SPLIT = (160, 256)
+TURN_ENGINES = (SCALAR, SCALAR, SCALAR, SCALAR, SCALAR, SCALAR, VECTOR, VECTOR)
 FLOPS = 3 * 2 * QUERIES * SLOTS * FEATURES
 
 
@@ -89,15 +94,8 @@ def tile_attend_gat_q_ts_kernel(tc, qT, kT, vT, doT, rw, ts, offs, out):
                 planes.rearrange("p j (run x) -> p run j x", x=LINE),
             )
 
-        def interleave_dealt(engine, grouped, planes, span):
-            copy_on(
-                engine,
-                grouped.rearrange("p (u m z) j -> p m j u z", u=2, z=2)[:, span],
-                planes.rearrange("p j (m u z) -> p m j u z", u=2, z=2)[:, span],
-            )
-
-        def mx_tiles(name, width, fmt):
-            return held(name + "_codes", [P, width], U32), held(name + "_scales", [P, width], U8), fmt
+        def mx_tiles(name, width, fmt, tag=None):
+            return held(name + "_codes", [P, width], U32, tag=tag), held(name + "_scales", [P, width], U8), fmt
 
         def quantize(operand, cols, grouped):
             codes, scales, fmt = operand
@@ -105,8 +103,8 @@ def tile_attend_gat_q_ts_kernel(tc, qT, kT, vT, doT, rw, ts, offs, out):
                 out=codes[:, cols].bitcast(fmt), scales=scales[:, cols], in_=grouped.rearrange("p col j -> p (col j)")
             )
 
-        def quantized(name, grouped, width, fmt):
-            operand = mx_tiles(name, width, fmt)
+        def quantized(name, grouped, width, fmt, tag=None):
+            operand = mx_tiles(name, width, fmt, tag)
             quantize(operand, slice(0, width), grouped)
             return operand
 
@@ -136,106 +134,80 @@ def tile_attend_gat_q_ts_kernel(tc, qT, kT, vT, doT, rw, ts, offs, out):
             nc.sync.dma_start(out=plane[:], in_=src.rearrange("(p j) token -> p j token", j=PACK)[:, j, :])
             return plane
 
-        def load_part(name, src, width, h):
+        def load_part(name, src, first, width, h):
             part = held(name + str(h), [P, PACK, width], F32)
             rows = src[0].rearrange("(p j) r -> p j r", j=PACK)
-            nc.sync.dma_start(out=part[:], in_=rows[:, :, h * width : (h + 1) * width])
+            nc.sync.dma_start(out=part[:], in_=rows[:, :, first : first + width])
             return part
 
-        nc.sync.dma_start(offsets[:], offs)
         k_pool, v_pool, q_raw, do_raw = [], [], [], []
         for load in LOADS.split():
-            if load == "k":
+            if load == "l":
+                nc.sync.dma_start(offsets[:], offs)
+            elif load == "k":
                 k_pool.append(load_plane("k_pool", kT, len(k_pool)))
             elif load == "v":
                 v_pool.append(load_plane("v_pool", vT, len(v_pool)))
             elif load == "q":
-                q_raw.append(load_part("q_raw", qT, Q_COLS, len(q_raw)))
+                q_raw.append(load_part("q_raw", qT, Q_COLS * len(q_raw), Q_COLS, len(q_raw)))
             else:
-                do_raw.append(load_part("do_raw", doT, DO_COLS, len(do_raw)))
+                do_raw.append(load_part("do_raw", doT, sum(DO_LOADS[: len(do_raw)]), DO_LOADS[len(do_raw)], len(do_raw)))
 
         ident = held("ident", [P, P], F32)
         make_identity(nc, ident[:])
 
         ts_listed = held("ts_listed", [P, SLOTS], F32)
         nc.vector.tensor_copy(out=ts_listed[:], in_=ts_pool[:].indirect(offsets[:]))
-        ts_dealt = held("ts_dealt", [P, SLOTS], F32)
-        nc.scalar.copy(
-            out=ts_dealt[:].rearrange("p (u m z) -> p u m z", u=2, z=2),
-            in_=ts_listed[:].rearrange("p (m u z) -> p u m z", u=2, z=2),
-        )
         bank = next_bank("turn").rearrange("p (c x) -> p c x", x=P)
         for c in range(SLOT_TILES):
-            nc.tensor.transpose(bank[:, c, :], ts_dealt[:, c * P : (c + 1) * P], ident[:])
+            nc.tensor.transpose(bank[:, c, :], ts_listed[:, c * P : (c + 1) * P], ident[:])
         ts_col = held("ts_col", [P, SLOT_TILES], F32)
         nc.scalar.copy(out=ts_col[:], in_=bank[:, :, P - 1])
-        bank = next_bank("turn").rearrange("p (c x) -> p c x", x=P)
-        for c in range(SLOT_TILES):
-            nc.tensor.transpose(bank[:, c, :], ts_col[:, c : c + 1].to_broadcast([P, P]), ident[:])
-        ts_row = held("ts_row", [P, SLOTS], F32)
-        nc.scalar.copy(out=ts_row[:], in_=bank.rearrange("r c p -> r (c p)"))
         bank = next_bank("turn").rearrange("p (c x) -> p c x", x=P)
         nc.tensor.transpose(bank[:, 0, :], rw_rows[:], ident[:])
         rw2 = held("rw2", [P, CHUNKS], F32)
         nc.scalar.mul(rw2[:], bank[:, 0, P - CHUNKS : P], 2.0)
 
-        def gather_pool(name, pool, split, dealt, tag=None):
-            listed = held(name + "_listed", [P, PACK, SLOTS], F32, tag=tag)
+        def gather_pool(name, pool):
             grouped = held(name + "_grouped", [P, SLOTS, PACK], BF16)
-            for j in range(PACK - 1):
-                nc.vector.tensor_copy(out=listed[:, j, :], in_=pool[j][:].indirect(offsets[:]))
-            halves = [slice(0, split), slice(split, SLOTS)]
-            for cols in halves:
-                entries = offsets[:, cols.start // LIST_ROWS : cols.stop // LIST_ROWS]
-                nc.vector.tensor_copy(out=listed[:, PACK - 1, cols], in_=pool[PACK - 1][:].indirect(entries))
-            for engine, cols in zip(POOL_ENGINES[name], (slice(0, WEAVE_SPLIT[name]), slice(WEAVE_SPLIT[name], SLOTS))):
-                if dealt:
-                    interleave_dealt(engine, grouped[:], listed[:], slice(cols.start // PACK, cols.stop // PACK))
-                else:
-                    interleave(engine, grouped[:, cols, :], listed[:, :, cols])
-            return listed, quantized(name, grouped[:], SLOTS, E4M3)
+            for j in range(PACK):
+                nc.vector.tensor_copy(out=grouped[:, :, j], in_=pool[j][:].indirect(offsets[:]))
+            return grouped, quantized(name, grouped[:], SLOTS, E4M3)
 
-        k_listed, k_mx = gather_pool("k", k_pool, POOL_SPLIT, True)
-
-        v_mx = gather_pool("v", v_pool, POOL_SPLIT, False, tag="ts_pool")[1]
+        k_grouped, k_mx = gather_pool("k", k_pool)
+        v_mx = gather_pool("v", v_pool)[1]
 
         do_mx = []
 
         def prepare_gradient(piece):
             width, engine, tag = DO_PIECES[piece]
-            h, first = divmod(len(do_mx) * P, DO_COLS)
+            h = max(n for n in range(len(DO_LOADS)) if sum(DO_LOADS[:n]) <= len(do_mx) * P)
+            first = len(do_mx) * P - sum(DO_LOADS[:h])
             grouped = held("do_grouped" + str(piece), [P, width, PACK], BF16, tag=tag)
             interleave(engine, grouped[:], do_raw[h][:, :, first : first + width])
-            operand = quantized("do" + str(piece), grouped[:], width, E5M2)
+            operand = quantized("do" + str(piece), grouped[:], width, E5M2, DO_CODES_ON.get(piece))
             do_mx.extend((operand, col) for col in range(0, width, P))
 
 
         def prepare_queries(h):
             grouped = held("q_grouped" + str(h), [P, Q_COLS, PACK], BF16)
-            for half in range(2):
-                cols = slice(half * Q_COLS // 2, (half + 1) * Q_COLS // 2)
+            for half, cols in enumerate((slice(0, Q_SPLIT[h]), slice(Q_SPLIT[h], Q_COLS))):
                 interleave(Q_ENGINES[h][half], grouped[:, cols, :], q_raw[h][:, :, cols])
             q_mx.append(quantized("q" + str(h), grouped[:], Q_COLS, E4M3))
-
-        def turn_keys(grouped, col, j):
-            bank = next_bank("turn").rearrange("p (c x) -> p c x", x=P)
-            for t in range(PACK):
-                nc.tensor.transpose(bank[:, t, :], k_listed[:, j, t:SLOTS:PACK], ident[:])
-            nc.scalar.copy(out=grouped[:, col * P : (col + 1) * P, :], in_=bank.rearrange("m t p -> m p t"))
 
         q_mx = []
         for step in FIRST.split():
             (prepare_gradient if step[0] == "g" else prepare_queries)(int(step[1:]))
-        kt_early = held("kt_early", [P, KT_EARLY * P, PACK], BF16)
-        for j in range(KT_EARLY):
-            turn_keys(kt_early, j, j)
-        kt_late = held("kt_late", [P, (PACK - KT_EARLY) * P, PACK], BF16, tag=KT_LATE_ON)
-        for j in range(KT_EARLY, PACK):
-            turn_keys(kt_late, j - KT_EARLY, j)
+        k_words = k_grouped[:].rearrange("p slot j -> p (slot j)").bitcast(F32).rearrange("p (m t u) -> p t u m", t=PACK, u=2)
+        kt_grouped = held("kt_grouped", [P, 2, 2 * P, PACK], BF16, tag=KT_LATE_ON)
+        for u in range(2):
+            bank = next_bank("turn")
+            for t in range(PACK):
+                nc.tensor.transpose(bank[:, t * P : (t + 1) * P], k_words[:, t, u, :], ident[:])
+            nc.scalar.copy(out=kt_grouped[:, u], in_=bank.bitcast(BF16).rearrange("m (t col) -> m col t", t=PACK))
         kt_mx = held("kt_codes", [P, FEATURES], U32, tag=KT_ON), held("kt_scales", [P, FEATURES], U8), E4M3
-        for first, width in KT_CALLS:
-            grouped, start = (kt_early, first) if first < KT_EARLY else (kt_late, first - KT_EARLY)
-            quantize(kt_mx, slice(first * P, (first + width) * P), grouped[:, start * P : (start + width) * P, :])
+        for u in range(2):
+            quantize(kt_mx, slice(u * 2 * P, (u + 1) * 2 * P), kt_grouped[:, u])
 
         gated = []
 
@@ -271,26 +243,24 @@ def tile_attend_gat_q_ts_kernel(tc, qT, kT, vT, doT, rw, ts, offs, out):
 
         def make_weights(chunk):
             h, first = divmod(chunk * P, Q_COLS)
-            source = gated[h][0 if chunk % 4 < VECTOR_WEIGHTS[h] else 1]
-            bank = next_bank("turn").rearrange("p (c x) -> p c x", x=P)
+            bank = next_bank("turn")
             for c in range(SLOT_TILES):
-                nc.tensor.transpose(bank[:, c, :], source[:, c, first : first + P], ident[:])
-            weight = held("weights" + str(chunk), [P, SLOTS], F32, tag=WEIGHTS_ON[chunk])[:]
-            turned = bank.rearrange("r c p -> r (c p)")
-            if chunk % 4 < VECTOR_WEIGHTS[h]:
-                nc.vector.scalar_tensor_tensor(
-                    out=weight, in0=turned, scalar=rw2[:, chunk : chunk + 1], in1=ts_row[:], op0=MULT, op1=MULT
-                )
-            else:
-                nc.scalar.activation(out=weight, in_=turned, func=COPY, scale=rw2[:, chunk : chunk + 1])
-            weights.append(weight.rearrange("r (u m z) -> r u m z", u=2, z=2))
+                nc.tensor.transpose(bank[:, c * P : (c + 1) * P], gated[h][1][:, c, first : first + P], ident[:])
+            weight = held("weights" + str(chunk), [P, 2, P, 2], F32, tag=WEIGHTS_ON[chunk])
+            nc.scalar.activation(
+                out=weight[:],
+                in_=bank.rearrange("r (m u z) -> r u m z", u=2, z=2),
+                func=COPY,
+                scale=rw2[:, chunk : chunk + 1],
+            )
+            weights.append(weight[:])
 
         ds_tiles, ds_mx, turned = [], [], []
 
         def make_ds(chunk):
             bank = next_bank("dp")
             product(bank, do_mx[chunk][0], do_mx[chunk][1], v_mx)
-            ds = held("ds" + str(chunk), [P, 2, P, 2], BF16)
+            ds = held("ds" + str(chunk), [P, 2, P, 2], BF16, tag=DS_ON.get(chunk))
             nc.vector.tensor_tensor(
                 out=ds[:], in0=bank.rearrange("r (m u z) -> r u m z", u=2, z=2), in1=weights[chunk], op=MULT
             )
@@ -303,10 +273,11 @@ def tile_attend_gat_q_ts_kernel(tc, qT, kT, vT, doT, rw, ts, offs, out):
                 for u in range(2):
                     nc.tensor.transpose(bank[:, c, u, :], words[:, u * P : (u + 1) * P], ident[:])
             name = "ds_turned" + str(unit[0])
-            grouped = held(name + "_grouped", [P, len(unit) * P, PACK], BF16)
-            nc.scalar.copy(
-                out=grouped[:].bitcast(F32).rearrange("m (c r) u -> m c r u", r=P),
-                in_=bank.rearrange("m c u r -> m c r u"),
+            grouped = held(name + "_grouped", [P, len(unit) * P, PACK], BF16, tag=TURNED_ON.get(unit[0]))
+            copy_on(
+                TURN_ENGINES[unit[0]],
+                grouped[:].bitcast(F32).rearrange("m (c r) u -> m c r u", r=P),
+                bank.rearrange("m c u r -> m c r u"),
             )
             turned.append((name, grouped))
 
@@ -318,15 +289,15 @@ def tile_attend_gat_q_ts_kernel(tc, qT, kT, vT, doT, rw, ts, offs, out):
         def finish(chunk):
             bank = next_bank("result")
             product(bank, ds_mx[chunk][0], ds_mx[chunk][1], kt_mx)
-            result = held("result" + str(chunk), [P, P, PACK], F32)
+            result = held("result" + str(chunk), [P, P, 2, 2], F32)
             pieces = 2 if chunk >= CHUNKS - HALVED_CHUNKS else 1
             for piece in range(pieces):
                 span = slice(piece * P // pieces, (piece + 1) * P // pieces)
-                ordered = bank.rearrange("r (j p) -> r p j", j=PACK)[:, span, :]
-                copy_on(RESULT_ENGINES[chunk], result[:, span, :], ordered)
+                ordered = bank.rearrange("r (u p z) -> r p u z", u=2, z=2)[:, span]
+                copy_on(RESULT_ENGINES[chunk], result[:, span], ordered)
                 nc.sync.dma_start(
                     out=out[0, chunk * P : (chunk + 1) * P, span.start * PACK : span.stop * PACK],
-                    in_=result[:, span, :].rearrange("r p j -> r (p j)"),
+                    in_=result[:, span].rearrange("r p u z -> r (p u z)"),
                 )
 
         stages = {"g": prepare_gradient, "d": make_ds, "t": lambda u: turn_ds(UNITS[u]), "q": quantize_ds, "f": finish, "a": prepare_queries, "s": make_scores, "w": make_weights}

@@ -22,7 +22,7 @@ LINE = 4
 SLOTS, TOKENS, FEATURES, QUERIES = 512, 2048, 512, 1024
 CHUNKS = QUERIES // P
 Q_COLS = 512
-DO_LOADS = (256, 256, 512)
+DO_LOADS = (256, 256, 256, 256)
 SLOT_TILES = SLOTS // P
 UNITS = ((0,), (1,), (2,), (3,), (4,), (5,), (6,), (7,))
 HALVED_CHUNKS = 1
@@ -33,7 +33,7 @@ DO_PIECES = ((128, SCALAR, None), (128, SCALAR, None), (256, SCALAR, None), (256
 RESULT_ENGINES = (SCALAR, SCALAR, SCALAR, SCALAR, SCALAR, SCALAR, SCALAR, VECTOR)
 
 GATED_ON = ("k_pool0", "k_pool1")
-WEIGHTS_ON = (None, None, None, None, None, None, None, "do_grouped1")
+WEIGHTS_ON = (None, None, None, None, None, None, "do_raw1", "do_grouped1")
 
 KT_EARLY = 2
 KT_CALLS = ((0, 2), (2, 2))
@@ -45,20 +45,22 @@ POOL_SPLIT = 256
 POOL_ENGINES = {"k": (SCALAR, VECTOR), "v": (SCALAR, VECTOR)}
 SECOND_GRADIENT_STEP = 2
 BANK, BANKS = 512, 8
-BANKS_OF = {"score": (0, 1, 2), "turn": (3, 4, 5, 6, 7), "dp": (0, 1, 2), "ds": (3, 4), "result": (5, 6, 7)}
+BANKS_OF = {"score": (0, 1, 2, 3), "turn": (4, 5, 6, 7), "weight": (0, 1, 2, 3, 4, 5, 6, 7), "dp": (0, 1, 2), "ds": (3, 4), "result": (5, 6, 7)}
 WEAVE_SPLIT = {"k": 192, "v": 192}
 TWICE_ON = (None, None)
-KT_LATE_ON = "q_raw0"
+KT_LATE_ON = ("q_raw0", "q_grouped0")
 EARLY_PIECES = 3
-ORDER = "s0 s1 w0 w1 w2 w3 w4 w5 w6 w7 g3 g4 d0 t0 d1 q0 t1 d2 q1 t2 d3 f0 q2 t3 d4 f1 q3 t4 d5 f2 q4 t5 d6 f3 q5 t6 d7 f4 q6 t7 f5 q7 f6 f7"
-LOADS = "k l k k k q q v v v v o o o"
-FIRST = "g0 g1 g2 a0 a1"
-TWICE_ENGINES = (GPSIMD, GPSIMD)
+ORDER = "s0 s1 w0 w1 w2 w3 w4 w5 w6 w7 d0 t0 d1 q0 t1 d2 q1 t2 d3 f0 q2 t3 d4 f1 q3 t4 d5 f2 q4 t5 d6 f3 q5 t6 d7 f4 q6 t7 f5 q7 f6 f7"
+LOADS = "k l k k k q q v v v v o o o o"
+FIRST = "g0 g1 g2 g3 g4 a0 a1"
+TWICE_ENGINES = (GPSIMD, GPSIMD, GPSIMD, GPSIMD, GPSIMD, GPSIMD, GPSIMD, GPSIMD)
 DO_CODES_ON = {}
 TURNED_ON = {}
 DS_ON = {}
 Q_SPLIT = (160, 256)
 TURN_ENGINES = (SCALAR, SCALAR, SCALAR, SCALAR, SCALAR, SCALAR, VECTOR, VECTOR)
+WEIGHT_ENGINES = (SCALAR, SCALAR, SCALAR, SCALAR, SCALAR, SCALAR, SCALAR, SCALAR)
+KT_ENGINES = (SCALAR, SCALAR)
 FLOPS = 3 * 2 * QUERIES * SLOTS * FEATURES
 
 
@@ -199,15 +201,15 @@ def tile_attend_gat_q_ts_kernel(tc, qT, kT, vT, doT, rw, ts, offs, out):
         for step in FIRST.split():
             (prepare_gradient if step[0] == "g" else prepare_queries)(int(step[1:]))
         k_words = k_grouped[:].rearrange("p slot j -> p (slot j)").bitcast(F32).rearrange("p (m t u) -> p t u m", t=PACK, u=2)
-        kt_grouped = held("kt_grouped", [P, 2, 2 * P, PACK], BF16, tag=KT_LATE_ON)
+        kt_grouped = [held("kt_grouped" + str(u), [P, 2 * P, PACK], BF16, tag=KT_LATE_ON[u]) for u in range(2)]
         for u in range(2):
             bank = next_bank("turn")
             for t in range(PACK):
                 nc.tensor.transpose(bank[:, t * P : (t + 1) * P], k_words[:, t, u, :], ident[:])
-            nc.scalar.copy(out=kt_grouped[:, u], in_=bank.bitcast(BF16).rearrange("m (t col) -> m col t", t=PACK))
+            copy_on(KT_ENGINES[u], kt_grouped[u][:], bank.bitcast(BF16).rearrange("m (t col) -> m col t", t=PACK))
         kt_mx = held("kt_codes", [P, FEATURES], U32, tag=KT_ON), held("kt_scales", [P, FEATURES], U8), E4M3
         for u in range(2):
-            quantize(kt_mx, slice(u * 2 * P, (u + 1) * 2 * P), kt_grouped[:, u])
+            quantize(kt_mx, slice(u * 2 * P, (u + 1) * 2 * P), kt_grouped[u][:])
 
         gated = []
 
@@ -221,7 +223,7 @@ def tile_attend_gat_q_ts_kernel(tc, qT, kT, vT, doT, rw, ts, offs, out):
                 product(bank, k_mx, c * P, q_mx[h])
                 nc.scalar.activation(out=relu[:, c, :], in_=bank, func=RELU, scale=ts_col[:, c : c + 1])
                 if scaled.start < Q_COLS:
-                    if TWICE_ENGINES[h] == VECTOR:
+                    if TWICE_ENGINES[h * SLOT_TILES + c] == VECTOR:
                         nc.vector.tensor_scalar(
                             out=twice[:, c, scaled],
                             in0=relu[:, c, scaled],
@@ -243,16 +245,17 @@ def tile_attend_gat_q_ts_kernel(tc, qT, kT, vT, doT, rw, ts, offs, out):
 
         def make_weights(chunk):
             h, first = divmod(chunk * P, Q_COLS)
-            bank = next_bank("turn")
+            bank = next_bank("weight")
             for c in range(SLOT_TILES):
                 nc.tensor.transpose(bank[:, c * P : (c + 1) * P], gated[h][1][:, c, first : first + P], ident[:])
             weight = held("weights" + str(chunk), [P, 2, P, 2], F32, tag=WEIGHTS_ON[chunk])
-            nc.scalar.activation(
-                out=weight[:],
-                in_=bank.rearrange("r (m u z) -> r u m z", u=2, z=2),
-                func=COPY,
-                scale=rw2[:, chunk : chunk + 1],
-            )
+            turned_scores = bank.rearrange("r (m u z) -> r u m z", u=2, z=2)
+            if WEIGHT_ENGINES[chunk] == VECTOR:
+                nc.vector.tensor_scalar(
+                    out=weight[:], in0=turned_scores, scalar1=rw2[:, chunk : chunk + 1], scalar2=None, op0=MULT
+                )
+            else:
+                nc.scalar.activation(out=weight[:], in_=turned_scores, func=COPY, scale=rw2[:, chunk : chunk + 1])
             weights.append(weight[:])
 
         ds_tiles, ds_mx, turned = [], [], []

@@ -19,48 +19,28 @@ P = 128
 PACK = 4
 LIST_ROWS = 16
 LINE = 4
+BANK, BANKS = 512, 8
 SLOTS, TOKENS, FEATURES, QUERIES = 512, 2048, 512, 1024
 CHUNKS = QUERIES // P
-Q_COLS = 512
-DO_LOADS = (256, 256, 256, 256)
 SLOT_TILES = SLOTS // P
-UNITS = ((0,), (1,), (2,), (3,), (4,), (5,), (6,), (7,))
-HALVED_CHUNKS = 1
+Q_COLS = 512
+DO_COLS = 256
 
-VECTOR, SCALAR, GPSIMD = "vector", "scalar", "gpsimd"
-Q_ENGINES = ((SCALAR, VECTOR), (VECTOR, VECTOR))
-DO_PIECES = ((128, SCALAR, None), (128, SCALAR, None), (256, SCALAR, None), (256, VECTOR, None), (256, SCALAR, None))
-RESULT_ENGINES = (SCALAR, SCALAR, SCALAR, SCALAR, SCALAR, SCALAR, SCALAR, VECTOR)
+VECTOR, SCALAR = "vector", "scalar"
+Q_ON_SCALAR = 160
+DO_ON_VECTOR = 2
+TURNS_ON_VECTOR = 2
+TURN_LAG, QUANTIZE_LAG, FINISH_LAG = 1, 2, 3
 
-GATED_ON = ("k_pool0", "k_pool1")
-WEIGHTS_ON = (None, None, None, None, None, None, "do_raw1", "do_grouped1")
+BANKS_OF = {
+    "score": (0, 1, 2, 3),
+    "turn": (4, 5, 6, 7),
+    "weight": (0, 1, 2, 3, 4, 5, 6, 7),
+    "dp": (0, 1, 2),
+    "ds": (3, 4),
+    "result": (5, 6, 7),
+}
 
-KT_EARLY = 2
-KT_CALLS = ((0, 2), (2, 2))
-KT_ON = "do_grouped0"
-LAGS = (1, 2)
-
-VECTOR_WEIGHTS = (0, 0)
-POOL_SPLIT = 256
-POOL_ENGINES = {"k": (SCALAR, VECTOR), "v": (SCALAR, VECTOR)}
-SECOND_GRADIENT_STEP = 2
-BANK, BANKS = 512, 8
-BANKS_OF = {"score": (0, 1, 2, 3), "turn": (4, 5, 6, 7), "weight": (0, 1, 2, 3, 4, 5, 6, 7), "dp": (0, 1, 2), "ds": (3, 4), "result": (5, 6, 7)}
-WEAVE_SPLIT = {"k": 192, "v": 192}
-TWICE_ON = (None, None)
-KT_LATE_ON = ("q_raw0", "q_grouped0")
-EARLY_PIECES = 3
-ORDER = "s0 s1 w0 w1 w2 w3 w4 w5 w6 w7 d0 t0 d1 q0 t1 d2 q1 t2 d3 f0 q2 t3 d4 f1 q3 t4 d5 f2 q4 t5 d6 f3 q5 t6 d7 f4 q6 t7 f5 q7 f6 f7"
-LOADS = "k l k k k q q v v v v o o o o"
-FIRST = "g0 g1 g2 g3 g4 a0 a1"
-TWICE_ENGINES = (GPSIMD, GPSIMD, GPSIMD, GPSIMD, GPSIMD, GPSIMD, GPSIMD, GPSIMD)
-DO_CODES_ON = {}
-TURNED_ON = {}
-DS_ON = {}
-Q_SPLIT = (160, 256)
-TURN_ENGINES = (SCALAR, SCALAR, SCALAR, SCALAR, SCALAR, SCALAR, VECTOR, VECTOR)
-WEIGHT_ENGINES = (SCALAR, SCALAR, SCALAR, SCALAR, SCALAR, SCALAR, SCALAR, SCALAR)
-KT_ENGINES = (SCALAR, SCALAR)
 FLOPS = 3 * 2 * QUERIES * SLOTS * FEATURES
 
 
@@ -71,21 +51,19 @@ def tile_attend_gat_q_ts_kernel(tc, qT, kT, vT, doT, rw, ts, offs, out):
         keep = ctx.enter_context(tc.tile_pool(name="keep", bufs=1))
         psum = ctx.enter_context(tc.psum_pool(name="psum", bufs=1))
         banks = [psum.tile([P, BANK], F32, name="bank" + str(b)) for b in range(BANKS)]
-        uses = {role: [] for role in BANKS_OF}
+        taken = {role: [] for role in BANKS_OF}
 
         def next_bank(role):
             numbers = BANKS_OF[role]
-            uses[role].append(numbers[len(uses[role]) % len(numbers)])
-            return banks[uses[role][-1]][:]
+            taken[role].append(numbers[len(taken[role]) % len(numbers)])
+            return banks[taken[role][-1]][:]
 
-        def held(name, shape, dtype, tag=None):
-            return keep.tile(shape, dtype, name=name, tag=tag or name, align_bytes=64)
+        def held(name, shape, dtype, on=None):
+            return keep.tile(shape, dtype, name=name, tag=on or name, align_bytes=64)
 
         def copy_on(engine, dst, src):
             if engine == VECTOR:
                 nc.vector.tensor_copy(out=dst, in_=src)
-            elif engine == GPSIMD:
-                nc.gpsimd.tensor_copy(out=dst, in_=src)
             else:
                 nc.scalar.copy(out=dst, in_=src)
 
@@ -96,8 +74,8 @@ def tile_attend_gat_q_ts_kernel(tc, qT, kT, vT, doT, rw, ts, offs, out):
                 planes.rearrange("p j (run x) -> p run j x", x=LINE),
             )
 
-        def mx_tiles(name, width, fmt, tag=None):
-            return held(name + "_codes", [P, width], U32, tag=tag), held(name + "_scales", [P, width], U8), fmt
+        def mx_tiles(name, width, fmt, on=None):
+            return held(name + "_codes", [P, width], U32, on), held(name + "_scales", [P, width], U8), fmt
 
         def quantize(operand, cols, grouped):
             codes, scales, fmt = operand
@@ -105,8 +83,8 @@ def tile_attend_gat_q_ts_kernel(tc, qT, kT, vT, doT, rw, ts, offs, out):
                 out=codes[:, cols].bitcast(fmt), scales=scales[:, cols], in_=grouped.rearrange("p col j -> p (col j)")
             )
 
-        def quantized(name, grouped, width, fmt, tag=None):
-            operand = mx_tiles(name, width, fmt, tag)
+        def quantized(name, grouped, width, fmt):
+            operand = mx_tiles(name, width, fmt)
             quantize(operand, slice(0, width), grouped)
             return operand
 
@@ -136,24 +114,18 @@ def tile_attend_gat_q_ts_kernel(tc, qT, kT, vT, doT, rw, ts, offs, out):
             nc.sync.dma_start(out=plane[:], in_=src.rearrange("(p j) token -> p j token", j=PACK)[:, j, :])
             return plane
 
-        def load_part(name, src, first, width, h):
+        def load_part(name, src, width, h):
             part = held(name + str(h), [P, PACK, width], F32)
             rows = src[0].rearrange("(p j) r -> p j r", j=PACK)
-            nc.sync.dma_start(out=part[:], in_=rows[:, :, first : first + width])
+            nc.sync.dma_start(out=part[:], in_=rows[:, :, h * width : (h + 1) * width])
             return part
 
-        k_pool, v_pool, q_raw, do_raw = [], [], [], []
-        for load in LOADS.split():
-            if load == "l":
-                nc.sync.dma_start(offsets[:], offs)
-            elif load == "k":
-                k_pool.append(load_plane("k_pool", kT, len(k_pool)))
-            elif load == "v":
-                v_pool.append(load_plane("v_pool", vT, len(v_pool)))
-            elif load == "q":
-                q_raw.append(load_part("q_raw", qT, Q_COLS * len(q_raw), Q_COLS, len(q_raw)))
-            else:
-                do_raw.append(load_part("do_raw", doT, sum(DO_LOADS[: len(do_raw)]), DO_LOADS[len(do_raw)], len(do_raw)))
+        k_pool = [load_plane("k_pool", kT, 0)]
+        nc.sync.dma_start(offsets[:], offs)
+        k_pool += [load_plane("k_pool", kT, j) for j in range(1, PACK)]
+        q_raw = [load_part("q_raw", qT, Q_COLS, h) for h in range(QUERIES // Q_COLS)]
+        v_pool = [load_plane("v_pool", vT, j) for j in range(PACK)]
+        do_raw = [load_part("do_raw", doT, DO_COLS, h) for h in range(QUERIES // DO_COLS)]
 
         ident = held("ident", [P, P], F32)
         make_identity(nc, ident[:])
@@ -165,10 +137,11 @@ def tile_attend_gat_q_ts_kernel(tc, qT, kT, vT, doT, rw, ts, offs, out):
             nc.tensor.transpose(bank[:, c, :], ts_listed[:, c * P : (c + 1) * P], ident[:])
         ts_col = held("ts_col", [P, SLOT_TILES], F32)
         nc.scalar.copy(out=ts_col[:], in_=bank[:, :, P - 1])
-        bank = next_bank("turn").rearrange("p (c x) -> p c x", x=P)
-        nc.tensor.transpose(bank[:, 0, :], rw_rows[:], ident[:])
+        bank = next_bank("turn")
+        nc.tensor.transpose(bank[:, :P], rw_rows[:], ident[:])
         rw2 = held("rw2", [P, CHUNKS], F32)
-        nc.scalar.mul(rw2[:], bank[:, 0, P - CHUNKS : P], 2.0)
+        nc.scalar.mul(rw2[:], bank[:, P - CHUNKS : P], 2.0)
+
 
         def gather_pool(name, pool):
             grouped = held(name + "_grouped", [P, SLOTS, PACK], BF16)
@@ -179,130 +152,112 @@ def tile_attend_gat_q_ts_kernel(tc, qT, kT, vT, doT, rw, ts, offs, out):
         k_grouped, k_mx = gather_pool("k", k_pool)
         v_mx = gather_pool("v", v_pool)[1]
 
-        do_mx = []
-
-        def prepare_gradient(piece):
-            width, engine, tag = DO_PIECES[piece]
-            h = max(n for n in range(len(DO_LOADS)) if sum(DO_LOADS[:n]) <= len(do_mx) * P)
-            first = len(do_mx) * P - sum(DO_LOADS[:h])
-            grouped = held("do_grouped" + str(piece), [P, width, PACK], BF16, tag=tag)
-            interleave(engine, grouped[:], do_raw[h][:, :, first : first + width])
-            operand = quantized("do" + str(piece), grouped[:], width, E5M2, DO_CODES_ON.get(piece))
-            do_mx.extend((operand, col) for col in range(0, width, P))
-
-
-        def prepare_queries(h):
-            grouped = held("q_grouped" + str(h), [P, Q_COLS, PACK], BF16)
-            for half, cols in enumerate((slice(0, Q_SPLIT[h]), slice(Q_SPLIT[h], Q_COLS))):
-                interleave(Q_ENGINES[h][half], grouped[:, cols, :], q_raw[h][:, :, cols])
-            q_mx.append(quantized("q" + str(h), grouped[:], Q_COLS, E4M3))
+        do_mx, do_pieces = [], []
+        for h, part in enumerate(do_raw):
+            width = P if h == 0 else DO_COLS
+            for first in range(0, DO_COLS, width):
+                do_pieces.append("do_grouped" + str(len(do_pieces)))
+                grouped = held(do_pieces[-1], [P, width, PACK], BF16)
+                interleave(VECTOR if h == DO_ON_VECTOR else SCALAR, grouped[:], part[:, :, first : first + width])
+                operand = quantized(do_pieces[-1], grouped[:], width, E5M2)
+                do_mx.extend((operand, col) for col in range(0, width, P))
 
         q_mx = []
-        for step in FIRST.split():
-            (prepare_gradient if step[0] == "g" else prepare_queries)(int(step[1:]))
-        k_words = k_grouped[:].rearrange("p slot j -> p (slot j)").bitcast(F32).rearrange("p (m t u) -> p t u m", t=PACK, u=2)
-        kt_grouped = [held("kt_grouped" + str(u), [P, 2 * P, PACK], BF16, tag=KT_LATE_ON[u]) for u in range(2)]
+        for h, part in enumerate(q_raw):
+            grouped = held("q_grouped" + str(h), [P, Q_COLS, PACK], BF16)
+            split = Q_ON_SCALAR if h == 0 else Q_COLS // 2
+            interleave(SCALAR if h == 0 else VECTOR, grouped[:, :split, :], part[:, :, :split])
+            interleave(VECTOR, grouped[:, split:, :], part[:, :, split:])
+            q_mx.append(quantized("q" + str(h), grouped[:], Q_COLS, E4M3))
+
+        k_words = k_grouped[:].rearrange("p slot j -> p (slot j)").bitcast(F32)
+        k_words = k_words.rearrange("p (m t u) -> p t u m", t=PACK, u=2)
+        kt_grouped = [
+            held("kt_grouped" + str(u), [P, 2 * P, PACK], BF16, on) for u, on in enumerate(("q_raw0", "q_grouped0"))
+        ]
         for u in range(2):
             bank = next_bank("turn")
             for t in range(PACK):
                 nc.tensor.transpose(bank[:, t * P : (t + 1) * P], k_words[:, t, u, :], ident[:])
-            copy_on(KT_ENGINES[u], kt_grouped[u][:], bank.bitcast(BF16).rearrange("m (t col) -> m col t", t=PACK))
-        kt_mx = held("kt_codes", [P, FEATURES], U32, tag=KT_ON), held("kt_scales", [P, FEATURES], U8), E4M3
+            nc.scalar.copy(out=kt_grouped[u][:], in_=bank.bitcast(BF16).rearrange("m (t col) -> m col t", t=PACK))
+        kt_mx = mx_tiles("kt", FEATURES, E4M3, do_pieces[0])
         for u in range(2):
             quantize(kt_mx, slice(u * 2 * P, (u + 1) * 2 * P), kt_grouped[u][:])
 
         gated = []
-
-        def make_scores(h):
-            relu = held("relu" + str(h), [P, SLOT_TILES, Q_COLS], F32, tag=GATED_ON[h])
-            twice = held("twice" + str(h), [P, SLOT_TILES, Q_COLS], F32, tag=TWICE_ON[h])
-            scaled = slice(VECTOR_WEIGHTS[h] * P, Q_COLS)
-            gated.append((relu, twice))
+        for h in range(QUERIES // Q_COLS):
+            relu = held("relu" + str(h), [P, SLOT_TILES, Q_COLS], F32, "k_pool" + str(h))
+            gated.append(held("gated" + str(h), [P, SLOT_TILES, Q_COLS], F32))
             for c in range(SLOT_TILES):
                 bank = next_bank("score")
                 product(bank, k_mx, c * P, q_mx[h])
                 nc.scalar.activation(out=relu[:, c, :], in_=bank, func=RELU, scale=ts_col[:, c : c + 1])
-                if scaled.start < Q_COLS:
-                    if TWICE_ENGINES[h * SLOT_TILES + c] == VECTOR:
-                        nc.vector.tensor_scalar(
-                            out=twice[:, c, scaled],
-                            in0=relu[:, c, scaled],
-                            scalar1=ts_col[:, c : c + 1],
-                            scalar2=None,
-                            op0=MULT,
-                        )
-                    else:
-                        nc.gpsimd.tensor_scalar(
-                            out=twice[:, c, scaled],
-                            in0=relu[:, c, scaled],
-                            scalar1=ts_col[:, c : c + 1],
-                            scalar2=0.0,
-                            op0=MULT,
-                            op1=ADD,
-                        )
+                nc.gpsimd.tensor_scalar(
+                    out=gated[h][:, c, :],
+                    in0=relu[:, c, :],
+                    scalar1=ts_col[:, c : c + 1],
+                    scalar2=0.0,
+                    op0=MULT,
+                    op1=ADD,
+                )
 
+        late_on = ["do_raw1", do_pieces[1]]
+        weights_on = [None] * (CHUNKS - len(late_on)) + late_on
         weights = []
-
-        def make_weights(chunk):
+        for chunk in range(CHUNKS):
             h, first = divmod(chunk * P, Q_COLS)
             bank = next_bank("weight")
             for c in range(SLOT_TILES):
-                nc.tensor.transpose(bank[:, c * P : (c + 1) * P], gated[h][1][:, c, first : first + P], ident[:])
-            weight = held("weights" + str(chunk), [P, 2, P, 2], F32, tag=WEIGHTS_ON[chunk])
-            turned_scores = bank.rearrange("r (m u z) -> r u m z", u=2, z=2)
-            if WEIGHT_ENGINES[chunk] == VECTOR:
-                nc.vector.tensor_scalar(
-                    out=weight[:], in0=turned_scores, scalar1=rw2[:, chunk : chunk + 1], scalar2=None, op0=MULT
-                )
-            else:
-                nc.scalar.activation(out=weight[:], in_=turned_scores, func=COPY, scale=rw2[:, chunk : chunk + 1])
-            weights.append(weight[:])
+                nc.tensor.transpose(bank[:, c * P : (c + 1) * P], gated[h][:, c, first : first + P], ident[:])
+            weights.append(held("weights" + str(chunk), [P, 2, P, 2], F32, weights_on[chunk]))
+            nc.scalar.activation(
+                out=weights[chunk][:],
+                in_=bank.rearrange("r (m u z) -> r u m z", u=2, z=2),
+                func=COPY,
+                scale=rw2[:, chunk : chunk + 1],
+            )
 
-        ds_tiles, ds_mx, turned = [], [], []
+        ds_tiles, ds_grouped, ds_mx = [], [], []
 
         def make_ds(chunk):
             bank = next_bank("dp")
-            product(bank, do_mx[chunk][0], do_mx[chunk][1], v_mx)
-            ds = held("ds" + str(chunk), [P, 2, P, 2], BF16, tag=DS_ON.get(chunk))
+            product(bank, *do_mx[chunk], v_mx)
+            ds_tiles.append(held("ds" + str(chunk), [P, 2, P, 2], BF16))
             nc.vector.tensor_tensor(
-                out=ds[:], in0=bank.rearrange("r (m u z) -> r u m z", u=2, z=2), in1=weights[chunk], op=MULT
+                out=ds_tiles[chunk][:],
+                in0=bank.rearrange("r (m u z) -> r u m z", u=2, z=2),
+                in1=weights[chunk][:],
+                op=MULT,
             )
-            ds_tiles.append(ds)
 
-        def turn_ds(unit):
-            bank = next_bank("ds")[:, : len(unit) * 2 * P].rearrange("m (c u r) -> m c u r", u=2, r=P)
-            for c, chunk in enumerate(unit):
-                words = ds_tiles[chunk][:].rearrange("r u m z -> r (u m z)").bitcast(F32)
-                for u in range(2):
-                    nc.tensor.transpose(bank[:, c, u, :], words[:, u * P : (u + 1) * P], ident[:])
-            name = "ds_turned" + str(unit[0])
-            grouped = held(name + "_grouped", [P, len(unit) * P, PACK], BF16, tag=TURNED_ON.get(unit[0]))
-            copy_on(
-                TURN_ENGINES[unit[0]],
-                grouped[:].bitcast(F32).rearrange("m (c r) u -> m c r u", r=P),
-                bank.rearrange("m c u r -> m c r u"),
-            )
-            turned.append((name, grouped))
+        def turn_ds(chunk):
+            bank = next_bank("ds")[:, : 2 * P].rearrange("m (u r) -> m u r", u=2)
+            words = ds_tiles[chunk][:].rearrange("r u m z -> r (u m z)").bitcast(F32)
+            for u in range(2):
+                nc.tensor.transpose(bank[:, u, :], words[:, u * P : (u + 1) * P], ident[:])
+            ds_grouped.append(held("ds_grouped" + str(chunk), [P, P, PACK], BF16))
+            engine = VECTOR if chunk >= CHUNKS - TURNS_ON_VECTOR else SCALAR
+            copy_on(engine, ds_grouped[chunk][:].bitcast(F32), bank.rearrange("m u r -> m r u"))
 
-        def quantize_ds(u):
-            name, grouped = turned[u]
-            operand = quantized(name, grouped[:], len(UNITS[u]) * P, E5M2)
-            ds_mx.extend((operand, c * P) for c in range(len(UNITS[u])))
+        def quantize_ds(chunk):
+            ds_mx.append(quantized("ds_mx" + str(chunk), ds_grouped[chunk][:], P, E5M2))
 
         def finish(chunk):
             bank = next_bank("result")
-            product(bank, ds_mx[chunk][0], ds_mx[chunk][1], kt_mx)
+            product(bank, ds_mx[chunk], 0, kt_mx)
             result = held("result" + str(chunk), [P, P, 2, 2], F32)
-            pieces = 2 if chunk >= CHUNKS - HALVED_CHUNKS else 1
+            last = chunk == CHUNKS - 1
+            pieces = 2 if last else 1
             for piece in range(pieces):
                 span = slice(piece * P // pieces, (piece + 1) * P // pieces)
                 ordered = bank.rearrange("r (u p z) -> r p u z", u=2, z=2)[:, span]
-                copy_on(RESULT_ENGINES[chunk], result[:, span], ordered)
+                copy_on(VECTOR if last else SCALAR, result[:, span], ordered)
                 nc.sync.dma_start(
                     out=out[0, chunk * P : (chunk + 1) * P, span.start * PACK : span.stop * PACK],
                     in_=result[:, span].rearrange("r p u z -> r (p u z)"),
                 )
 
-        stages = {"g": prepare_gradient, "d": make_ds, "t": lambda u: turn_ds(UNITS[u]), "q": quantize_ds, "f": finish, "a": prepare_queries, "s": make_scores, "w": make_weights}
-        for step in ORDER.split():
-            stages[step[0]](int(step[1:]))
+        for step in range(CHUNKS + FINISH_LAG):
+            for stage, lag in ((quantize_ds, QUANTIZE_LAG), (turn_ds, TURN_LAG), (make_ds, 0), (finish, FINISH_LAG)):
+                if 0 <= step - lag < CHUNKS:
+                    stage(step - lag)

@@ -120,9 +120,8 @@ def tile_attend_gat_q_ts_kernel(tc, qT, kT, vT, doT, rw, ts, offs, out):
             nc.sync.dma_start(out=part[:], in_=rows[:, :, h * width : (h + 1) * width])
             return part
 
-        k_pool = [load_plane("k_pool", kT, 0)]
         nc.sync.dma_start(offsets[:], offs)
-        k_pool += [load_plane("k_pool", kT, j) for j in range(1, PACK)]
+        k_pool = [load_plane("k_pool", kT, j) for j in range(PACK)]
         q_raw = [load_part("q_raw", qT, Q_COLS, h) for h in range(QUERIES // Q_COLS)]
         v_pool = [load_plane("v_pool", vT, j) for j in range(PACK)]
         do_raw = [load_part("do_raw", doT, DO_COLS, h) for h in range(QUERIES // DO_COLS)]

@@ -27,8 +27,14 @@ Q_COLS = 512
 DO_COLS = 256
 
 VECTOR, SCALAR = "vector", "scalar"
-Q_ON_SCALAR = 160
-DO_ON_VECTOR = 2
+TS_ON_VECTOR = 2
+LATE_WEIGHTS = 1
+Q_ON_SCALAR = (256, 256)
+DO_ON_VECTOR = (2,)
+DO_LEAD = 4
+DO_EARLY = 6
+DS_BEHIND = 2
+RESULTS_ON_VECTOR = (7,)
 TURNS_ON_VECTOR = 2
 TURN_LAG, QUANTIZE_LAG, FINISH_LAG = 1, 2, 3
 
@@ -142,46 +148,57 @@ def tile_attend_gat_q_ts_kernel(tc, qT, kT, vT, doT, rw, ts, offs, out):
         nc.scalar.mul(rw2[:], bank[:, P - CHUNKS : P], 2.0)
 
 
-        def gather_pool(name, pool):
-            grouped = held(name + "_grouped", [P, SLOTS, PACK], BF16)
-            for j in range(PACK):
-                nc.vector.tensor_copy(out=grouped[:, :, j], in_=pool[j][:].indirect(offsets[:]))
-            return grouped, quantized(name, grouped[:], SLOTS, E4M3)
+        k_grouped = held("k_grouped", [P, SLOTS, PACK], BF16)
+        k_planes = []
+        for u, engine in enumerate((SCALAR, VECTOR)):
+            pair = held("k_listed" + str(u), [P, 2 * SLOTS], BF16)
+            for z in range(2):
+                k_planes.append(pair[:, z * SLOTS : (z + 1) * SLOTS])
+                nc.vector.tensor_copy(out=k_planes[-1], in_=k_pool[2 * u + z][:].indirect(offsets[:]))
+            interleave(engine, k_grouped[:, :, 2 * u : 2 * u + 2], pair[:].rearrange("p (z slot) -> p z slot", z=2))
+        k_mx = quantized("k", k_grouped[:], SLOTS, E4M3)
 
-        k_grouped, k_mx = gather_pool("k", k_pool)
-        v_mx = gather_pool("v", v_pool)[1]
+        v_grouped = held("v_grouped", [P, SLOTS, PACK], BF16)
+        for j in range(PACK):
+            nc.vector.tensor_copy(out=v_grouped[:, :, j], in_=v_pool[j][:].indirect(offsets[:]))
+        v_mx = quantized("v", v_grouped[:], SLOTS, E4M3)
 
-        do_mx, do_pieces = [], []
-        for h, part in enumerate(do_raw):
-            width = P if h == 0 else DO_COLS
-            for first in range(0, DO_COLS, width):
-                do_pieces.append("do_grouped" + str(len(do_pieces)))
-                grouped = held(do_pieces[-1], [P, width, PACK], BF16)
-                interleave(VECTOR if h == DO_ON_VECTOR else SCALAR, grouped[:], part[:, :, first : first + width])
-                operand = quantized(do_pieces[-1], grouped[:], width, E5M2)
-                do_mx.extend((operand, col) for col in range(0, width, P))
+        do_grouped, do_mx = [], []
+
+        def interleave_do(chunk):
+            h, first = divmod(chunk * P, DO_COLS)
+            do_grouped.append(held("do_grouped" + str(chunk), [P, P, PACK], BF16))
+            engine = VECTOR if chunk in DO_ON_VECTOR else SCALAR
+            interleave(engine, do_grouped[chunk][:], do_raw[h][:, :, first : first + P])
+
+        def quantize_do(chunk, on=None):
+            do_mx.append(mx_tiles("do" + str(chunk), P, E5M2, on))
+            quantize(do_mx[chunk], slice(0, P), do_grouped[chunk][:])
+
+        for chunk in range(DO_EARLY):
+            interleave_do(chunk)
+            if chunk < DO_LEAD:
+                quantize_do(chunk)
 
         q_mx = []
         for h, part in enumerate(q_raw):
             grouped = held("q_grouped" + str(h), [P, Q_COLS, PACK], BF16)
-            split = Q_ON_SCALAR if h == 0 else Q_COLS // 2
+            split = Q_ON_SCALAR[h]
             interleave(SCALAR if h == 0 else VECTOR, grouped[:, :split, :], part[:, :, :split])
             interleave(VECTOR, grouped[:, split:, :], part[:, :, split:])
             q_mx.append(quantized("q" + str(h), grouped[:], Q_COLS, E4M3))
 
-        k_words = k_grouped[:].rearrange("p slot j -> p (slot j)").bitcast(F32)
-        k_words = k_words.rearrange("p (m t u) -> p t u m", t=PACK, u=2)
-        kt_grouped = [
-            held("kt_grouped" + str(u), [P, 2 * P, PACK], BF16, on) for u, on in enumerate(("q_raw0", "q_grouped0"))
-        ]
-        for u in range(2):
-            bank = next_bank("turn")
-            for t in range(PACK):
-                nc.tensor.transpose(bank[:, t * P : (t + 1) * P], k_words[:, t, u, :], ident[:])
-            nc.scalar.copy(out=kt_grouped[u][:], in_=bank.bitcast(BF16).rearrange("m (t col) -> m col t", t=PACK))
-        kt_mx = mx_tiles("kt", FEATURES, E4M3, do_pieces[0])
-        for u in range(2):
-            quantize(kt_mx, slice(u * 2 * P, (u + 1) * 2 * P), kt_grouped[u][:])
+        kt_grouped = [held("kt_grouped" + str(u), [P, 2 * P, PACK], BF16, on) for u, on in enumerate((None, "q_raw0"))]
+        for j in range(PACK):
+            bank = next_bank("turn")[:, : 2 * P].rearrange("m (u p) -> m u p", u=2)
+            words = k_planes[j].bitcast(F32).rearrange("p (m u) -> p u m", u=2)
+            for u in range(2):
+                nc.tensor.transpose(bank[:, u, :], words[:, u, :], ident[:])
+            columns = kt_grouped[j // 2][:, j % 2 * P : (j % 2 + 1) * P, :]
+            nc.scalar.copy(out=columns.bitcast(F32), in_=bank.rearrange("m u p -> m p u"))
+        kt_mx = mx_tiles("kt", FEATURES, E4M3)
+        for half in range(2):
+            quantize(kt_mx, slice(half * 2 * P, (half + 1) * 2 * P), kt_grouped[half][:])
 
         gated = []
         for h in range(QUERIES // Q_COLS):
@@ -191,7 +208,7 @@ def tile_attend_gat_q_ts_kernel(tc, qT, kT, vT, doT, rw, ts, offs, out):
                 bank = next_bank("score")
                 product(bank, k_mx, c * P, q_mx[h])
                 nc.scalar.activation(out=relu[:, c, :], in_=bank, func=RELU, scale=ts_col[:, c : c + 1])
-                nc.gpsimd.tensor_scalar(
+                (nc.vector if h * SLOT_TILES + c < TS_ON_VECTOR else nc.gpsimd).tensor_scalar(
                     out=gated[h][:, c, :],
                     in0=relu[:, c, :],
                     scalar1=ts_col[:, c : c + 1],
@@ -200,15 +217,14 @@ def tile_attend_gat_q_ts_kernel(tc, qT, kT, vT, doT, rw, ts, offs, out):
                     op1=ADD,
                 )
 
-        late_on = ["do_raw1", do_pieces[1]]
-        weights_on = [None] * (CHUNKS - len(late_on)) + late_on
         weights = []
         for chunk in range(CHUNKS):
             h, first = divmod(chunk * P, Q_COLS)
             bank = next_bank("weight")
             for c in range(SLOT_TILES):
                 nc.tensor.transpose(bank[:, c * P : (c + 1) * P], gated[h][:, c, first : first + P], ident[:])
-            weights.append(held("weights" + str(chunk), [P, 2, P, 2], F32, weights_on[chunk]))
+            on = "do_raw1" if chunk >= CHUNKS - LATE_WEIGHTS else None
+            weights.append(held("weights" + str(chunk), [P, 2, P, 2], F32, on))
             nc.scalar.activation(
                 out=weights[chunk][:],
                 in_=bank.rearrange("r (m u z) -> r u m z", u=2, z=2),
@@ -220,8 +236,9 @@ def tile_attend_gat_q_ts_kernel(tc, qT, kT, vT, doT, rw, ts, offs, out):
 
         def make_ds(chunk):
             bank = next_bank("dp")
-            product(bank, *do_mx[chunk], v_mx)
-            ds_tiles.append(held("ds" + str(chunk), [P, 2, P, 2], BF16))
+            product(bank, do_mx[chunk], 0, v_mx)
+            on = "do_grouped" + str(chunk + DS_BEHIND) if chunk + DS_BEHIND < CHUNKS else None
+            ds_tiles.append(held("ds" + str(chunk), [P, 2, P, 2], BF16, on))
             nc.vector.tensor_tensor(
                 out=ds_tiles[chunk][:],
                 in0=bank.rearrange("r (m u z) -> r u m z", u=2, z=2),
@@ -244,19 +261,23 @@ def tile_attend_gat_q_ts_kernel(tc, qT, kT, vT, doT, rw, ts, offs, out):
         def finish(chunk):
             bank = next_bank("result")
             product(bank, ds_mx[chunk], 0, kt_mx)
-            result = held("result" + str(chunk), [P, P, 2, 2], F32)
+            result = held("result" + str(chunk), [P, P, PACK], F32)
             last = chunk == CHUNKS - 1
             pieces = 2 if last else 1
             for piece in range(pieces):
                 span = slice(piece * P // pieces, (piece + 1) * P // pieces)
-                ordered = bank.rearrange("r (u p z) -> r p u z", u=2, z=2)[:, span]
-                copy_on(VECTOR if last else SCALAR, result[:, span], ordered)
+                ordered = bank.rearrange("r (j p) -> r p j", j=PACK)[:, span]
+                copy_on(VECTOR if chunk in RESULTS_ON_VECTOR else SCALAR, result[:, span], ordered)
                 nc.sync.dma_start(
                     out=out[0, chunk * P : (chunk + 1) * P, span.start * PACK : span.stop * PACK],
-                    in_=result[:, span].rearrange("r p u z -> r (p u z)"),
+                    in_=result[:, span].rearrange("r p j -> r (p j)"),
                 )
 
         for step in range(CHUNKS + FINISH_LAG):
             for stage, lag in ((quantize_ds, QUANTIZE_LAG), (turn_ds, TURN_LAG), (make_ds, 0), (finish, FINISH_LAG)):
                 if 0 <= step - lag < CHUNKS:
                     stage(step - lag)
+            if len(do_grouped) < CHUNKS and step >= TURN_LAG:
+                interleave_do(len(do_grouped))
+            if step + DO_LEAD < CHUNKS:
+                quantize_do(step + DO_LEAD, "weights" + str(step))

@@ -12,6 +12,7 @@ E4M3 = mybir.dt.float8_e4m3fn_x4
 E5M2 = mybir.dt.float8_e5m2_x4
 MULT = mybir.AluOpType.mult
 ADD = mybir.AluOpType.add
+MAX = mybir.AluOpType.max
 RELU = mybir.ActivationFunctionType.Relu
 COPY = mybir.ActivationFunctionType.Copy
 
@@ -34,17 +35,27 @@ DO_ON_VECTOR = (2,)
 DO_LEAD = 4
 DO_EARLY = 6
 DS_BEHIND = 2
+DS_HELD = 2
+LAST_RELU = 1
+HALVED = 2
+DS_SPLIT = 0
+LAST_PIECES = 2
+WEIGHTS_ON_VECTOR = -1
+DOQ_HOLD = 0
+DO_ON_GPSIMD = ()
+WARM = 4
 RESULTS_ON_VECTOR = (7,)
 TURNS_ON_VECTOR = 2
 TURN_LAG, QUANTIZE_LAG, FINISH_LAG = 1, 2, 3
 
+DPB, DSB, RSB = (0, 1, 2), (3, 4), (5, 6, 7)
 BANKS_OF = {
     "score": (0, 1, 2, 3),
     "turn": (4, 5, 6, 7),
     "weight": (0, 1, 2, 3, 4, 5, 6, 7),
-    "dp": (0, 1, 2),
-    "ds": (3, 4),
-    "result": (5, 6, 7),
+    "dp": DPB,
+    "ds": DSB,
+    "result": RSB,
 }
 
 FLOPS = 3 * 2 * QUERIES * SLOTS * FEATURES
@@ -159,9 +170,15 @@ def tile_attend_gat_q_ts_kernel(tc, qT, kT, vT, doT, rw, ts, offs, out):
         k_mx = quantized("k", k_grouped[:], SLOTS, E4M3)
 
         v_grouped = held("v_grouped", [P, SLOTS, PACK], BF16)
-        for j in range(PACK):
+        for j in range(PACK - 1):
             nc.vector.tensor_copy(out=v_grouped[:, :, j], in_=v_pool[j][:].indirect(offsets[:]))
-        v_mx = quantized("v", v_grouped[:], SLOTS, E4M3)
+        v_mx = mx_tiles("v", SLOTS, E4M3)
+        halves = [slice(half * SLOTS // 2, (half + 1) * SLOTS // 2) for half in range(2)]
+        for slots in halves:
+            entries = offsets[:, slots.start // LIST_ROWS : slots.stop // LIST_ROWS]
+            nc.vector.tensor_copy(out=v_grouped[:, slots, PACK - 1], in_=v_pool[PACK - 1][:].indirect(entries))
+        for slots in halves:
+            quantize(v_mx, slots, v_grouped[:, slots, :])
 
         do_grouped, do_mx = [], []
 
@@ -169,6 +186,16 @@ def tile_attend_gat_q_ts_kernel(tc, qT, kT, vT, doT, rw, ts, offs, out):
             h, first = divmod(chunk * P, DO_COLS)
             do_grouped.append(held("do_grouped" + str(chunk), [P, P, PACK], BF16))
             engine = VECTOR if chunk in DO_ON_VECTOR else SCALAR
+            if chunk in DO_ON_GPSIMD:
+                nc.gpsimd.tensor_scalar(
+                    out=do_grouped[chunk][:].rearrange("p (run x) j -> p run j x", x=LINE),
+                    in0=do_raw[h][:, :, first : first + P].rearrange("p j (run x) -> p run j x", x=LINE),
+                    scalar1=1.0,
+                    scalar2=0.0,
+                    op0=MULT,
+                    op1=ADD,
+                )
+                return
             interleave(engine, do_grouped[chunk][:], do_raw[h][:, :, first : first + P])
 
         def quantize_do(chunk, on=None):
@@ -200,51 +227,71 @@ def tile_attend_gat_q_ts_kernel(tc, qT, kT, vT, doT, rw, ts, offs, out):
         for half in range(2):
             quantize(kt_mx, slice(half * 2 * P, (half + 1) * 2 * P), kt_grouped[half][:])
 
+        def times_ts(engine, c, dst, src):
+            engine.tensor_scalar(out=dst, in0=src, scalar1=ts_col[:, c : c + 1], scalar2=0.0, op0=MULT, op1=ADD)
+
         gated = []
         for h in range(QUERIES // Q_COLS):
             relu = held("relu" + str(h), [P, SLOT_TILES, Q_COLS], F32, "k_pool" + str(h))
-            gated.append(held("gated" + str(h), [P, SLOT_TILES, Q_COLS], F32))
+            relu = [relu[:, c, :] for c in range(SLOT_TILES)]
+            tile = held("gated" + str(h), [P, SLOT_TILES, Q_COLS], F32)
+            gated.append([tile[:, c, :] for c in range(SLOT_TILES)])
             for c in range(SLOT_TILES):
                 bank = next_bank("score")
                 product(bank, k_mx, c * P, q_mx[h])
-                nc.scalar.activation(out=relu[:, c, :], in_=bank, func=RELU, scale=ts_col[:, c : c + 1])
-                (nc.vector if h * SLOT_TILES + c < TS_ON_VECTOR else nc.gpsimd).tensor_scalar(
-                    out=gated[h][:, c, :],
-                    in0=relu[:, c, :],
-                    scalar1=ts_col[:, c : c + 1],
-                    scalar2=0.0,
-                    op0=MULT,
-                    op1=ADD,
-                )
+                scale = ts_col[:, c : c + 1]
+                last = h * SLOT_TILES + c == 2 * SLOT_TILES - 1
+                if last and LAST_RELU:
+                    relu[c] = held("last_relu", [P, Q_COLS], F32, "v_pool0")[:]
+                    nc.vector.tensor_scalar(out=relu[c], in0=bank, scalar1=scale, scalar2=0.0, op0=MULT, op1=MAX)
+                else:
+                    nc.scalar.activation(out=relu[c], in_=bank, func=RELU, scale=scale)
+                if h * SLOT_TILES + c < 2 * SLOT_TILES - HALVED:
+                    times_ts(nc.vector if h * SLOT_TILES + c < TS_ON_VECTOR else nc.gpsimd, c, gated[h][c], relu[c])
+        for cols in (slice(0, Q_COLS // 2), slice(Q_COLS // 2, Q_COLS)):
+            for c in range(SLOT_TILES - HALVED, SLOT_TILES):
+                times_ts(nc.gpsimd, c, gated[1][c][:, cols], relu[c][:, cols])
 
+        weight_banks = [next_bank("weight") for chunk in range(CHUNKS)]
+
+        def turn_gated(chunk, c):
+            h, first = divmod(chunk * P, Q_COLS)
+            nc.tensor.transpose(weight_banks[chunk][:, c * P : (c + 1) * P], gated[h][c][:, first : first + P], ident[:])
+
+        for chunk in range(CHUNKS // 2):
+            for c in range(SLOT_TILES):
+                turn_gated(chunk, c)
+        for c in range(SLOT_TILES - HALVED):
+            for chunk in range(CHUNKS // 2, CHUNKS):
+                turn_gated(chunk, c)
+        for chunk in range(CHUNKS // 2, CHUNKS):
+            for c in range(SLOT_TILES - HALVED, SLOT_TILES):
+                turn_gated(chunk, c)
         weights = []
         for chunk in range(CHUNKS):
-            h, first = divmod(chunk * P, Q_COLS)
-            bank = next_bank("weight")
-            for c in range(SLOT_TILES):
-                nc.tensor.transpose(bank[:, c * P : (c + 1) * P], gated[h][:, c, first : first + P], ident[:])
-            on = "do_raw1" if chunk >= CHUNKS - LATE_WEIGHTS else None
+            on = "do_raw1" if chunk >= CHUNKS - LATE_WEIGHTS else "v_pool2" if chunk == WEIGHTS_ON_VECTOR else None
             weights.append(held("weights" + str(chunk), [P, 2, P, 2], F32, on))
-            nc.scalar.activation(
-                out=weights[chunk][:],
-                in_=bank.rearrange("r (m u z) -> r u m z", u=2, z=2),
-                func=COPY,
-                scale=rw2[:, chunk : chunk + 1],
-            )
+            turned = weight_banks[chunk].rearrange("r (m u z) -> r u m z", u=2, z=2)
+            if chunk == WEIGHTS_ON_VECTOR:
+                nc.vector.tensor_scalar_mul(weights[chunk][:], turned, rw2[:, chunk : chunk + 1])
+            else:
+                nc.scalar.activation(out=weights[chunk][:], in_=turned, func=COPY, scale=rw2[:, chunk : chunk + 1])
+
+        for _ in range(WARM):
+            product(banks[4][:], k_mx, 0, q_mx[1])
 
         ds_tiles, ds_grouped, ds_mx = [], [], []
 
         def make_ds(chunk):
             bank = next_bank("dp")
             product(bank, do_mx[chunk], 0, v_mx)
-            on = "do_grouped" + str(chunk + DS_BEHIND) if chunk + DS_BEHIND < CHUNKS else None
+            on = "do_grouped" + str(chunk + DS_BEHIND) if chunk < DS_HELD else None
             ds_tiles.append(held("ds" + str(chunk), [P, 2, P, 2], BF16, on))
-            nc.vector.tensor_tensor(
-                out=ds_tiles[chunk][:],
-                in0=bank.rearrange("r (m u z) -> r u m z", u=2, z=2),
-                in1=weights[chunk][:],
-                op=MULT,
-            )
+            dp = bank.rearrange("r (m u z) -> r u m z", u=2, z=2)
+            for us in [slice(0, 1), slice(1, 2)] if chunk >= CHUNKS - DS_SPLIT else [slice(0, 2)]:
+                nc.vector.tensor_tensor(
+                    out=ds_tiles[chunk][:, us], in0=dp[:, us], in1=weights[chunk][:, us], op=MULT
+                )
 
         def turn_ds(chunk):
             bank = next_bank("ds")[:, : 2 * P].rearrange("m (u r) -> m u r", u=2)
@@ -263,7 +310,7 @@ def tile_attend_gat_q_ts_kernel(tc, qT, kT, vT, doT, rw, ts, offs, out):
             product(bank, ds_mx[chunk], 0, kt_mx)
             result = held("result" + str(chunk), [P, P, PACK], F32)
             last = chunk == CHUNKS - 1
-            pieces = 2 if last else 1
+            pieces = LAST_PIECES if last else 1
             for piece in range(pieces):
                 span = slice(piece * P // pieces, (piece + 1) * P // pieces)
                 ordered = bank.rearrange("r (j p) -> r p j", j=PACK)[:, span]
@@ -280,4 +327,4 @@ def tile_attend_gat_q_ts_kernel(tc, qT, kT, vT, doT, rw, ts, offs, out):
             if len(do_grouped) < CHUNKS and step >= TURN_LAG:
                 interleave_do(len(do_grouped))
             if step + DO_LEAD < CHUNKS:
-                quantize_do(step + DO_LEAD, "weights" + str(step))
+                quantize_do(step + DO_LEAD, "weights" + str(step) if DOQ_HOLD else None)

@@ -28,34 +28,23 @@ Q_COLS = 512
 DO_COLS = 256
 
 VECTOR, SCALAR = "vector", "scalar"
-TS_ON_VECTOR = 2
-LATE_WEIGHTS = 1
-Q_ON_SCALAR = (256, 256)
-DO_ON_VECTOR = (2,)
-DO_LEAD = 4
+FIRST_ON_VECTOR = 2
+HALVED_TILES = 2
+DO_ON_VECTOR = 2
 DO_EARLY = 6
-DS_BEHIND = 2
-DS_HELD = 2
-LAST_RELU = 1
-HALVED = 2
-DS_SPLIT = 0
-LAST_PIECES = 2
-WEIGHTS_ON_VECTOR = -1
-DOQ_HOLD = 0
-DO_ON_GPSIMD = ()
-WARM = 4
-RESULTS_ON_VECTOR = (7,)
+DO_LEAD = 4
+HELD_DS = 2
 TURNS_ON_VECTOR = 2
+WARM_UPS = 4
 TURN_LAG, QUANTIZE_LAG, FINISH_LAG = 1, 2, 3
 
-DPB, DSB, RSB = (0, 1, 2), (3, 4), (5, 6, 7)
 BANKS_OF = {
     "score": (0, 1, 2, 3),
     "turn": (4, 5, 6, 7),
     "weight": (0, 1, 2, 3, 4, 5, 6, 7),
-    "dp": DPB,
-    "ds": DSB,
-    "result": RSB,
+    "dp": (0, 1, 2),
+    "ds": (3, 4),
+    "result": (5, 6, 7),
 }
 
 FLOPS = 3 * 2 * QUERIES * SLOTS * FEATURES
@@ -91,8 +80,8 @@ def tile_attend_gat_q_ts_kernel(tc, qT, kT, vT, doT, rw, ts, offs, out):
                 planes.rearrange("p j (run x) -> p run j x", x=LINE),
             )
 
-        def mx_tiles(name, width, fmt, on=None):
-            return held(name + "_codes", [P, width], U32, on), held(name + "_scales", [P, width], U8), fmt
+        def mx_tiles(name, width, fmt):
+            return held(name + "_codes", [P, width], U32), held(name + "_scales", [P, width], U8), fmt
 
         def quantize(operand, cols, grouped):
             codes, scales, fmt = operand
@@ -161,23 +150,26 @@ def tile_attend_gat_q_ts_kernel(tc, qT, kT, vT, doT, rw, ts, offs, out):
 
         k_grouped = held("k_grouped", [P, SLOTS, PACK], BF16)
         k_planes = []
-        for u, engine in enumerate((SCALAR, VECTOR)):
-            pair = held("k_listed" + str(u), [P, 2 * SLOTS], BF16)
-            for z in range(2):
-                k_planes.append(pair[:, z * SLOTS : (z + 1) * SLOTS])
-                nc.vector.tensor_copy(out=k_planes[-1], in_=k_pool[2 * u + z][:].indirect(offsets[:]))
-            interleave(engine, k_grouped[:, :, 2 * u : 2 * u + 2], pair[:].rearrange("p (z slot) -> p z slot", z=2))
+        for first, engine in ((0, SCALAR), (2, VECTOR)):
+            pair = held("k_listed" + str(first), [P, 2 * SLOTS], BF16)
+            for j in range(first, first + 2):
+                k_planes.append(pair[:, (j - first) * SLOTS : (j - first + 1) * SLOTS])
+                nc.vector.tensor_copy(out=k_planes[j], in_=k_pool[j][:].indirect(offsets[:]))
+            interleave(engine, k_grouped[:, :, first : first + 2], pair[:].rearrange("p (j slot) -> p j slot", j=2))
         k_mx = quantized("k", k_grouped[:], SLOTS, E4M3)
 
-        v_grouped = held("v_grouped", [P, SLOTS, PACK], BF16)
+        v_listed = held("v_listed", [P, (PACK - 1) * SLOTS], BF16)
+        v_planes = v_listed[:].rearrange("p (j slot) -> p j slot", j=PACK - 1)
         for j in range(PACK - 1):
-            nc.vector.tensor_copy(out=v_grouped[:, :, j], in_=v_pool[j][:].indirect(offsets[:]))
+            nc.vector.tensor_copy(out=v_planes[:, j, :], in_=v_pool[j][:].indirect(offsets[:]))
+        v_grouped = held("v_grouped", [P, SLOTS, PACK], BF16)
+        interleave(VECTOR, v_grouped[:, :, : PACK - 1], v_planes)
         v_mx = mx_tiles("v", SLOTS, E4M3)
-        halves = [slice(half * SLOTS // 2, (half + 1) * SLOTS // 2) for half in range(2)]
-        for slots in halves:
+        slot_halves = (slice(0, SLOTS // 2), slice(SLOTS // 2, SLOTS))
+        for slots in slot_halves:
             entries = offsets[:, slots.start // LIST_ROWS : slots.stop // LIST_ROWS]
             nc.vector.tensor_copy(out=v_grouped[:, slots, PACK - 1], in_=v_pool[PACK - 1][:].indirect(entries))
-        for slots in halves:
+        for slots in slot_halves:
             quantize(v_mx, slots, v_grouped[:, slots, :])
 
         do_grouped, do_mx = [], []
@@ -185,37 +177,26 @@ def tile_attend_gat_q_ts_kernel(tc, qT, kT, vT, doT, rw, ts, offs, out):
         def interleave_do(chunk):
             h, first = divmod(chunk * P, DO_COLS)
             do_grouped.append(held("do_grouped" + str(chunk), [P, P, PACK], BF16))
-            engine = VECTOR if chunk in DO_ON_VECTOR else SCALAR
-            if chunk in DO_ON_GPSIMD:
-                nc.gpsimd.tensor_scalar(
-                    out=do_grouped[chunk][:].rearrange("p (run x) j -> p run j x", x=LINE),
-                    in0=do_raw[h][:, :, first : first + P].rearrange("p j (run x) -> p run j x", x=LINE),
-                    scalar1=1.0,
-                    scalar2=0.0,
-                    op0=MULT,
-                    op1=ADD,
-                )
-                return
+            engine = VECTOR if chunk == DO_ON_VECTOR else SCALAR
             interleave(engine, do_grouped[chunk][:], do_raw[h][:, :, first : first + P])
 
-        def quantize_do(chunk, on=None):
-            do_mx.append(mx_tiles("do" + str(chunk), P, E5M2, on))
-            quantize(do_mx[chunk], slice(0, P), do_grouped[chunk][:])
+        def quantize_do(chunk):
+            do_mx.append(quantized("do" + str(chunk), do_grouped[chunk][:], P, E5M2))
 
         for chunk in range(DO_EARLY):
             interleave_do(chunk)
             if chunk < DO_LEAD:
                 quantize_do(chunk)
 
+        query_halves = (slice(0, Q_COLS // 2), slice(Q_COLS // 2, Q_COLS))
         q_mx = []
         for h, part in enumerate(q_raw):
             grouped = held("q_grouped" + str(h), [P, Q_COLS, PACK], BF16)
-            split = Q_ON_SCALAR[h]
-            interleave(SCALAR if h == 0 else VECTOR, grouped[:, :split, :], part[:, :, :split])
-            interleave(VECTOR, grouped[:, split:, :], part[:, :, split:])
+            for engine, cols in zip((SCALAR if h == 0 else VECTOR, VECTOR), query_halves):
+                interleave(engine, grouped[:, cols, :], part[:, :, cols])
             q_mx.append(quantized("q" + str(h), grouped[:], Q_COLS, E4M3))
 
-        kt_grouped = [held("kt_grouped" + str(u), [P, 2 * P, PACK], BF16, on) for u, on in enumerate((None, "q_raw0"))]
+        kt_grouped = [held("kt_grouped0", [P, 2 * P, PACK], BF16), held("kt_grouped1", [P, 2 * P, PACK], BF16, "q_raw0")]
         for j in range(PACK):
             bank = next_bank("turn")[:, : 2 * P].rearrange("m (u p) -> m u p", u=2)
             words = k_planes[j].bitcast(F32).rearrange("p (m u) -> p u m", u=2)
@@ -232,66 +213,69 @@ def tile_attend_gat_q_ts_kernel(tc, qT, kT, vT, doT, rw, ts, offs, out):
 
         gated = []
         for h in range(QUERIES // Q_COLS):
-            relu = held("relu" + str(h), [P, SLOT_TILES, Q_COLS], F32, "k_pool" + str(h))
-            relu = [relu[:, c, :] for c in range(SLOT_TILES)]
-            tile = held("gated" + str(h), [P, SLOT_TILES, Q_COLS], F32)
-            gated.append([tile[:, c, :] for c in range(SLOT_TILES)])
+            last_load = h == QUERIES // Q_COLS - 1
+            on_scalar = SLOT_TILES - 1 if last_load else SLOT_TILES
+            whole_tiles = SLOT_TILES - HALVED_TILES if last_load else SLOT_TILES
+            relu_tile = held("relu" + str(h), [P, on_scalar, Q_COLS], F32, "k_pool" + str(h))
+            gated.append(held("gated" + str(h), [P, SLOT_TILES, Q_COLS], F32))
+            relu = []
             for c in range(SLOT_TILES):
                 bank = next_bank("score")
                 product(bank, k_mx, c * P, q_mx[h])
                 scale = ts_col[:, c : c + 1]
-                last = h * SLOT_TILES + c == 2 * SLOT_TILES - 1
-                if last and LAST_RELU:
-                    relu[c] = held("last_relu", [P, Q_COLS], F32, "v_pool0")[:]
-                    nc.vector.tensor_scalar(out=relu[c], in0=bank, scalar1=scale, scalar2=0.0, op0=MULT, op1=MAX)
-                else:
+                if c < on_scalar:
+                    relu.append(relu_tile[:, c, :])
                     nc.scalar.activation(out=relu[c], in_=bank, func=RELU, scale=scale)
-                if h * SLOT_TILES + c < 2 * SLOT_TILES - HALVED:
-                    times_ts(nc.vector if h * SLOT_TILES + c < TS_ON_VECTOR else nc.gpsimd, c, gated[h][c], relu[c])
-        for cols in (slice(0, Q_COLS // 2), slice(Q_COLS // 2, Q_COLS)):
-            for c in range(SLOT_TILES - HALVED, SLOT_TILES):
-                times_ts(nc.gpsimd, c, gated[1][c][:, cols], relu[c][:, cols])
+                else:
+                    relu.append(held("last_relu", [P, Q_COLS], F32, "v_pool0")[:])
+                    nc.vector.tensor_scalar(out=relu[c], in0=bank, scalar1=scale, scalar2=0.0, op0=MULT, op1=MAX)
+                if c < whole_tiles:
+                    engine = nc.vector if h == 0 and c < FIRST_ON_VECTOR else nc.gpsimd
+                    times_ts(engine, c, gated[h][:, c, :], relu[c])
+            for cols in query_halves:
+                for c in range(whole_tiles, SLOT_TILES):
+                    times_ts(nc.gpsimd, c, gated[h][:, c, cols], relu[c][:, cols])
 
         weight_banks = [next_bank("weight") for chunk in range(CHUNKS)]
 
         def turn_gated(chunk, c):
             h, first = divmod(chunk * P, Q_COLS)
-            nc.tensor.transpose(weight_banks[chunk][:, c * P : (c + 1) * P], gated[h][c][:, first : first + P], ident[:])
+            place = weight_banks[chunk][:, c * P : (c + 1) * P]
+            nc.tensor.transpose(place, gated[h][:, c, first : first + P], ident[:])
 
-        for chunk in range(CHUNKS // 2):
+        first_chunks, second_chunks = range(CHUNKS // 2), range(CHUNKS // 2, CHUNKS)
+        for chunk in first_chunks:
             for c in range(SLOT_TILES):
                 turn_gated(chunk, c)
-        for c in range(SLOT_TILES - HALVED):
-            for chunk in range(CHUNKS // 2, CHUNKS):
+        for c in range(SLOT_TILES - HALVED_TILES):
+            for chunk in second_chunks:
                 turn_gated(chunk, c)
-        for chunk in range(CHUNKS // 2, CHUNKS):
-            for c in range(SLOT_TILES - HALVED, SLOT_TILES):
+        for chunk in second_chunks:
+            for c in range(SLOT_TILES - HALVED_TILES, SLOT_TILES):
                 turn_gated(chunk, c)
         weights = []
         for chunk in range(CHUNKS):
-            on = "do_raw1" if chunk >= CHUNKS - LATE_WEIGHTS else "v_pool2" if chunk == WEIGHTS_ON_VECTOR else None
+            on = "do_raw1" if chunk == CHUNKS - 1 else None
             weights.append(held("weights" + str(chunk), [P, 2, P, 2], F32, on))
-            turned = weight_banks[chunk].rearrange("r (m u z) -> r u m z", u=2, z=2)
-            if chunk == WEIGHTS_ON_VECTOR:
-                nc.vector.tensor_scalar_mul(weights[chunk][:], turned, rw2[:, chunk : chunk + 1])
-            else:
-                nc.scalar.activation(out=weights[chunk][:], in_=turned, func=COPY, scale=rw2[:, chunk : chunk + 1])
+            nc.scalar.activation(
+                out=weights[chunk][:],
+                in_=weight_banks[chunk].rearrange("r (m u z) -> r u m z", u=2, z=2),
+                func=COPY,
+                scale=rw2[:, chunk : chunk + 1],
+            )
 
-        for _ in range(WARM):
-            product(banks[4][:], k_mx, 0, q_mx[1])
+        for warm_up in range(WARM_UPS):
+            product(weight_banks[CHUNKS // 2], k_mx, 0, q_mx[1])
 
         ds_tiles, ds_grouped, ds_mx = [], [], []
 
         def make_ds(chunk):
             bank = next_bank("dp")
             product(bank, do_mx[chunk], 0, v_mx)
-            on = "do_grouped" + str(chunk + DS_BEHIND) if chunk < DS_HELD else None
+            on = "do_grouped" + str(chunk + DO_COLS // P) if chunk < HELD_DS else None
             ds_tiles.append(held("ds" + str(chunk), [P, 2, P, 2], BF16, on))
             dp = bank.rearrange("r (m u z) -> r u m z", u=2, z=2)
-            for us in [slice(0, 1), slice(1, 2)] if chunk >= CHUNKS - DS_SPLIT else [slice(0, 2)]:
-                nc.vector.tensor_tensor(
-                    out=ds_tiles[chunk][:, us], in0=dp[:, us], in1=weights[chunk][:, us], op=MULT
-                )
+            nc.vector.tensor_tensor(out=ds_tiles[chunk][:], in0=dp, in1=weights[chunk][:], op=MULT)
 
         def turn_ds(chunk):
             bank = next_bank("ds")[:, : 2 * P].rearrange("m (u r) -> m u r", u=2)
@@ -310,11 +294,11 @@ def tile_attend_gat_q_ts_kernel(tc, qT, kT, vT, doT, rw, ts, offs, out):
             product(bank, ds_mx[chunk], 0, kt_mx)
             result = held("result" + str(chunk), [P, P, PACK], F32)
             last = chunk == CHUNKS - 1
-            pieces = LAST_PIECES if last else 1
+            pieces = 2 if last else 1
             for piece in range(pieces):
                 span = slice(piece * P // pieces, (piece + 1) * P // pieces)
                 ordered = bank.rearrange("r (j p) -> r p j", j=PACK)[:, span]
-                copy_on(VECTOR if chunk in RESULTS_ON_VECTOR else SCALAR, result[:, span], ordered)
+                copy_on(VECTOR if last else SCALAR, result[:, span], ordered)
                 nc.sync.dma_start(
                     out=out[0, chunk * P : (chunk + 1) * P, span.start * PACK : span.stop * PACK],
                     in_=result[:, span].rearrange("r p j -> r (p j)"),
@@ -327,4 +311,4 @@ def tile_attend_gat_q_ts_kernel(tc, qT, kT, vT, doT, rw, ts, offs, out):
             if len(do_grouped) < CHUNKS and step >= TURN_LAG:
                 interleave_do(len(do_grouped))
             if step + DO_LEAD < CHUNKS:
-                quantize_do(step + DO_LEAD, "weights" + str(step) if DOQ_HOLD else None)
+                quantize_do(step + DO_LEAD)

@@ -30,12 +30,11 @@ DO_COLS = 256
 VECTOR, SCALAR = "vector", "scalar"
 FIRST_ON_VECTOR = 2
 HALVED_TILES = 2
-DO_ON_VECTOR = 2
-DO_EARLY = 6
+DO_ON_VECTOR = (2, 7)
+DO_EARLY = 5
 DO_LEAD = 4
 HELD_DS = 2
 TURNS_ON_VECTOR = 2
-WARM_UPS = 4
 TURN_LAG, QUANTIZE_LAG, FINISH_LAG = 1, 2, 3
 
 BANKS_OF = {
@@ -174,10 +173,10 @@ def tile_attend_gat_q_ts_kernel(tc, qT, kT, vT, doT, rw, ts, offs, out):
 
         do_grouped, do_mx = [], []
 
-        def interleave_do(chunk):
+        def interleave_do(chunk, on=None):
             h, first = divmod(chunk * P, DO_COLS)
-            do_grouped.append(held("do_grouped" + str(chunk), [P, P, PACK], BF16))
-            engine = VECTOR if chunk == DO_ON_VECTOR else SCALAR
+            do_grouped.append(held("do_grouped" + str(chunk), [P, P, PACK], BF16, on))
+            engine = VECTOR if chunk in DO_ON_VECTOR else SCALAR
             interleave(engine, do_grouped[chunk][:], do_raw[h][:, :, first : first + P])
 
         def quantize_do(chunk):
@@ -196,7 +195,8 @@ def tile_attend_gat_q_ts_kernel(tc, qT, kT, vT, doT, rw, ts, offs, out):
                 interleave(engine, grouped[:, cols, :], part[:, :, cols])
             q_mx.append(quantized("q" + str(h), grouped[:], Q_COLS, E4M3))
 
-        kt_grouped = [held("kt_grouped0", [P, 2 * P, PACK], BF16), held("kt_grouped1", [P, 2 * P, PACK], BF16, "q_raw0")]
+        kt_shape = [P, 2 * P, PACK]
+        kt_grouped = [held("kt_grouped0", kt_shape, BF16), held("kt_grouped1", kt_shape, BF16, "q_raw0")]
         for j in range(PACK):
             bank = next_bank("turn")[:, : 2 * P].rearrange("m (u p) -> m u p", u=2)
             words = k_planes[j].bitcast(F32).rearrange("p (m u) -> p u m", u=2)
@@ -264,16 +264,13 @@ def tile_attend_gat_q_ts_kernel(tc, qT, kT, vT, doT, rw, ts, offs, out):
                 scale=rw2[:, chunk : chunk + 1],
             )
 
-        for warm_up in range(WARM_UPS):
-            product(weight_banks[CHUNKS // 2], k_mx, 0, q_mx[1])
-
-        ds_tiles, ds_grouped, ds_mx = [], [], []
+        ds_bytes, ds_tiles, ds_grouped, ds_mx = [], [], [], []
 
         def make_ds(chunk):
             bank = next_bank("dp")
             product(bank, do_mx[chunk], 0, v_mx)
-            on = "do_grouped" + str(chunk + DO_COLS // P) if chunk < HELD_DS else None
-            ds_tiles.append(held("ds" + str(chunk), [P, 2, P, 2], BF16, on))
+            ds_bytes.append("do_grouped" + str(chunk + DO_COLS // P) if chunk < HELD_DS else "ds" + str(chunk))
+            ds_tiles.append(held("ds" + str(chunk), [P, 2, P, 2], BF16, ds_bytes[chunk]))
             dp = bank.rearrange("r (m u z) -> r u m z", u=2, z=2)
             nc.vector.tensor_tensor(out=ds_tiles[chunk][:], in0=dp, in1=weights[chunk][:], op=MULT)
 
@@ -308,7 +305,8 @@ def tile_attend_gat_q_ts_kernel(tc, qT, kT, vT, doT, rw, ts, offs, out):
             for stage, lag in ((quantize_ds, QUANTIZE_LAG), (turn_ds, TURN_LAG), (make_ds, 0), (finish, FINISH_LAG)):
                 if 0 <= step - lag < CHUNKS:
                     stage(step - lag)
-            if len(do_grouped) < CHUNKS and step >= TURN_LAG:
-                interleave_do(len(do_grouped))
+            turned = step - TURN_LAG
+            if 0 <= turned < CHUNKS - DO_EARLY:
+                interleave_do(DO_EARLY + turned, ds_bytes[turned])
             if step + DO_LEAD < CHUNKS:
                 quantize_do(step + DO_LEAD)

@@ -150,11 +150,11 @@ def tile_attend_gat_q_ts_kernel(tc, qT, kT, vT, doT, rw, ts, offs, out):
         k_grouped = held("k_grouped", [P, SLOTS, PACK], BF16)
         k_planes = []
         for first, engine in ((0, SCALAR), (2, VECTOR)):
-            pair = held("k_listed" + str(first), [P, 2 * SLOTS], BF16)
+            listed = held("k_listed" + str(first), [P, 2 * SLOTS], BF16)
             for j in range(first, first + 2):
-                k_planes.append(pair[:, (j - first) * SLOTS : (j - first + 1) * SLOTS])
+                k_planes.append(listed[:, (j - first) * SLOTS : (j - first + 1) * SLOTS])
                 nc.vector.tensor_copy(out=k_planes[j], in_=k_pool[j][:].indirect(offsets[:]))
-            interleave(engine, k_grouped[:, :, first : first + 2], pair[:].rearrange("p (j slot) -> p j slot", j=2))
+            interleave(engine, k_grouped[:, :, first : first + 2], listed[:].rearrange("p (j slot) -> p j slot", j=2))
         k_mx = quantized("k", k_grouped[:], SLOTS, E4M3)
 
         v_listed = held("v_listed", [P, (PACK - 1) * SLOTS], BF16)
@@ -195,18 +195,19 @@ def tile_attend_gat_q_ts_kernel(tc, qT, kT, vT, doT, rw, ts, offs, out):
                 interleave(engine, grouped[:, cols, :], part[:, :, cols])
             q_mx.append(quantized("q" + str(h), grouped[:], Q_COLS, E4M3))
 
-        kt_shape = [P, 2 * P, PACK]
-        kt_grouped = [held("kt_grouped0", kt_shape, BF16), held("kt_grouped1", kt_shape, BF16, "q_raw0")]
-        for j in range(PACK):
-            bank = next_bank("turn")[:, : 2 * P].rearrange("m (u p) -> m u p", u=2)
-            words = k_planes[j].bitcast(F32).rearrange("p (m u) -> p u m", u=2)
-            for u in range(2):
-                nc.tensor.transpose(bank[:, u, :], words[:, u, :], ident[:])
-            columns = kt_grouped[j // 2][:, j % 2 * P : (j % 2 + 1) * P, :]
-            nc.scalar.copy(out=columns.bitcast(F32), in_=bank.rearrange("m u p -> m p u"))
         kt_mx = mx_tiles("kt", FEATURES, E4M3)
-        for half in range(2):
-            quantize(kt_mx, slice(half * 2 * P, (half + 1) * 2 * P), kt_grouped[half][:])
+        for pair, on in enumerate((None, "q_raw0")):
+            bank = next_bank("turn").rearrange("m (odd u p) -> m odd u p", odd=2, u=2)
+            for odd in range(2):
+                words = k_planes[2 * pair + odd].bitcast(F32).rearrange("p (m u) -> p u m", u=2)
+                for u in range(2):
+                    nc.tensor.transpose(bank[:, odd, u, :], words[:, u, :], ident[:])
+            kt_grouped = held("kt_grouped" + str(pair), [P, 2 * P, PACK], BF16, on)
+            nc.scalar.copy(
+                out=kt_grouped[:].bitcast(F32).rearrange("m (p odd) u -> m p odd u", odd=2),
+                in_=bank.rearrange("m odd u p -> m p odd u"),
+            )
+            quantize(kt_mx, slice(pair * 2 * P, (pair + 1) * 2 * P), kt_grouped[:])
 
         def times_ts(engine, c, dst, src):
             engine.tensor_scalar(out=dst, in0=src, scalar1=ts_col[:, c : c + 1], scalar2=0.0, op0=MULT, op1=ADD)
@@ -289,16 +290,16 @@ def tile_attend_gat_q_ts_kernel(tc, qT, kT, vT, doT, rw, ts, offs, out):
         def finish(chunk):
             bank = next_bank("result")
             product(bank, ds_mx[chunk], 0, kt_mx)
-            result = held("result" + str(chunk), [P, P, PACK], F32)
+            result = held("result" + str(chunk), [P, P, 2, 2], F32)
             last = chunk == CHUNKS - 1
             pieces = 2 if last else 1
             for piece in range(pieces):
                 span = slice(piece * P // pieces, (piece + 1) * P // pieces)
-                ordered = bank.rearrange("r (j p) -> r p j", j=PACK)[:, span]
+                ordered = bank.rearrange("r (pair p odd) -> r p pair odd", pair=2, odd=2)[:, span]
                 copy_on(VECTOR if last else SCALAR, result[:, span], ordered)
                 nc.sync.dma_start(
                     out=out[0, chunk * P : (chunk + 1) * P, span.start * PACK : span.stop * PACK],
-                    in_=result[:, span].rearrange("r p j -> r (p j)"),
+                    in_=result[:, span].rearrange("r p pair odd -> r (p pair odd)"),
                 )
 
         for step in range(CHUNKS + FINISH_LAG):

@@ -28,22 +28,19 @@ Q_COLS = 512
 DO_COLS = 256
 
 VECTOR, SCALAR = "vector", "scalar"
-FIRST_ON_VECTOR = 2
-HALVED_TILES = 2
-DO_ON_VECTOR = (2, 7)
-DO_EARLY = 5
-DO_LEAD = 4
-HELD_DS = 2
-TURNS_ON_VECTOR = 2
-TURN_LAG, QUANTIZE_LAG, FINISH_LAG = 1, 2, 3
+LAST_ON_VECTOR = 320
+Q_ON_SCALAR = 192
+DO_ON_VECTOR = (1,)
+DO_EARLY = 6
+DO_LEAD = 3
+RESULT_ON = {0: "do_raw2", 2: "do_raw3"}
+QUANTIZE_LAG, FINISH_LAG = 1, 1
 
 BANKS_OF = {
     "score": (0, 1, 2, 3),
     "turn": (4, 5, 6, 7),
-    "weight": (0, 1, 2, 3, 4, 5, 6, 7),
-    "dp": (0, 1, 2),
-    "ds": (3, 4),
-    "result": (5, 6, 7),
+    "dp": (0, 1, 2, 3),
+    "result": (4, 5, 6, 7),
 }
 
 FLOPS = 3 * 2 * QUERIES * SLOTS * FEATURES
@@ -79,8 +76,8 @@ def tile_attend_gat_q_ts_kernel(tc, qT, kT, vT, doT, rw, ts, offs, out):
                 planes.rearrange("p j (run x) -> p run j x", x=LINE),
             )
 
-        def mx_tiles(name, width, fmt):
-            return held(name + "_codes", [P, width], U32), held(name + "_scales", [P, width], U8), fmt
+        def mx_tiles(name, width, fmt, on=None):
+            return held(name + "_codes", [P, width], U32, on), held(name + "_scales", [P, width], U8), fmt
 
         def quantize(operand, cols, grouped):
             codes, scales, fmt = operand
@@ -93,15 +90,15 @@ def tile_attend_gat_q_ts_kernel(tc, qT, kT, vT, doT, rw, ts, offs, out):
             quantize(operand, slice(0, width), grouped)
             return operand
 
-        def product(bank, stationary, first, moving):
+        def product(bank, stationary, first, moving, start, width):
             s_codes, s_scales, s_fmt = stationary
             m_codes, m_scales, m_fmt = moving
             nc.tensor.matmul_mx(
                 out=bank,
                 lhsT=s_codes[:, first : first + P].bitcast(s_fmt),
                 lhsT_scale=s_scales[:, first : first + P],
-                rhs=m_codes[:].bitcast(m_fmt),
-                rhs_scale=m_scales[:],
+                rhs=m_codes[:, start : start + width].bitcast(m_fmt),
+                rhs_scale=m_scales[:, start : start + width],
                 start=True,
                 stop=True,
             )
@@ -134,60 +131,57 @@ def tile_attend_gat_q_ts_kernel(tc, qT, kT, vT, doT, rw, ts, offs, out):
         ident = held("ident", [P, P], F32)
         make_identity(nc, ident[:])
 
-        ts_listed = held("ts_listed", [P, SLOTS], F32)
-        nc.vector.tensor_copy(out=ts_listed[:], in_=ts_pool[:].indirect(offsets[:]))
-        bank = next_bank("turn").rearrange("p (c x) -> p c x", x=P)
-        for c in range(SLOT_TILES):
-            nc.tensor.transpose(bank[:, c, :], ts_listed[:, c * P : (c + 1) * P], ident[:])
-        ts_col = held("ts_col", [P, SLOT_TILES], F32)
-        nc.scalar.copy(out=ts_col[:], in_=bank[:, :, P - 1])
         bank = next_bank("turn")
         nc.tensor.transpose(bank[:, :P], rw_rows[:], ident[:])
-        rw2 = held("rw2", [P, CHUNKS], F32)
-        nc.scalar.mul(rw2[:], bank[:, P - CHUNKS : P], 2.0)
+        rw_col = held("rw_col", [P, CHUNKS], F32)
+        nc.scalar.mul(rw_col[:], bank[:, P - CHUNKS : P], 2.0)
+        ts_listed = held("ts_listed", [P, SLOTS], F32)
+        nc.vector.tensor_copy(out=ts_listed[:], in_=ts_pool[:].indirect(offsets[:]))
+        bank = next_bank("turn").rearrange("p (t x) -> p t x", x=P)
+        for t in range(PACK):
+            nc.tensor.transpose(bank[:, t, :], ts_listed[:].rearrange("p (m t) -> p t m", t=PACK)[:, t, :], ident[:])
+        ts_col = held("ts_col", [P, PACK], F32)
+        nc.scalar.copy(out=ts_col[:], in_=bank[:, :, P - 1])
+        rw_banks = [next_bank("turn") for h in range(QUERIES // Q_COLS)]
+        for chunk in range(CHUNKS):
+            h, first = divmod(chunk * P, Q_COLS)
+            column = rw_col[:, chunk : chunk + 1].to_broadcast([P, P])
+            nc.tensor.transpose(rw_banks[h][:, first : first + P], column, ident[:])
 
+        def gather(engine, dst, plane, slots):
+            window = plane[:].indirect(offsets[:, slots.start // LIST_ROWS : slots.stop // LIST_ROWS])
+            if engine == VECTOR:
+                nc.vector.tensor_copy(out=dst[:, slots], in_=window)
+            else:
+                nc.scalar.activation(out=dst[:, slots], in_=window, func=COPY)
+
+        def deal(engine, grouped, listed, planes, tiles):
+            copy_on(
+                engine,
+                grouped[:].rearrange("p (t run x) j -> p run t x j", t=PACK, x=2)[:, :, tiles, :, planes],
+                listed[:].rearrange("p (j run x t) -> p run t x j", j=PACK, t=PACK, x=2)[:, :, tiles, :, planes],
+            )
+
+        all_slots = slice(0, SLOTS)
+        low, high, both = slice(0, 2), slice(2, PACK), slice(0, PACK)
+
+        def last_plane(planes, pool):
+            for engine, slots in ((VECTOR, slice(0, LAST_ON_VECTOR)), (SCALAR, slice(LAST_ON_VECTOR, SLOTS))):
+                gather(engine, planes[PACK - 1], pool[PACK - 1], slots)
 
         k_grouped = held("k_grouped", [P, SLOTS, PACK], BF16)
-        k_planes = []
-        for first, engine in ((0, SCALAR), (2, VECTOR)):
-            listed = held("k_listed" + str(first), [P, 2 * SLOTS], BF16)
-            for j in range(first, first + 2):
-                k_planes.append(listed[:, (j - first) * SLOTS : (j - first + 1) * SLOTS])
-                nc.vector.tensor_copy(out=k_planes[j], in_=k_pool[j][:].indirect(offsets[:]))
-            interleave(engine, k_grouped[:, :, first : first + 2], listed[:].rearrange("p (j slot) -> p j slot", j=2))
+        k_listed = held("k_listed", [P, PACK * SLOTS], BF16)
+        k_planes = [k_listed[:, j * SLOTS : (j + 1) * SLOTS] for j in range(PACK)]
+        for j in range(PACK - 1):
+            gather(VECTOR, k_planes[j], k_pool[j], all_slots)
+            if j == 1:
+                deal(VECTOR, k_grouped, k_listed, low, both)
+        last_plane(k_planes, k_pool)
+        deal(VECTOR, k_grouped, k_listed, high, slice(0, PACK - 1))
+        deal(SCALAR, k_grouped, k_listed, high, slice(PACK - 1, PACK))
         k_mx = quantized("k", k_grouped[:], SLOTS, E4M3)
 
-        v_listed = held("v_listed", [P, (PACK - 1) * SLOTS], BF16)
-        v_planes = v_listed[:].rearrange("p (j slot) -> p j slot", j=PACK - 1)
-        for j in range(PACK - 1):
-            nc.vector.tensor_copy(out=v_planes[:, j, :], in_=v_pool[j][:].indirect(offsets[:]))
-        v_grouped = held("v_grouped", [P, SLOTS, PACK], BF16)
-        interleave(VECTOR, v_grouped[:, :, : PACK - 1], v_planes)
-        v_mx = mx_tiles("v", SLOTS, E4M3)
-        slot_halves = (slice(0, SLOTS // 2), slice(SLOTS // 2, SLOTS))
-        for slots in slot_halves:
-            entries = offsets[:, slots.start // LIST_ROWS : slots.stop // LIST_ROWS]
-            nc.vector.tensor_copy(out=v_grouped[:, slots, PACK - 1], in_=v_pool[PACK - 1][:].indirect(entries))
-        for slots in slot_halves:
-            quantize(v_mx, slots, v_grouped[:, slots, :])
-
-        do_grouped, do_mx = [], []
-
-        def interleave_do(chunk, on=None):
-            h, first = divmod(chunk * P, DO_COLS)
-            do_grouped.append(held("do_grouped" + str(chunk), [P, P, PACK], BF16, on))
-            engine = VECTOR if chunk in DO_ON_VECTOR else SCALAR
-            interleave(engine, do_grouped[chunk][:], do_raw[h][:, :, first : first + P])
-
-        def quantize_do(chunk):
-            do_mx.append(quantized("do" + str(chunk), do_grouped[chunk][:], P, E5M2))
-
-        for chunk in range(DO_EARLY):
-            interleave_do(chunk)
-            if chunk < DO_LEAD:
-                quantize_do(chunk)
-
-        query_halves = (slice(0, Q_COLS // 2), slice(Q_COLS // 2, Q_COLS))
+        query_halves = (slice(0, Q_ON_SCALAR), slice(Q_ON_SCALAR, Q_COLS))
         q_mx = []
         for h, part in enumerate(q_raw):
             grouped = held("q_grouped" + str(h), [P, Q_COLS, PACK], BF16)
@@ -195,7 +189,7 @@ def tile_attend_gat_q_ts_kernel(tc, qT, kT, vT, doT, rw, ts, offs, out):
                 interleave(engine, grouped[:, cols, :], part[:, :, cols])
             q_mx.append(quantized("q" + str(h), grouped[:], Q_COLS, E4M3))
 
-        kt_mx = mx_tiles("kt", FEATURES, E4M3)
+        kt_mx = mx_tiles("kt", FEATURES, E4M3, "q_grouped1")
         for pair, on in enumerate((None, "q_raw0")):
             bank = next_bank("turn").rearrange("m (odd u p) -> m odd u p", odd=2, u=2)
             for odd in range(2):
@@ -209,88 +203,78 @@ def tile_attend_gat_q_ts_kernel(tc, qT, kT, vT, doT, rw, ts, offs, out):
             )
             quantize(kt_mx, slice(pair * 2 * P, (pair + 1) * 2 * P), kt_grouped[:])
 
-        def times_ts(engine, c, dst, src):
-            engine.tensor_scalar(out=dst, in0=src, scalar1=ts_col[:, c : c + 1], scalar2=0.0, op0=MULT, op1=ADD)
+        factor = held("factor", [P, PACK, Q_COLS], F32)
+        for t in range(PACK):
+            nc.scalar.activation(out=factor[:, t, :], in_=rw_banks[1], func=COPY, scale=ts_col[:, t : t + 1])
 
-        gated = []
-        for h in range(QUERIES // Q_COLS):
-            last_load = h == QUERIES // Q_COLS - 1
-            on_scalar = SLOT_TILES - 1 if last_load else SLOT_TILES
-            whole_tiles = SLOT_TILES - HALVED_TILES if last_load else SLOT_TILES
-            relu_tile = held("relu" + str(h), [P, on_scalar, Q_COLS], F32, "k_pool" + str(h))
-            gated.append(held("gated" + str(h), [P, SLOT_TILES, Q_COLS], F32))
-            relu = []
-            for c in range(SLOT_TILES):
-                bank = next_bank("score")
-                product(bank, k_mx, c * P, q_mx[h])
-                scale = ts_col[:, c : c + 1]
-                if c < on_scalar:
-                    relu.append(relu_tile[:, c, :])
-                    nc.scalar.activation(out=relu[c], in_=bank, func=RELU, scale=scale)
-                else:
-                    relu.append(held("last_relu", [P, Q_COLS], F32, "v_pool0")[:])
-                    nc.vector.tensor_scalar(out=relu[c], in0=bank, scalar1=scale, scalar2=0.0, op0=MULT, op1=MAX)
-                if c < whole_tiles:
-                    engine = nc.vector if h == 0 and c < FIRST_ON_VECTOR else nc.gpsimd
-                    times_ts(engine, c, gated[h][:, c, :], relu[c])
-            for cols in query_halves:
-                for c in range(whole_tiles, SLOT_TILES):
-                    times_ts(nc.gpsimd, c, gated[h][:, c, cols], relu[c][:, cols])
-
-        weight_banks = [next_bank("weight") for chunk in range(CHUNKS)]
-
-        def turn_gated(chunk, c):
-            h, first = divmod(chunk * P, Q_COLS)
-            place = weight_banks[chunk][:, c * P : (c + 1) * P]
-            nc.tensor.transpose(place, gated[h][:, c, first : first + P], ident[:])
-
-        first_chunks, second_chunks = range(CHUNKS // 2), range(CHUNKS // 2, CHUNKS)
-        for chunk in first_chunks:
-            for c in range(SLOT_TILES):
-                turn_gated(chunk, c)
-        for c in range(SLOT_TILES - HALVED_TILES):
-            for chunk in second_chunks:
-                turn_gated(chunk, c)
-        for chunk in second_chunks:
-            for c in range(SLOT_TILES - HALVED_TILES, SLOT_TILES):
-                turn_gated(chunk, c)
         weights = []
-        for chunk in range(CHUNKS):
-            on = "do_raw1" if chunk == CHUNKS - 1 else None
-            weights.append(held("weights" + str(chunk), [P, 2, P, 2], F32, on))
-            nc.scalar.activation(
-                out=weights[chunk][:],
-                in_=weight_banks[chunk].rearrange("r (m u z) -> r u m z", u=2, z=2),
-                func=COPY,
-                scale=rw2[:, chunk : chunk + 1],
-            )
+        for h in range(QUERIES // Q_COLS):
+            relu = held("relu" + str(h), [P, PACK, Q_COLS], F32, "k_pool" + str(h))
+            weights.append(held("weights" + str(h), [P, PACK, Q_COLS], F32, "q_raw1" if h == 0 else None))
+            for t in range(PACK):
+                bank = next_bank("score")
+                product(bank, k_mx, t * P, q_mx[h], 0, Q_COLS)
+                scale = ts_col[:, t : t + 1]
+                nc.scalar.activation(out=relu[:, t, :], in_=bank, func=RELU, scale=scale)
+                if h == 0:
+                    nc.vector.scalar_tensor_tensor(
+                        out=weights[h][:, t, :], in0=relu[:, t, :], scalar=scale, in1=rw_banks[h], op0=MULT, op1=MULT
+                    )
+                else:
+                    nc.gpsimd.tensor_tensor(out=weights[h][:, t, :], in0=relu[:, t, :], in1=factor[:, t, :], op=MULT)
 
-        ds_bytes, ds_tiles, ds_grouped, ds_mx = [], [], [], []
+        v_grouped = held("v_grouped", [P, SLOTS, PACK], BF16)
+        v_listed = held("v_listed", [P, PACK * SLOTS], BF16)
+        v_planes = [v_listed[:, j * SLOTS : (j + 1) * SLOTS] for j in range(PACK)]
+        for j, engine in enumerate((VECTOR, SCALAR, VECTOR)):
+            gather(engine, v_planes[j], v_pool[j], all_slots)
+        deal(SCALAR, v_grouped, v_listed, low, high)
+        last_plane(v_planes, v_pool)
+        deal(VECTOR, v_grouped, v_listed, both, low)
+        deal(SCALAR, v_grouped, v_listed, high, high)
+        v_mx = mx_tiles("v", SLOTS, E4M3)
+
+        do_grouped, do_mx = [], []
+
+        def interleave_do(chunk, on=None):
+            h, first = divmod(chunk * P, DO_COLS)
+            do_grouped.append(held("do_grouped" + str(chunk), [P, P, PACK], BF16, on))
+            engine = VECTOR if chunk in DO_ON_VECTOR else SCALAR
+            interleave(engine, do_grouped[chunk][:], do_raw[h][:, :, first : first + P])
+
+        def quantize_do(chunk):
+            do_mx.append(quantized("do" + str(chunk), do_grouped[chunk][:], P, E5M2))
+
+        for t in range(PACK):
+            quantize(v_mx, slice(t * P, (t + 1) * P), v_grouped[:, t * P : (t + 1) * P, :])
+        for chunk in range(DO_EARLY):
+            interleave_do(chunk)
+            if chunk < DO_LEAD:
+                quantize_do(chunk)
+
+        ds_grouped, ds_mx = [], []
 
         def make_ds(chunk):
             bank = next_bank("dp")
-            product(bank, do_mx[chunk], 0, v_mx)
-            ds_bytes.append("do_grouped" + str(chunk + DO_COLS // P) if chunk < HELD_DS else "ds" + str(chunk))
-            ds_tiles.append(held("ds" + str(chunk), [P, 2, P, 2], BF16, ds_bytes[chunk]))
-            dp = bank.rearrange("r (m u z) -> r u m z", u=2, z=2)
-            nc.vector.tensor_tensor(out=ds_tiles[chunk][:], in0=dp, in1=weights[chunk][:], op=MULT)
-
-        def turn_ds(chunk):
-            bank = next_bank("ds")[:, : 2 * P].rearrange("m (u r) -> m u r", u=2)
-            words = ds_tiles[chunk][:].rearrange("r u m z -> r (u m z)").bitcast(F32)
-            for u in range(2):
-                nc.tensor.transpose(bank[:, u, :], words[:, u * P : (u + 1) * P], ident[:])
-            ds_grouped.append(held("ds_grouped" + str(chunk), [P, P, PACK], BF16))
-            engine = VECTOR if chunk >= CHUNKS - TURNS_ON_VECTOR else SCALAR
-            copy_on(engine, ds_grouped[chunk][:].bitcast(F32), bank.rearrange("m u r -> m r u"))
+            for t in range(PACK):
+                product(bank[:, t * P : (t + 1) * P], v_mx, t * P, do_mx[chunk], 0, P)
+            on = "do_grouped" + str(chunk + 1) if chunk + 1 < CHUNKS else None
+            ds_grouped.append(held("ds_grouped" + str(chunk), [P, P, PACK], BF16, on))
+            h, first = divmod(chunk * P, Q_COLS)
+            nc.vector.tensor_tensor(
+                out=ds_grouped[chunk][:].rearrange("m (run x) t -> m run t x", x=LINE),
+                in0=bank.rearrange("m (t run x) -> m run t x", t=PACK, x=LINE),
+                in1=weights[h][:, :, first : first + P].rearrange("m t (run x) -> m run t x", x=LINE),
+                op=MULT,
+            )
 
         def quantize_ds(chunk):
             ds_mx.append(quantized("ds_mx" + str(chunk), ds_grouped[chunk][:], P, E5M2))
 
         def finish(chunk):
             bank = next_bank("result")
-            product(bank, ds_mx[chunk], 0, kt_mx)
-            result = held("result" + str(chunk), [P, P, 2, 2], F32)
+            product(bank, ds_mx[chunk], 0, kt_mx, 0, FEATURES)
+            result = held("result" + str(chunk), [P, P, 2, 2], F32, RESULT_ON.get(chunk))
             last = chunk == CHUNKS - 1
             pieces = 2 if last else 1
             for piece in range(pieces):
@@ -303,11 +287,11 @@ def tile_attend_gat_q_ts_kernel(tc, qT, kT, vT, doT, rw, ts, offs, out):
                 )
 
         for step in range(CHUNKS + FINISH_LAG):
-            for stage, lag in ((quantize_ds, QUANTIZE_LAG), (turn_ds, TURN_LAG), (make_ds, 0), (finish, FINISH_LAG)):
+            for stage, lag in ((make_ds, 0), (quantize_ds, QUANTIZE_LAG), (finish, FINISH_LAG)):
                 if 0 <= step - lag < CHUNKS:
                     stage(step - lag)
-            turned = step - TURN_LAG
-            if 0 <= turned < CHUNKS - DO_EARLY:
-                interleave_do(DO_EARLY + turned, ds_bytes[turned])
+            finished = step - FINISH_LAG
+            if 0 <= finished < CHUNKS - DO_EARLY:
+                interleave_do(DO_EARLY + finished)
             if step + DO_LEAD < CHUNKS:
                 quantize_do(step + DO_LEAD)

from contextlib import ExitStack

import concourse.mybir as mybir
from concourse.masks import make_identity

F32 = mybir.dt.float32
BF16 = mybir.dt.bfloat16
U32 = mybir.dt.uint32
U16 = mybir.dt.uint16
U8 = mybir.dt.uint8
E4M3 = mybir.dt.float8_e4m3fn_x4
E5M2 = mybir.dt.float8_e5m2_x4
MULT = mybir.AluOpType.mult
ADD = mybir.AluOpType.add
MAX = mybir.AluOpType.max
RELU = mybir.ActivationFunctionType.Relu
COPY = mybir.ActivationFunctionType.Copy

P = 128
PACK = 4
LIST_ROWS = 16
LINE = 4
BANK, BANKS = 512, 8
SLOTS, TOKENS, FEATURES, QUERIES = 512, 2048, 512, 1024
CHUNKS = QUERIES // P
SLOT_TILES = SLOTS // P
Q_COLS = 512
DO_COLS = 256

VECTOR, SCALAR = "vector", "scalar"
LAST_ON_VECTOR = 320
Q_ON_SCALAR = 192
DO_ON_VECTOR = (1,)
DO_EARLY = 6
DO_LEAD = 3
RESULT_ON = {0: "do_raw2", 2: "do_raw3"}
QUANTIZE_LAG, FINISH_LAG = 1, 1

BANKS_OF = {
    "score": (0, 1, 2, 3),
    "turn": (4, 5, 6, 7),
    "dp": (0, 1, 2, 3),
    "result": (4, 5, 6, 7),
}

FLOPS = 3 * 2 * QUERIES * SLOTS * FEATURES


def tile_attend_gat_q_ts_kernel(tc, qT, kT, vT, doT, rw, ts, offs, out):
    nc = tc.nc

    with ExitStack() as ctx:
        keep = ctx.enter_context(tc.tile_pool(name="keep", bufs=1))
        psum = ctx.enter_context(tc.psum_pool(name="psum", bufs=1))
        banks = [psum.tile([P, BANK], F32, name="bank" + str(b)) for b in range(BANKS)]
        taken = {role: [] for role in BANKS_OF}

        def next_bank(role):
            numbers = BANKS_OF[role]
            taken[role].append(numbers[len(taken[role]) % len(numbers)])
            return banks[taken[role][-1]][:]

        def held(name, shape, dtype, on=None):
            return keep.tile(shape, dtype, name=name, tag=on or name, align_bytes=64)

        def copy_on(engine, dst, src):
            if engine == VECTOR:
                nc.vector.tensor_copy(out=dst, in_=src)
            else:
                nc.scalar.copy(out=dst, in_=src)

        def interleave(engine, grouped, planes):
            copy_on(
                engine,
                grouped.rearrange("p (run x) j -> p run j x", x=LINE),
                planes.rearrange("p j (run x) -> p run j x", x=LINE),
            )

        def mx_tiles(name, width, fmt, on=None):
            return held(name + "_codes", [P, width], U32, on), held(name + "_scales", [P, width], U8), fmt

        def quantize(operand, cols, grouped):
            codes, scales, fmt = operand
            nc.vector.quantize_mx(
                out=codes[:, cols].bitcast(fmt), scales=scales[:, cols], in_=grouped.rearrange("p col j -> p (col j)")
            )

        def quantized(name, grouped, width, fmt):
            operand = mx_tiles(name, width, fmt)
            quantize(operand, slice(0, width), grouped)
            return operand

        def product(bank, stationary, first, moving, start, width):
            s_codes, s_scales, s_fmt = stationary
            m_codes, m_scales, m_fmt = moving
            nc.tensor.matmul_mx(
                out=bank,
                lhsT=s_codes[:, first : first + P].bitcast(s_fmt),
                lhsT_scale=s_scales[:, first : first + P],
                rhs=m_codes[:, start : start + width].bitcast(m_fmt),
                rhs_scale=m_scales[:, start : start + width],
                start=True,
                stop=True,
            )

        offsets = keep.tile([P, SLOTS // LIST_ROWS], U16, name="offsets")
        ts_pool = held("ts_pool", [P, TOKENS], F32)
        nc.scalar.dma_start(out=ts_pool[P - 1 : P, :], in_=ts[0:1, :])
        nc.vector.memset(ts_pool[0 : P - 1, :], 0.0)
        rw_rows = held("rw_rows", [P, P], F32)
        nc.scalar.dma_start(out=rw_rows[P - CHUNKS : P, :], in_=rw[0].rearrange("(chunk p) one -> chunk (p one)", p=P))
        nc.vector.memset(rw_rows[0 : P - CHUNKS, :], 0.0)

        def load_plane(name, src, j):
            plane = held(name + str(j), [P, TOKENS], F32)
            nc.sync.dma_start(out=plane[:], in_=src.rearrange("(p j) token -> p j token", j=PACK)[:, j, :])
            return plane

        def load_part(name, src, width, h):
            part = held(name + str(h), [P, PACK, width], F32)
            rows = src[0].rearrange("(p j) r -> p j r", j=PACK)
            nc.sync.dma_start(out=part[:], in_=rows[:, :, h * width : (h + 1) * width])
            return part

        nc.sync.dma_start(offsets[:], offs)
        k_pool = [load_plane("k_pool", kT, j) for j in range(PACK)]
        q_raw = [load_part("q_raw", qT, Q_COLS, h) for h in range(QUERIES // Q_COLS)]
        v_pool = [load_plane("v_pool", vT, j) for j in range(PACK)]
        do_raw = [load_part("do_raw", doT, DO_COLS, h) for h in range(QUERIES // DO_COLS)]

        ident = held("ident", [P, P], F32)
        make_identity(nc, ident[:])

        bank = next_bank("turn")
        nc.tensor.transpose(bank[:, :P], rw_rows[:], ident[:])
        rw_col = held("rw_col", [P, CHUNKS], F32)
        nc.scalar.mul(rw_col[:], bank[:, P - CHUNKS : P], 2.0)
        ts_listed = held("ts_listed", [P, SLOTS], F32)
        nc.vector.tensor_copy(out=ts_listed[:], in_=ts_pool[:].indirect(offsets[:]))
        bank = next_bank("turn").rearrange("p (t x) -> p t x", x=P)
        for t in range(PACK):
            nc.tensor.transpose(bank[:, t, :], ts_listed[:].rearrange("p (m t) -> p t m", t=PACK)[:, t, :], ident[:])
        ts_col = held("ts_col", [P, PACK], F32)
        nc.scalar.copy(out=ts_col[:], in_=bank[:, :, P - 1])
        rw_banks = [next_bank("turn") for h in range(QUERIES // Q_COLS)]
        for chunk in range(CHUNKS):
            h, first = divmod(chunk * P, Q_COLS)
            column = rw_col[:, chunk : chunk + 1].to_broadcast([P, P])
            nc.tensor.transpose(rw_banks[h][:, first : first + P], column, ident[:])

        def gather(engine, dst, plane, slots):
            window = plane[:].indirect(offsets[:, slots.start // LIST_ROWS : slots.stop // LIST_ROWS])
            if engine == VECTOR:
                nc.vector.tensor_copy(out=dst[:, slots], in_=window)
            else:
                nc.scalar.activation(out=dst[:, slots], in_=window, func=COPY)

        def deal(engine, grouped, listed, planes, tiles):
            copy_on(
                engine,
                grouped[:].rearrange("p (t run x) j -> p run t x j", t=PACK, x=2)[:, :, tiles, :, planes],
                listed[:].rearrange("p (j run x t) -> p run t x j", j=PACK, t=PACK, x=2)[:, :, tiles, :, planes],
            )

        all_slots = slice(0, SLOTS)
        low, high, both = slice(0, 2), slice(2, PACK), slice(0, PACK)

        def last_plane(planes, pool):
            for engine, slots in ((VECTOR, slice(0, LAST_ON_VECTOR)), (SCALAR, slice(LAST_ON_VECTOR, SLOTS))):
                gather(engine, planes[PACK - 1], pool[PACK - 1], slots)

        k_grouped = held("k_grouped", [P, SLOTS, PACK], BF16)
        k_listed = held("k_listed", [P, PACK * SLOTS], BF16)
        k_planes = [k_listed[:, j * SLOTS : (j + 1) * SLOTS] for j in range(PACK)]
        for j in range(PACK - 1):
            gather(VECTOR, k_planes[j], k_pool[j], all_slots)
            if j == 1:
                deal(VECTOR, k_grouped, k_listed, low, both)
        last_plane(k_planes, k_pool)
        deal(VECTOR, k_grouped, k_listed, high, slice(0, PACK - 1))
        deal(SCALAR, k_grouped, k_listed, high, slice(PACK - 1, PACK))
        k_mx = quantized("k", k_grouped[:], SLOTS, E4M3)

        query_halves = (slice(0, Q_ON_SCALAR), slice(Q_ON_SCALAR, Q_COLS))
        q_mx = []
        for h, part in enumerate(q_raw):
            grouped = held("q_grouped" + str(h), [P, Q_COLS, PACK], BF16)
            for engine, cols in zip((SCALAR if h == 0 else VECTOR, VECTOR), query_halves):
                interleave(engine, grouped[:, cols, :], part[:, :, cols])
            q_mx.append(quantized("q" + str(h), grouped[:], Q_COLS, E4M3))

        kt_mx = mx_tiles("kt", FEATURES, E4M3, "q_grouped1")
        for pair, on in enumerate((None, "q_raw0")):
            bank = next_bank("turn").rearrange("m (odd u p) -> m odd u p", odd=2, u=2)
            for odd in range(2):
                words = k_planes[2 * pair + odd].bitcast(F32).rearrange("p (m u) -> p u m", u=2)
                for u in range(2):
                    nc.tensor.transpose(bank[:, odd, u, :], words[:, u, :], ident[:])
            kt_grouped = held("kt_grouped" + str(pair), [P, 2 * P, PACK], BF16, on)
            nc.scalar.copy(
                out=kt_grouped[:].bitcast(F32).rearrange("m (p odd) u -> m p odd u", odd=2),
                in_=bank.rearrange("m odd u p -> m p odd u"),
            )
            quantize(kt_mx, slice(pair * 2 * P, (pair + 1) * 2 * P), kt_grouped[:])

        factor = held("factor", [P, PACK, Q_COLS], F32)
        for t in range(PACK):
            nc.scalar.activation(out=factor[:, t, :], in_=rw_banks[1], func=COPY, scale=ts_col[:, t : t + 1])

        weights = []
        for h in range(QUERIES // Q_COLS):
            relu = held("relu" + str(h), [P, PACK, Q_COLS], F32, "k_pool" + str(h))
            weights.append(held("weights" + str(h), [P, PACK, Q_COLS], F32, "q_raw1" if h == 0 else None))
            for t in range(PACK):
                bank = next_bank("score")
                product(bank, k_mx, t * P, q_mx[h], 0, Q_COLS)
                scale = ts_col[:, t : t + 1]
                nc.scalar.activation(out=relu[:, t, :], in_=bank, func=RELU, scale=scale)
                if h == 0:
                    nc.vector.scalar_tensor_tensor(
                        out=weights[h][:, t, :], in0=relu[:, t, :], scalar=scale, in1=rw_banks[h], op0=MULT, op1=MULT
                    )
                else:
                    nc.gpsimd.tensor_tensor(out=weights[h][:, t, :], in0=relu[:, t, :], in1=factor[:, t, :], op=MULT)

        v_grouped = held("v_grouped", [P, SLOTS, PACK], BF16)
        v_listed = held("v_listed", [P, PACK * SLOTS], BF16)
        v_planes = [v_listed[:, j * SLOTS : (j + 1) * SLOTS] for j in range(PACK)]
        for j, engine in enumerate((VECTOR, SCALAR, VECTOR)):
            gather(engine, v_planes[j], v_pool[j], all_slots)
        deal(SCALAR, v_grouped, v_listed, low, high)
        last_plane(v_planes, v_pool)
        deal(VECTOR, v_grouped, v_listed, both, low)
        deal(SCALAR, v_grouped, v_listed, high, high)
        v_mx = mx_tiles("v", SLOTS, E4M3)

        do_grouped, do_mx = [], []

        def interleave_do(chunk, on=None):
            h, first = divmod(chunk * P, DO_COLS)
            do_grouped.append(held("do_grouped" + str(chunk), [P, P, PACK], BF16, on))
            engine = VECTOR if chunk in DO_ON_VECTOR else SCALAR
            interleave(engine, do_grouped[chunk][:], do_raw[h][:, :, first : first + P])

        def quantize_do(chunk):
            do_mx.append(quantized("do" + str(chunk), do_grouped[chunk][:], P, E5M2))

        for t in range(PACK):
            quantize(v_mx, slice(t * P, (t + 1) * P), v_grouped[:, t * P : (t + 1) * P, :])
        for chunk in range(DO_EARLY):
            interleave_do(chunk)
            if chunk < DO_LEAD:
                quantize_do(chunk)

        ds_grouped, ds_mx = [], []

        def make_ds(chunk):
            bank = next_bank("dp")
            for t in range(PACK):
                product(bank[:, t * P : (t + 1) * P], v_mx, t * P, do_mx[chunk], 0, P)
            on = "do_grouped" + str(chunk + 1) if chunk + 1 < CHUNKS else None
            ds_grouped.append(held("ds_grouped" + str(chunk), [P, P, PACK], BF16, on))
            h, first = divmod(chunk * P, Q_COLS)
            nc.vector.tensor_tensor(
                out=ds_grouped[chunk][:].rearrange("m (run x) t -> m run t x", x=LINE),
                in0=bank.rearrange("m (t run x) -> m run t x", t=PACK, x=LINE),
                in1=weights[h][:, :, first : first + P].rearrange("m t (run x) -> m run t x", x=LINE),
                op=MULT,
            )

        def quantize_ds(chunk):
            ds_mx.append(quantized("ds_mx" + str(chunk), ds_grouped[chunk][:], P, E5M2))

        def finish(chunk):
            bank = next_bank("result")
            product(bank, ds_mx[chunk], 0, kt_mx, 0, FEATURES)
            result = held("result" + str(chunk), [P, P, 2, 2], F32, RESULT_ON.get(chunk))
            last = chunk == CHUNKS - 1
            pieces = 2 if last else 1
            for piece in range(pieces):
                span = slice(piece * P // pieces, (piece + 1) * P // pieces)
                ordered = bank.rearrange("r (pair p odd) -> r p pair odd", pair=2, odd=2)[:, span]
                copy_on(VECTOR if last else SCALAR, result[:, span], ordered)
                nc.sync.dma_start(
                    out=out[0, chunk * P : (chunk + 1) * P, span.start * PACK : span.stop * PACK],
                    in_=result[:, span].rearrange("r p pair odd -> r (p pair odd)"),
                )

        for step in range(CHUNKS + FINISH_LAG):
            for stage, lag in ((make_ds, 0), (quantize_ds, QUANTIZE_LAG), (finish, FINISH_LAG)):
                if 0 <= step - lag < CHUNKS:
                    stage(step - lag)
            finished = step - FINISH_LAG
            if 0 <= finished < CHUNKS - DO_EARLY:
                interleave_do(DO_EARLY + finished)
            if step + DO_LEAD < CHUNKS:
                quantize_do(step + DO_LEAD)
